import numpy as np
import ml_dtypes


def mxq(x, axis, fmt="e4m3"):
    dtype, down = {"e4m3": (ml_dtypes.float8_e4m3fn, 7), "e5m2": (ml_dtypes.float8_e5m2, 14)}[fmt]
    v = np.moveaxis(np.asarray(x, np.float32).astype(ml_dtypes.bfloat16).astype(np.float64), axis, -1)
    blocks = v.reshape(v.shape[:-1] + (-1, 32))
    amax = np.abs(blocks).max(-1, keepdims=True)
    byte = np.maximum(np.where(amax > 0, np.frexp(amax)[1] - 1 + 127, 0) - down, 1)
    scale = np.exp2(byte - 127.0)
    codes = (blocks / scale).astype(np.float32).astype(dtype).astype(np.float64)
    return np.moveaxis((codes * scale).reshape(v.shape), -1, axis)


WIDE = False


def mx_kscale(k):
    if not WIDE:
        return np.ones(k)
    levels = np.array([10, -10, 5, -5, 0])
    if k % 512:
        return np.exp2(np.random.permutation(np.resize(levels, k // 32))).repeat(32)
    a = np.empty((k // 512, 16))
    for p in range(k // 512):
        a[p, :8] = np.random.permutation(np.resize(levels, 8))
        for g in range(8):
            far = levels[np.abs(levels - a[p, g]) >= 10]
            a[p, g + 8] = far[np.random.randint(len(far))]
    return np.exp2(a.ravel()).repeat(32)


def f64(x):
    return np.asarray(x).astype(np.float64)


def striped(idx):
    return np.tile(idx.reshape(-1, 16).T, (8, 1)).astype(np.uint16)


def unstriped(offs):
    return offs[:16].T.reshape(-1).astype(np.int64)


E2M1 = np.array([0.0, 0.5, 1.0, 1.5, 2.0, 3.0, 4.0, 6.0, -0.0, -0.5, -1.0, -1.5, -2.0, -3.0, -4.0, -6.0])


def pack_weight(w, fmt):
    k, n = w.shape
    w = f64(np.asarray(w, np.float32).astype(ml_dtypes.bfloat16)).reshape(k // 32, 32, n)
    amax = np.abs(w).max(1)
    if fmt == "e4m3":
        byte = np.frexp(amax)[1] - 1 + 127 - 7
    else:
        mant, ex = np.frexp(amax / 6.0)
        byte = np.where(mant > 0.5, ex, ex - 1) + 127
    byte = np.clip(np.where(amax > 0, byte, 1), 1, 254)
    scaled = (w * np.exp2(127.0 - byte)[:, None, :]).reshape(k, n).astype(np.float32)
    by_word = np.ascontiguousarray(scaled.reshape(k // 512, 128, 4, n).transpose(0, 1, 3, 2))
    if fmt == "e4m3":
        words = by_word.astype(ml_dtypes.float8_e4m3fn).view(np.uint8)
    else:
        c = by_word.astype(ml_dtypes.float4_e2m1fn).view(np.uint8) & 0xF
        words = (c[..., 0::2] | (c[..., 1::2] << 4)).reshape(k // 512, 128, 2 * n)
    return np.ascontiguousarray(words), np.ascontiguousarray(byte.astype(np.uint8).reshape(k // 512, 16, n))


def unpack_weight(words, scales, fmt):
    g, _, n = scales.shape
    words = np.ascontiguousarray(words).reshape(g, 128, n, -1)
    if fmt == "e4m3":
        vals = words.view(ml_dtypes.float8_e4m3fn).astype(np.float64)
    else:
        nib = np.empty((g, 128, n, 4), np.uint8)
        nib[..., 0::2] = words & 0xF
        nib[..., 1::2] = words >> 4
        vals = E2M1[nib]
    vals = vals * np.repeat(np.exp2(scales.astype(np.float64) - 127.0), 8, axis=1)[..., None]
    return vals.transpose(0, 1, 3, 2).reshape(g * 512, n)


def sigmoid(v):
    return 1.0 / (1.0 + np.exp(-np.maximum(v, -700.0)))


K, T, E, C, H, N = 1024, 768, 4, 128, 512, 512


def by_expert(wq, xq):
    return np.concatenate([wq[e].T @ xq[:, e * C:(e + 1) * C] for e in range(E)], axis=1)


def setup_inputs():
    n = np.random.standard_normal
    s = mx_kscale(K)[:, None]
    u = mx_kscale(H)
    w1 = [pack_weight(m, "e2m1") for m in n((E + 1, K, H)) / np.sqrt(K) / s[None]]
    w3 = [pack_weight(m, "e2m1") for m in n((E + 1, K, H)) / np.sqrt(K) / s[None] * u[None, None, :]]
    w2 = [pack_weight(m, "e2m1") for m in n((E + 1, H, N)) / np.sqrt(H) / u[None, :, None]]
    return {
        "xT": (n((K, T)) * s).astype(np.float32),
        "w1_words": np.stack([m[0] for m in w1]),
        "w1_scales": np.stack([m[1] for m in w1]),
        "w3_words": np.stack([m[0] for m in w3]),
        "w3_scales": np.stack([m[1] for m in w3]),
        "w2_words": np.stack([m[0] for m in w2]),
        "w2_scales": np.stack([m[1] for m in w2]),
        "gate": np.tile(np.random.uniform(0.2, 1.0, E * C), (N, 1)).astype(np.float32),
        "offs": striped(np.random.permutation(T)[:E * C]),
    }


def reference(xT, w1_words, w1_scales, w3_words, w3_scales, w2_words, w2_scales, gate, offs):
    idx = unstriped(offs)
    w1 = np.stack([unpack_weight(w1_words[e], w1_scales[e], "e2m1") for e in range(E + 1)])
    w3 = np.stack([unpack_weight(w3_words[e], w3_scales[e], "e2m1") for e in range(E + 1)])
    w2 = np.stack([unpack_weight(w2_words[e], w2_scales[e], "e2m1") for e in range(E + 1)])
    w1q, w3q, w2q = w1, w3, w2
    xs = mxq(f64(xT), 0, "e4m3")
    hs = sigmoid(w1q[E].T @ xs) * (w3q[E].T @ xs)
    ys = w2q[E].T @ mxq(hs, 0, "e4m3")
    xq = mxq(f64(xT)[:, idx], 0, "e4m3")
    h = sigmoid(by_expert(w1q, xq))
    h = h * by_expert(w3q, xq)
    y = by_expert(w2q, mxq(h, 0, "e4m3"))
    out = ys
    out[:, idx] += f64(gate) * y
    return out

@@ -1,0 +1,273 @@
+from contextlib import ExitStack
+
+import concourse.mybir as mybir
+from concourse.masks import make_identity
+
+K, T, E, C, H, N = 1024, 768, 4, 128, 512, 512
+P = 128
+S = K // 512
+SLOTS = E * C
+LOW, HIGH = slice(0, 512), slice(512, 768)
+FLOPS = 2 * (T + SLOTS) * (2 * K * H + H * N)
+
+F32 = mybir.dt.float32
+BF16 = mybir.dt.bfloat16
+U32 = mybir.dt.uint32
+I32 = mybir.dt.int32
+U16 = mybir.dt.uint16
+U8 = mybir.dt.uint8
+FP8X4 = mybir.dt.float8_e4m3fn_x4
+FP4X4 = mybir.dt.float4_e2m1fn_x4
+MULT = mybir.AluOpType.mult
+ADD = mybir.AluOpType.add
+SIGMOID = mybir.ActivationFunctionType.Sigmoid
+
+
+def tile_moe_shr_glu_sigmoid_kernel(
+    tc, xT, w1_words, w1_scales, w3_words, w3_scales, w2_words, w2_scales, gate, offs, out
+):
+    nc = tc.nc
+    with ExitStack() as ctx:
+        held = ctx.enter_context(tc.tile_pool(name="held", bufs=1))
+        work = ctx.enter_context(tc.tile_pool(name="work", bufs=3))
+        psum = ctx.enter_context(tc.psum_pool(name="psum", bufs=2))
+        psum3 = ctx.enter_context(tc.psum_pool(name="psum3", bufs=3))
+        psum1 = ctx.enter_context(tc.psum_pool(name="psum1", bufs=1))
+
+        offsets = held.tile([P, SLOTS // 16], U16, name="offsets")
+        nc.sync.dma_start(offsets[:], offs)
+
+        planes1 = held.tile([P, (E + 1) * S, H], U8, name="planes1", align_bytes=64)
+        planes3 = held.tile([P, (E + 1) * S, H], U8, name="planes3", align_bytes=64)
+        planes2 = held.tile([P, E + 1, N], U8, name="planes2", align_bytes=64)
+        for planes in (planes1, planes3, planes2):
+            nc.gpsimd.memset(planes[:].rearrange("p g i -> p (g i)").bitcast(I32), 0)
+
+        def load_scales(queue, planes, scales):
+            rows = scales.bitcast(I32).rearrange("e s (q r) i -> r q (e s) i", r=4)
+            for r in range(4):
+                queue.dma_start(out=planes[:].bitcast(I32)[r:P:32, :, :], in_=rows[r])
+
+        load_scales(nc.gpsimd, planes2, w2_scales)
+
+        warm = held.tile([P, 1], F32, name="warm")
+        nc.vector.memset(warm[:], 0.0)
+        warmed = held.tile([P, 1], F32, name="warmed")
+        nc.scalar.activation(warmed[:], warm[:], SIGMOID)
+
+        ident = held.tile([P, P], F32, name="ident")
+        make_identity(nc, ident[:])
+
+        routed = []
+        for c in range(4):
+            window = held.tile([P, T], F32, name=f"routed{c}")
+            nc.vector.memset(window[:], 0.0)
+            routed.append(window)
+
+        rows = xT.rearrange("(s p u b) w -> s u p b w", s=S, p=P, u=2, b=2)
+        raws, pairs = [], []
+        for s in range(S):
+            raw = held.tile([P, 4, T], F32, name=f"raw{s}")
+            raws.append(raw)
+            for u in range(2):
+                for cols in (LOW, HIGH) if (s, u) == (1, 1) else (slice(0, T),):
+                    nc.sync.dma_start(out=raw[:, 2 * u : 2 * u + 2, cols], in_=rows[s, u][:, :, cols])
+
+        words1, words3, words2 = {}, {}, {}
+
+        def load_expert(e):
+            for name, held_words, source in (("w1", words1, w1_words), ("w3", words3, w3_words)):
+                tile = held.tile([P, S, 2 * H], U8, name=f"{name}_{e}", align_bytes=64)
+                nc.sync.dma_start(out=tile[:].bitcast(I32), in_=source[e].bitcast(I32).rearrange("s p b -> p s b"))
+                held_words[e] = tile
+            tile = held.tile([P, 2 * N], U8, name=f"w2_{e}", align_bytes=64)
+            nc.sync.dma_start(out=tile[:].bitcast(I32), in_=w2_words[e, 0].bitcast(I32))
+            words2[e] = tile
+
+        gates = held.tile([P, SLOTS], F32, name="gates")
+        load_scales(nc.sync, planes1, w1_scales)
+        load_scales(nc.sync, planes3, w3_scales)
+        load_expert(0)
+        nc.sync.dma_start(out=gates[:], in_=gate[:P, :])
+        load_expert(1)
+        load_expert(2)
+        load_expert(3)
+        load_expert(E)
+
+        slot_codes = [held.tile([P, SLOTS], U32, name=f"slot_codes{s}", align_bytes=64) for s in range(S)]
+        slot_scales = [held.tile([P, SLOTS], U8, name=f"slot_scales{s}", align_bytes=64) for s in range(S)]
+
+        def cast(s, u):
+            paired = pairs[s][:, u, :].rearrange("p (w b) -> p w b", b=2)
+            raw = raws[s][:, 2 * u : 2 * u + 2, :].rearrange("p b w -> p w b")
+            if (s, u) == (1, 1):
+                nc.scalar.copy(paired[:, LOW, :], raw[:, LOW, :])
+                nc.vector.tensor_copy(paired[:, HIGH, :], raw[:, HIGH, :])
+            else:
+                nc.scalar.copy(paired, raw)
+
+        gathered = {}
+
+        def gather(s, u, half):
+            if u == 0:
+                gathered[s, half] = held.tile([P, 2, SLOTS], BF16, name=f"gathered{s}{half}", align_bytes=64)
+            nc.vector.tensor_copy(
+                gathered[s, half][:, u, :].bitcast(U32),
+                pairs[s][:, u, :].bitcast(U32).indirect(offsets[:, 16 * half : 16 * half + 16]),
+            )
+
+        def quantise_slots(s, half):
+            grouped = held.tile([P, 2 * SLOTS], BF16, name=f"slots{s}{half}", align_bytes=64)
+            interleave = nc.scalar.copy if half else nc.vector.tensor_copy
+            interleave(
+                grouped[:].bitcast(F32).rearrange("p (c u) -> p c u", u=2),
+                gathered[s, half][:].bitcast(F32).rearrange("p u c -> p c u"),
+            )
+            cols = slice(2 * C * half, 2 * C * (half + 1))
+            nc.vector.quantize_mx(
+                out=slot_codes[s][:, cols].bitcast(FP8X4), scales=slot_scales[s][:, cols], in_=grouped[:]
+            )
+
+        for s in range(S):
+            pairs.append(held.tile([P, 2, 2 * T], BF16, name=f"pair{s}", align_bytes=64))
+            for u in range(2):
+                cast(s, u)
+                gather(s, u, 0)
+            quantise_slots(s, 0)
+
+        token_codes = [held.tile([P, T], U32, name=f"token_codes{s}", align_bytes=64) for s in range(S)]
+        token_scales = [held.tile([P, T], U8, name=f"token_scales{s}", align_bytes=64) for s in range(S)]
+
+        def quantise_tokens(s, lo, hi):
+            cols = slice(lo, hi)
+            grouped = held.tile([P, hi - lo, 4], BF16, name=f"tokens{s}_{lo}", align_bytes=64)
+            nc.scalar.copy(
+                grouped[:].rearrange("p w j -> p (w j)").bitcast(F32).rearrange("p (w u) -> p w u", u=2),
+                pairs[s][:].bitcast(F32)[:, :, cols].rearrange("p u w -> p w u"),
+            )
+            nc.vector.quantize_mx(
+                out=token_codes[s][:, cols].bitcast(FP8X4),
+                scales=token_scales[s][:, cols],
+                in_=grouped[:].rearrange("p w j -> p (w j)"),
+            )
+
+        results = [held.tile([P, T], F32, name=f"result{c}") for c in range(4)]
+        h_codes = held.tile([P, SLOTS + T], U32, name="h_codes", align_bytes=64)
+        h_scales = held.tile([P, SLOTS + T], U8, name="h_scales", align_bytes=64)
+        hs = {}
+
+        def first_layer(i):
+            if i < E:
+                e, codes, scales, cols = i, slot_codes, slot_scales, slice(i * P, (i + 1) * P)
+            else:
+                e, codes, scales, cols = E, token_codes, token_scales, slice((i - E) * P, (i - E + 1) * P)
+            a = psum.tile([P, H], F32, name="a")
+            g = psum3.tile([P, H], F32, name="g")
+            for acc, words, planes in ((a, words1, planes1), (g, words3, planes3)):
+                for s in range(S):
+                    nc.tensor.matmul_mx(
+                        out=acc[:],
+                        lhsT=codes[s][:, cols].bitcast(FP8X4),
+                        lhsT_scale=scales[s][:, cols],
+                        rhs=words[e][:, s, :].bitcast(FP4X4),
+                        rhs_scale=planes[:, e * S + s, :],
+                        start=(s == 0),
+                        stop=(s == S - 1),
+                    )
+            sig = work.tile([P, H], F32, name="sig")
+            nc.scalar.activation(sig[:], a[:], SIGMOID)
+            h = work.tile([P, H], BF16, name="h", align_bytes=64)
+            order = "t (p u b) -> t u p b"
+            nc.vector.tensor_tensor(
+                h[:].rearrange("t (u p b) -> t u p b", u=2, b=2),
+                sig[:].rearrange(order, u=2, b=2),
+                g[:].rearrange(order, u=2, b=2),
+                MULT,
+            )
+            hs[i] = h
+
+        def turn(i):
+            turned = psum1.tile([P, 2, P], F32, name="turned")
+            words = hs[i][:].bitcast(F32)
+            for u in range(2):
+                nc.tensor.transpose(turned[:, u, :], words[:, u * P : (u + 1) * P], ident[:])
+            grouped = work.tile([P, 4 * P], BF16, name="h_grouped", align_bytes=64)
+            nc.scalar.copy(
+                grouped[:].bitcast(F32).rearrange("p (c u) -> p c u", u=2), turned[:].rearrange("p u c -> p c u")
+            )
+            cols = slice(P * i, P * (i + 1))
+            nc.vector.quantize_mx(out=h_codes[:, cols].bitcast(FP8X4), scales=h_scales[:, cols], in_=grouped[:])
+
+        def second_layer(acc, e, c, lo, hi):
+            nc.tensor.matmul_mx(
+                out=acc,
+                lhsT=words2[e][:, 2 * P * c : 2 * P * (c + 1)].bitcast(FP4X4),
+                lhsT_scale=planes2[:, e, c * P : (c + 1) * P],
+                rhs=h_codes[:, lo:hi].bitcast(FP8X4),
+                rhs_scale=h_scales[:, lo:hi],
+                start=True,
+                stop=True,
+            )
+
+        gated = {}
+
+        def gated_out(first, count, c):
+            bank = psum.tile([P, count * C], F32, name="y")
+            for j in range(count):
+                e = first + j
+                second_layer(bank[:, j * C : (j + 1) * C], e, c, e * C, (e + 1) * C)
+            y = work.tile([P, count * C], F32, name=f"y{count}", bufs=5)
+            nc.scalar.copy(y[:], bank[:])
+            gated[first, c] = y
+
+        def scatter(first, count, c):
+            nc.vector.tensor_tensor(
+                routed[c][:].indirect(offsets[:, 8 * first : 8 * (first + count)]),
+                gated[first, c][:],
+                gates[:, first * C : (first + count) * C],
+                MULT,
+            )
+
+        def finish(c, lo, hi):
+            if lo > 0 and c < 2:
+                bank = psum.tile([P, hi - lo], F32, name="a")
+            else:
+                bank = psum.tile([P, hi - lo], F32, name="y")
+            second_layer(bank[:], E, c, SLOTS + lo, SLOTS + hi)
+            nc.vector.tensor_tensor(results[c][:, lo:hi], bank[:], routed[c][:, lo:hi], ADD)
+            nc.sync.dma_start(out=out[c * P : (c + 1) * P, lo:hi], in_=results[c][:, lo:hi])
+
+        groups = E + T // P
+        units = {
+            3: [(0, 1, 0)],
+            4: [(0, 1, 1)],
+            6: [(0, 1, 2), (0, 1, 3)],
+            7: [(1, 1, 0)],
+            8: [(1, 1, 1), (1, 1, 2)],
+            9: [(1, 1, 3), (2, 2, 0)],
+            10: [(2, 2, 1), (2, 2, 2)],
+            11: [(2, 2, 3)],
+        }
+        for step in range(groups + 3):
+            if step < groups:
+                first_layer(step)
+            if step == 0:
+                for s in range(S):
+                    for u in range(2):
+                        gather(s, u, 1)
+                    quantise_slots(s, 1)
+            if step in (1, 3):
+                for s in range(S):
+                    cols = LOW if step == 1 else HIGH
+                    quantise_tokens(s, cols.start, cols.stop)
+            if 0 <= step - 2 < groups:
+                turn(step - 2)
+            for unit in units.get(step, []):
+                gated_out(*unit)
+            for unit in units.get(step - 1, []):
+                scatter(*unit)
+            if step >= 11:
+                for c in (2 * (step - 11), 2 * (step - 11) + 1):
+                    finish(c, 0, 512)
+        for c in range(4):
+            finish(c, 512, 768)

@@ -7,8 +7,12 @@ K, T, E, C, H, N = 1024, 768, 4, 128, 512, 512
 P = 128
 S = K // 512
 SLOTS = E * C
+HALF = SLOTS // 2
 LOW, HIGH = slice(0, 512), slice(512, 768)
 FLOPS = 2 * (T + SLOTS) * (2 * K * H + H * N)
+GP = False
+LEAD = E - 1
+REST = LEAD * C
 
 F32 = mybir.dt.float32
 BF16 = mybir.dt.bfloat16
@@ -30,25 +34,38 @@ def tile_moe_shr_glu_sigmoid_kernel(
     with ExitStack() as ctx:
         held = ctx.enter_context(tc.tile_pool(name="held", bufs=1))
         work = ctx.enter_context(tc.tile_pool(name="work", bufs=3))
-        psum = ctx.enter_context(tc.psum_pool(name="psum", bufs=2))
-        psum3 = ctx.enter_context(tc.psum_pool(name="psum3", bufs=3))
-        psum1 = ctx.enter_context(tc.psum_pool(name="psum1", bufs=1))
+        psum = ctx.enter_context(tc.psum_pool(name="psum", bufs=1))
+        a_banks = [psum.tile([P, 512], F32, name=f"a{j}") for j in range(2)]
+        g_banks = [psum.tile([P, 512], F32, name=f"g{j}") for j in range(3)]
+        t_banks = [psum.tile([P, 512], F32, name=f"t{j}") for j in range(3)]
 
         offsets = held.tile([P, SLOTS // 16], U16, name="offsets")
         nc.sync.dma_start(offsets[:], offs)
 
-        planes1 = held.tile([P, (E + 1) * S, H], U8, name="planes1", align_bytes=64)
-        planes3 = held.tile([P, (E + 1) * S, H], U8, name="planes3", align_bytes=64)
-        planes2 = held.tile([P, E + 1, N], U8, name="planes2", align_bytes=64)
-        for planes in (planes1, planes3, planes2):
-            nc.gpsimd.memset(planes[:].rearrange("p g i -> p (g i)").bitcast(I32), 0)
+        runs = ((LEAD, E + 1), (0, LEAD))
+        planes13 = {}
+        for lo, hi in runs:
+            tile = held.tile([P, 2 * (hi - lo) * S * H], U8, name=f"planes13_{lo}", align_bytes=64)
+            for m in range(2):
+                nc.vector.memset(tile[:, m * (hi - lo) * S * H : (m + 1) * (hi - lo) * S * H].bitcast(I32), 0)
+            planes13[lo] = tile
+        planes2 = held.tile([P, (E + 1) * N], U8, name="planes2", align_bytes=64)
+        nc.vector.memset(planes2[:].bitcast(I32), 0)
 
-        def load_scales(queue, planes, scales):
+        def load_scales(queue, plane, scales):
             rows = scales.bitcast(I32).rearrange("e s (q r) i -> r q (e s) i", r=4)
+            view = plane.bitcast(I32).rearrange("p (g i) -> p g i", i=H // 4)
             for r in range(4):
-                queue.dma_start(out=planes[:].bitcast(I32)[r:P:32, :, :], in_=rows[r])
+                queue.dma_start(out=view[r:P:32, :, :], in_=rows[r])
 
-        load_scales(nc.gpsimd, planes2, w2_scales)
+        def load_run(queue, m, lo, hi):
+            width = (hi - lo) * S * H
+            load_scales(queue, planes13[lo][:, m * width : (m + 1) * width], (w1_scales, w3_scales)[m][lo:hi])
+
+        def plane13(m, e, s):
+            lo, hi = runs[0] if e >= LEAD else runs[1]
+            at = ((m * (hi - lo) + e - lo) * S + s) * H
+            return planes13[lo][:, at : at + H]
 
         warm = held.tile([P, 1], F32, name="warm")
         nc.vector.memset(warm[:], 0.0)
@@ -61,94 +78,108 @@ def tile_moe_shr_glu_sigmoid_kernel(
         routed = []
         for c in range(4):
             window = held.tile([P, T], F32, name=f"routed{c}")
-            nc.vector.memset(window[:], 0.0)
+            nc.gpsimd.memset(window[:], 0.0)
             routed.append(window)
 
         rows = xT.rearrange("(s p u b) w -> s u p b w", s=S, p=P, u=2, b=2)
-        raws, pairs = [], []
-        for s in range(S):
-            raw = held.tile([P, 4, T], F32, name=f"raw{s}")
-            raws.append(raw)
-            for u in range(2):
-                for cols in (LOW, HIGH) if (s, u) == (1, 1) else (slice(0, T),):
-                    nc.sync.dma_start(out=raw[:, 2 * u : 2 * u + 2, cols], in_=rows[s, u][:, :, cols])
+        pieces = {(s, u): (slice(0, T),) for s in range(S) for u in range(2)}
+        pieces[0, 0] = pieces[0, 1] = pieces[1, 1] = (LOW, HIGH)
+        raws = {}
+        for (s, u), cuts in pieces.items():
+            for j, cols in enumerate(cuts):
+                raw = held.tile([P, 2, cols.stop - cols.start], F32, name=f"raw{s}{u}{j}", align_bytes=64)
+                nc.sync.dma_start(out=raw[:], in_=rows[s, u][:, :, cols])
+                raws[s, u, j] = raw
 
-        words1, words3, words2 = {}, {}, {}
+        words13, words2 = {}, {}
 
-        def load_expert(e):
-            for name, held_words, source in (("w1", words1, w1_words), ("w3", words3, w3_words)):
-                tile = held.tile([P, S, 2 * H], U8, name=f"{name}_{e}", align_bytes=64)
-                nc.sync.dma_start(out=tile[:].bitcast(I32), in_=source[e].bitcast(I32).rearrange("s p b -> p s b"))
-                held_words[e] = tile
-            tile = held.tile([P, 2 * N], U8, name=f"w2_{e}", align_bytes=64)
-            nc.sync.dma_start(out=tile[:].bitcast(I32), in_=w2_words[e, 0].bitcast(I32))
-            words2[e] = tile
+        def load_first(m, lo, hi):
+            tile = held.tile([P, (hi - lo) * S, 2 * H], U8, name=f"w13_{m}{lo}", align_bytes=64)
+            source = (w1_words, w3_words)[m][lo:hi]
+            nc.sync.dma_start(out=tile[:].bitcast(I32), in_=source.bitcast(I32).rearrange("e s p b -> p (e s) b"))
+            for e in range(lo, hi):
+                for s in range(S):
+                    words13[m, e, s] = tile[:, (e - lo) * S + s, :]
+
+        def load_second(lo, hi):
+            tile = held.tile([P, hi - lo, 2 * N], U8, name=f"w2_{lo}", align_bytes=64)
+            nc.sync.dma_start(
+                out=tile[:].bitcast(I32), in_=w2_words[lo:hi, 0].bitcast(I32).rearrange("e p b -> p e b")
+            )
+            for e in range(lo, hi):
+                words2[e] = tile[:, e - lo, :]
 
         gates = held.tile([P, SLOTS], F32, name="gates")
-        load_scales(nc.sync, planes1, w1_scales)
-        load_scales(nc.sync, planes3, w3_scales)
-        load_expert(0)
+        for m in range(2):
+            load_run(nc.sync, m, *runs[0])
+            load_first(m, LEAD, LEAD + 1)
+        for m in range(2):
+            load_first(m, E, E + 1)
+        for m in range(2):
+            load_run(nc.sync, m, *runs[1])
+            load_first(m, 0, 1)
+        load_scales(nc.sync, planes2[:], w2_scales)
+        load_second(LEAD, E + 1)
         nc.sync.dma_start(out=gates[:], in_=gate[:P, :])
-        load_expert(1)
-        load_expert(2)
-        load_expert(3)
-        load_expert(E)
+        for e in range(1, LEAD):
+            for m in range(2):
+                load_first(m, e, e + 1)
+        load_second(0, LEAD)
 
         slot_codes = [held.tile([P, SLOTS], U32, name=f"slot_codes{s}", align_bytes=64) for s in range(S)]
         slot_scales = [held.tile([P, SLOTS], U8, name=f"slot_scales{s}", align_bytes=64) for s in range(S)]
+        pairs = [held.tile([P, 4 * T], BF16, name=f"pair{s}", align_bytes=64) for s in range(S)]
 
         def cast(s, u):
-            paired = pairs[s][:, u, :].rearrange("p (w b) -> p w b", b=2)
-            raw = raws[s][:, 2 * u : 2 * u + 2, :].rearrange("p b w -> p w b")
-            if (s, u) == (1, 1):
-                nc.scalar.copy(paired[:, LOW, :], raw[:, LOW, :])
-                nc.vector.tensor_copy(paired[:, HIGH, :], raw[:, HIGH, :])
-            else:
-                nc.scalar.copy(paired, raw)
+            paired = pairs[s][:, 2 * T * u : 2 * T * (u + 1)].rearrange("p (w b) -> p w b", b=2)
+            for j, cols in enumerate(pieces[s, u]):
+                move = nc.vector.tensor_copy if cols == (LOW if s else HIGH) else nc.scalar.copy
+                move(paired[:, cols, :], raws[s, u, j][:].rearrange("p b w -> p w b"))
 
-        gathered = {}
+        gathered = [held.tile([P, 4 * SLOTS], BF16, name=f"gathered{s}", align_bytes=64) for s in range(S)]
 
-        def gather(s, u, half):
-            if u == 0:
-                gathered[s, half] = held.tile([P, 2, SLOTS], BF16, name=f"gathered{s}{half}", align_bytes=64)
+        planes_apart = (2 * SLOTS, 2 * REST)
+
+        def gather(s, u, lo, hi):
+            at = u * planes_apart[s]
             nc.vector.tensor_copy(
-                gathered[s, half][:, u, :].bitcast(U32),
-                pairs[s][:, u, :].bitcast(U32).indirect(offsets[:, 16 * half : 16 * half + 16]),
+                gathered[s][:, at : at + 2 * (hi - lo)].bitcast(U32),
+                pairs[s][:, 2 * T * u : 2 * T * (u + 1)].bitcast(U32).indirect(offsets[:, lo // 16 : hi // 16]),
             )
 
-        def quantise_slots(s, half):
-            grouped = held.tile([P, 2 * SLOTS], BF16, name=f"slots{s}{half}", align_bytes=64)
-            interleave = nc.scalar.copy if half else nc.vector.tensor_copy
+        def quantise_slots(s, lo, hi, interleave, cuts):
+            grouped = held.tile([P, 4 * (hi - lo)], BF16, name=f"slots{s}_{lo}", align_bytes=64)
             interleave(
                 grouped[:].bitcast(F32).rearrange("p (c u) -> p c u", u=2),
-                gathered[s, half][:].bitcast(F32).rearrange("p u c -> p c u"),
+                gathered[s][:, : 2 * planes_apart[s]].bitcast(F32).rearrange("p (u c) -> p c u", u=2)[:, : hi - lo, :],
             )
-            cols = slice(2 * C * half, 2 * C * (half + 1))
-            nc.vector.quantize_mx(
-                out=slot_codes[s][:, cols].bitcast(FP8X4), scales=slot_scales[s][:, cols], in_=grouped[:]
-            )
+            for a, b in cuts:
+                nc.vector.quantize_mx(
+                    out=slot_codes[s][:, a:b].bitcast(FP8X4),
+                    scales=slot_scales[s][:, a:b],
+                    in_=grouped[:, 4 * (a - lo) : 4 * (b - lo)],
+                )
 
-        for s in range(S):
-            pairs.append(held.tile([P, 2, 2 * T], BF16, name=f"pair{s}", align_bytes=64))
-            for u in range(2):
-                cast(s, u)
-                gather(s, u, 0)
-            quantise_slots(s, 0)
+        for u in range(2):
+            cast(0, u)
+            gather(0, u, 0, SLOTS)
+        quantise_slots(0, 0, SLOTS, nc.vector.tensor_copy, ((0, SLOTS),))
+        for u in range(2):
+            cast(1, u)
+            gather(1, u, REST, SLOTS)
+        quantise_slots(1, REST, SLOTS, nc.vector.tensor_copy, ((REST, SLOTS),))
 
         token_codes = [held.tile([P, T], U32, name=f"token_codes{s}", align_bytes=64) for s in range(S)]
         token_scales = [held.tile([P, T], U8, name=f"token_scales{s}", align_bytes=64) for s in range(S)]
 
-        def quantise_tokens(s, lo, hi):
-            cols = slice(lo, hi)
-            grouped = held.tile([P, hi - lo, 4], BF16, name=f"tokens{s}_{lo}", align_bytes=64)
+        def quantise_tokens(s, cols, tag):
+            grouped = held.tile([P, 4 * (cols.stop - cols.start)], BF16, name=tag, align_bytes=64)
             nc.scalar.copy(
-                grouped[:].rearrange("p w j -> p (w j)").bitcast(F32).rearrange("p (w u) -> p w u", u=2),
-                pairs[s][:].bitcast(F32)[:, :, cols].rearrange("p u w -> p w u"),
+                grouped[:].bitcast(F32).rearrange("p (w u) -> p w u", u=2),
+                pairs[s][:].bitcast(F32).rearrange("p (u w) -> p w u", u=2)[:, cols, :],
             )
             nc.vector.quantize_mx(
-                out=token_codes[s][:, cols].bitcast(FP8X4),
-                scales=token_scales[s][:, cols],
-                in_=grouped[:].rearrange("p w j -> p (w j)"),
+                out=token_codes[s][:, cols].bitcast(FP8X4), scales=token_scales[s][:, cols], in_=grouped[:]
             )
 
         results = [held.tile([P, T], F32, name=f"result{c}") for c in range(4)]
@@ -156,44 +187,51 @@ def tile_moe_shr_glu_sigmoid_kernel(
         h_scales = held.tile([P, SLOTS + T], U8, name="h_scales", align_bytes=64)
         hs = {}
 
-        def first_layer(i):
+        ORDER = (LEAD, E, E + 1, E + 2, 0, 1, 2, E + 3, E + 4, E + 5)
+
+        def first_layer(step):
+            i = ORDER[step]
             if i < E:
                 e, codes, scales, cols = i, slot_codes, slot_scales, slice(i * P, (i + 1) * P)
             else:
                 e, codes, scales, cols = E, token_codes, token_scales, slice((i - E) * P, (i - E + 1) * P)
-            a = psum.tile([P, H], F32, name="a")
-            g = psum3.tile([P, H], F32, name="g")
-            for acc, words, planes in ((a, words1, planes1), (g, words3, planes3)):
-                for s in range(S):
+            a, g = a_banks[step % 2], g_banks[step % 3]
+            for s in range(S):
+                for m, acc in enumerate((a, g)):
                     nc.tensor.matmul_mx(
                         out=acc[:],
                         lhsT=codes[s][:, cols].bitcast(FP8X4),
                         lhsT_scale=scales[s][:, cols],
-                        rhs=words[e][:, s, :].bitcast(FP4X4),
-                        rhs_scale=planes[:, e * S + s, :],
+                        rhs=words13[m, e, s].bitcast(FP4X4),
+                        rhs_scale=plane13(m, e, s),
                         start=(s == 0),
                         stop=(s == S - 1),
                     )
-            sig = work.tile([P, H], F32, name="sig")
-            nc.scalar.activation(sig[:], a[:], SIGMOID)
+            order, flat = "t (p u b) -> t u p b", "t (u p b) -> t u p b"
+            if step == 0:
+                sig = gathered[1][:, 2 * REST : 2 * REST + 2 * H].bitcast(F32)
+            else:
+                sig = work.tile([P, H], F32, name="sig")
+            nc.scalar.activation(sig[:].rearrange(flat, u=2, b=2), a[:].rearrange(order, u=2, b=2), SIGMOID)
             h = work.tile([P, H], BF16, name="h", align_bytes=64)
-            order = "t (p u b) -> t u p b"
             nc.vector.tensor_tensor(
-                h[:].rearrange("t (u p b) -> t u p b", u=2, b=2),
-                sig[:].rearrange(order, u=2, b=2),
+                h[:].rearrange(flat, u=2, b=2),
+                sig[:].rearrange(flat, u=2, b=2),
                 g[:].rearrange(order, u=2, b=2),
                 MULT,
             )
             hs[i] = h
 
-        def turn(i):
-            turned = psum1.tile([P, 2, P], F32, name="turned")
+        def turn(step):
+            i = ORDER[step]
+            turned = t_banks[step % 3][:, : 2 * P].rearrange("p (u c) -> p u c", u=2)
             words = hs[i][:].bitcast(F32)
             for u in range(2):
                 nc.tensor.transpose(turned[:, u, :], words[:, u * P : (u + 1) * P], ident[:])
             grouped = work.tile([P, 4 * P], BF16, name="h_grouped", align_bytes=64)
-            nc.scalar.copy(
-                grouped[:].bitcast(F32).rearrange("p (c u) -> p c u", u=2), turned[:].rearrange("p u c -> p c u")
+            move = nc.scalar.copy
+            move(
+                grouped[:].bitcast(F32).rearrange("p (c u) -> p c u", u=2), turned.rearrange("p u c -> p c u")
             )
             cols = slice(P * i, P * (i + 1))
             nc.vector.quantize_mx(out=h_codes[:, cols].bitcast(FP8X4), scales=h_scales[:, cols], in_=grouped[:])
@@ -202,72 +240,82 @@ def tile_moe_shr_glu_sigmoid_kernel(
             nc.tensor.matmul_mx(
                 out=acc,
                 lhsT=words2[e][:, 2 * P * c : 2 * P * (c + 1)].bitcast(FP4X4),
-                lhsT_scale=planes2[:, e, c * P : (c + 1) * P],
+                lhsT_scale=planes2[:, e * N + c * P : e * N + (c + 1) * P],
                 rhs=h_codes[:, lo:hi].bitcast(FP8X4),
                 rhs_scale=h_scales[:, lo:hi],
                 start=True,
                 stop=True,
             )
 
-        gated = {}
+        def route(lo, hi, chunks, bank):
+            n = (hi - lo) * C
+            for j, c in enumerate(chunks):
+                for e in range(lo, hi):
+                    at = j * n + (e - lo) * C
+                    second_layer(bank[:, at : at + C], e, c, e * C, (e + 1) * C)
+            y = work.tile([P, len(chunks) * n], F32, name="y_slots", bufs=4)
+            move = nc.scalar.copy
+            move(y[:], bank[:, : len(chunks) * n])
+            weights = gates[:, lo * C : hi * C]
+            for j, c in enumerate(chunks):
+                window = routed[c][:].indirect(offsets[:, 8 * lo : 8 * hi])
+                if GP:
+                    gy = work.tile([P, n], F32, name="gy", bufs=4)
+                    nc.gpsimd.tensor_tensor(gy[:], y[:, j * n : (j + 1) * n], weights, MULT)
+                    nc.vector.tensor_copy(window, gy[:])
+                else:
+                    nc.vector.tensor_tensor(window, y[:, j * n : (j + 1) * n], weights, MULT)
 
-        def gated_out(first, count, c):
-            bank = psum.tile([P, count * C], F32, name="y")
-            for j in range(count):
-                e = first + j
-                second_layer(bank[:, j * C : (j + 1) * C], e, c, e * C, (e + 1) * C)
-            y = work.tile([P, count * C], F32, name=f"y{count}", bufs=5)
-            nc.scalar.copy(y[:], bank[:])
-            gated[first, c] = y
+        shared = {}
 
-        def scatter(first, count, c):
-            nc.vector.tensor_tensor(
-                routed[c][:].indirect(offsets[:, 8 * first : 8 * (first + count)]),
-                gated[first, c][:],
-                gates[:, first * C : (first + count) * C],
-                MULT,
-            )
-
-        def finish(c, lo, hi):
-            if lo > 0 and c < 2:
-                bank = psum.tile([P, hi - lo], F32, name="a")
+        def shared_out(c, cols):
+            if cols == LOW:
+                bank = (g_banks[1], g_banks[2], g_banks[0], t_banks[1])[c][:]
             else:
-                bank = psum.tile([P, hi - lo], F32, name="y")
-            second_layer(bank[:], E, c, SLOTS + lo, SLOTS + hi)
-            nc.vector.tensor_tensor(results[c][:, lo:hi], bank[:], routed[c][:, lo:hi], ADD)
-            nc.sync.dma_start(out=out[c * P : (c + 1) * P, lo:hi], in_=results[c][:, lo:hi])
+                bank = a_banks[c // 2][:, 256 * (c % 2) : 256 * (c % 2 + 1)]
+            second_layer(bank, E, c, SLOTS + cols.start, SLOTS + cols.stop)
+            if GP and c < 3:
+                if cols == LOW:
+                    shared[c] = held.tile([P, T], F32, name=f"shared{c}")
+                nc.scalar.copy(shared[c][:, cols], bank)
+            else:
+                shared[c, cols.start] = bank
+
+        def finish(c):
+            if GP and c < 3:
+                nc.gpsimd.tensor_tensor(results[c][:], shared[c][:], routed[c][:], ADD)
+                nc.sync.dma_start(out=out[c * P : (c + 1) * P, :], in_=results[c][:])
+                return
+            for cols in (LOW, HIGH):
+                nc.vector.tensor_tensor(results[c][:, cols], shared[c, cols.start], routed[c][:, cols], ADD)
+                nc.sync.dma_start(out=out[c * P : (c + 1) * P, cols], in_=results[c][:, cols])
 
         groups = E + T // P
-        units = {
-            3: [(0, 1, 0)],
-            4: [(0, 1, 1)],
-            6: [(0, 1, 2), (0, 1, 3)],
-            7: [(1, 1, 0)],
-            8: [(1, 1, 1), (1, 1, 2)],
-            9: [(1, 1, 3), (2, 2, 0)],
-            10: [(2, 2, 1), (2, 2, 2)],
-            11: [(2, 2, 3)],
-        }
-        for step in range(groups + 3):
+        for s in range(S):
+            quantise_tokens(s, LOW, ("raw100", "tokens1")[s])
+        for s in range(S):
+            quantise_tokens(s, HIGH, f"tokens_high{s}")
+        for step in range(groups + 2):
             if step < groups:
                 first_layer(step)
             if step == 0:
-                for s in range(S):
-                    for u in range(2):
-                        gather(s, u, 1)
-                    quantise_slots(s, 1)
-            if step in (1, 3):
-                for s in range(S):
-                    cols = LOW if step == 1 else HIGH
-                    quantise_tokens(s, cols.start, cols.stop)
-            if 0 <= step - 2 < groups:
+                for u in range(2):
+                    gather(1, u, 0, REST)
+                quantise_slots(1, 0, REST, nc.scalar.copy, ((0, C), (C, REST)))
+            if step == 1:
+                turn(0)
+            if step >= 3:
                 turn(step - 2)
-            for unit in units.get(step, []):
-                gated_out(*unit)
-            for unit in units.get(step - 1, []):
-                scatter(*unit)
-            if step >= 11:
-                for c in (2 * (step - 11), 2 * (step - 11) + 1):
-                    finish(c, 0, 512)
+            if step in (2, 3):
+                route(LEAD, E, (2 * step - 4, 2 * step - 3), t_banks[(2, 0)[step - 2]])
+            if step in (7, 8):
+                route(0, 1, (2 * step - 14, 2 * step - 13), t_banks[(step - 3) % 3])
+            if step in (9, 10, 11):
+                route(1, LEAD, (step - 9,), t_banks[(step - 3) % 3])
+        route(1, LEAD, (3,), t_banks[0])
         for c in range(4):
-            finish(c, 512, 768)
+            shared_out(c, LOW)
+        for c in range(4):
+            shared_out(c, HIGH)
+        for c in range(4):
+            finish(c)

@@ -42,6 +42,9 @@ def tile_moe_shr_glu_sigmoid_kernel(
         offsets = held.tile([P, SLOTS // 16], U16, name="offsets")
         nc.sync.dma_start(offsets[:], offs)
 
+        warm = held.tile([P, 1], F32, name="warm")
+        nc.vector.memset(warm[:], 0.0)
+
         runs = ((LEAD, E + 1), (0, LEAD))
         planes13 = {}
         for lo, hi in runs:
@@ -67,8 +70,6 @@ def tile_moe_shr_glu_sigmoid_kernel(
             at = ((m * (hi - lo) + e - lo) * S + s) * H
             return planes13[lo][:, at : at + H]
 
-        warm = held.tile([P, 1], F32, name="warm")
-        nc.vector.memset(warm[:], 0.0)
         warmed = held.tile([P, 1], F32, name="warmed")
         nc.scalar.activation(warmed[:], warm[:], SIGMOID)
 
@@ -78,7 +79,10 @@ def tile_moe_shr_glu_sigmoid_kernel(
         routed = []
         for c in range(4):
             window = held.tile([P, T], F32, name=f"routed{c}")
-            nc.gpsimd.memset(window[:], 0.0)
+            if c < 2:
+                nc.scalar.copy(window[:], warm[:].to_broadcast([P, T]))
+            else:
+                nc.gpsimd.memset(window[:], 0.0)
             routed.append(window)
 
         rows = xT.rearrange("(s p u b) w -> s u p b w", s=S, p=P, u=2, b=2)
@@ -115,12 +119,12 @@ def tile_moe_shr_glu_sigmoid_kernel(
             load_first(m, LEAD, LEAD + 1)
         for m in range(2):
             load_first(m, E, E + 1)
-        for m in range(2):
-            load_run(nc.sync, m, *runs[1])
-            load_first(m, 0, 1)
         load_scales(nc.sync, planes2[:], w2_scales)
         load_second(LEAD, E + 1)
         nc.sync.dma_start(out=gates[:], in_=gate[:P, :])
+        for m in range(2):
+            load_run(nc.sync, m, *runs[1])
+            load_first(m, 0, 1)
         for e in range(1, LEAD):
             for m in range(2):
                 load_first(m, e, e + 1)
@@ -187,7 +191,7 @@ def tile_moe_shr_glu_sigmoid_kernel(
         h_scales = held.tile([P, SLOTS + T], U8, name="h_scales", align_bytes=64)
         hs = {}
 
-        ORDER = (LEAD, E, E + 1, E + 2, 0, 1, 2, E + 3, E + 4, E + 5)
+        ORDER = (LEAD, E, E + 1, E + 2, E + 3, 0, 1, 2, E + 4, E + 5)
 
         def first_layer(step):
             i = ORDER[step]
@@ -301,21 +305,26 @@ def tile_moe_shr_glu_sigmoid_kernel(
             if step == 0:
                 for u in range(2):
                     gather(1, u, 0, REST)
-                quantise_slots(1, 0, REST, nc.scalar.copy, ((0, C), (C, REST)))
+                quantise_slots(1, 0, REST, nc.vector.tensor_copy, ((0, C), (C, REST)))
             if step == 1:
                 turn(0)
             if step >= 3:
                 turn(step - 2)
-            if step in (2, 3):
-                route(LEAD, E, (2 * step - 4, 2 * step - 3), t_banks[(2, 0)[step - 2]])
-            if step in (7, 8):
-                route(0, 1, (2 * step - 14, 2 * step - 13), t_banks[(step - 3) % 3])
-            if step in (9, 10, 11):
-                route(1, LEAD, (step - 9,), t_banks[(step - 3) % 3])
-        route(1, LEAD, (3,), t_banks[0])
+            if step == 2:
+                route(LEAD, E, (0, 1), t_banks[2])
+            if step == 5:
+                route(LEAD, E, (2, 3), t_banks[(step - 3) % 3])
+            if step in (8, 9):
+                route(0, 1, (2 * step - 16, 2 * step - 15), t_banks[(step - 3) % 3])
+            if step in (10, 11):
+                route(1, LEAD, (step - 10,), t_banks[(step - 3) % 3])
         for c in range(4):
             shared_out(c, LOW)
         for c in range(4):
             shared_out(c, HIGH)
-        for c in range(4):
-            finish(c)
+        finish(0)
+        route(1, LEAD, (2,), t_banks[0])
+        finish(1)
+        route(1, LEAD, (3,), t_banks[2])
+        finish(2)
+        finish(3)

@@ -11,7 +11,7 @@ HALF = SLOTS // 2
 LOW, HIGH = slice(0, 512), slice(512, 768)
 FLOPS = 2 * (T + SLOTS) * (2 * K * H + H * N)
 GP = False
-LEAD = E - 1
+LEAD = E - 2
 REST = LEAD * C
 
 F32 = mybir.dt.float32
@@ -116,22 +116,27 @@ def tile_moe_shr_glu_sigmoid_kernel(
         gates = held.tile([P, SLOTS], F32, name="gates")
         for m in range(2):
             load_run(nc.sync, m, *runs[0])
-            load_first(m, LEAD, LEAD + 1)
-        for m in range(2):
-            load_first(m, E, E + 1)
+            load_first(m, E - 1, E)
+        for e in (LEAD, E):
+            for m in range(2):
+                load_first(m, e, e + 1)
         load_scales(nc.sync, planes2[:], w2_scales)
         load_second(LEAD, E + 1)
         nc.sync.dma_start(out=gates[:], in_=gate[:P, :])
         for m in range(2):
             load_run(nc.sync, m, *runs[1])
             load_first(m, 0, 1)
-        for e in range(1, LEAD):
-            for m in range(2):
-                load_first(m, e, e + 1)
+        for m in range(2):
+            load_first(m, 1, 2)
         load_second(0, LEAD)
 
-        slot_codes = [held.tile([P, SLOTS], U32, name=f"slot_codes{s}", align_bytes=64) for s in range(S)]
-        slot_scales = [held.tile([P, SLOTS], U8, name=f"slot_scales{s}", align_bytes=64) for s in range(S)]
+        slot_codes = held.tile([P, S * SLOTS], U32, name="slot_codes", align_bytes=64)
+        slot_scales = held.tile([P, S * SLOTS], U8, name="slot_scales", align_bytes=64)
+        slot_values = held.tile([P, 4 * S * SLOTS], BF16, name="slot_values", align_bytes=64)
+
+        def slot_at(s, slot):
+            return (slot // HALF * S + s) * HALF + slot % HALF
+
         pairs = [held.tile([P, 4 * T], BF16, name=f"pair{s}", align_bytes=64) for s in range(S)]
 
         def cast(s, u):
@@ -151,27 +156,26 @@ def tile_moe_shr_glu_sigmoid_kernel(
                 pairs[s][:, 2 * T * u : 2 * T * (u + 1)].bitcast(U32).indirect(offsets[:, lo // 16 : hi // 16]),
             )
 
-        def quantise_slots(s, lo, hi, interleave, cuts):
-            grouped = held.tile([P, 4 * (hi - lo)], BF16, name=f"slots{s}_{lo}", align_bytes=64)
-            interleave(
-                grouped[:].bitcast(F32).rearrange("p (c u) -> p c u", u=2),
-                gathered[s][:, : 2 * planes_apart[s]].bitcast(F32).rearrange("p (u c) -> p c u", u=2)[:, : hi - lo, :],
-            )
-            for a, b in cuts:
-                nc.vector.quantize_mx(
-                    out=slot_codes[s][:, a:b].bitcast(FP8X4),
-                    scales=slot_scales[s][:, a:b],
-                    in_=grouped[:, 4 * (a - lo) : 4 * (b - lo)],
-                )
+        def interleave_slots(s, lo, source, move):
+            at = 4 * slot_at(s, lo)
+            move(slot_values[:, at : at + 4 * HALF].bitcast(F32).rearrange("p (c u) -> p c u", u=2), source)
 
+        def quantise_slots(lo, hi):
+            nc.vector.quantize_mx(
+                out=slot_codes[:, lo:hi].bitcast(FP8X4), scales=slot_scales[:, lo:hi], in_=slot_values[:, 4 * lo : 4 * hi]
+            )
+
+        planes = [gathered[s][:, : 2 * planes_apart[s]].bitcast(F32).rearrange("p (u c) -> p c u", u=2) for s in range(S)]
         for u in range(2):
             cast(0, u)
             gather(0, u, 0, SLOTS)
-        quantise_slots(0, 0, SLOTS, nc.vector.tensor_copy, ((0, SLOTS),))
+        interleave_slots(0, HALF, planes[0][:, HALF:, :], nc.vector.tensor_copy)
+        quantise_slots(2 * HALF, 3 * HALF)
         for u in range(2):
             cast(1, u)
             gather(1, u, REST, SLOTS)
-        quantise_slots(1, REST, SLOTS, nc.vector.tensor_copy, ((REST, SLOTS),))
+        interleave_slots(1, HALF, planes[1], nc.vector.tensor_copy)
+        quantise_slots(3 * HALF, 4 * HALF)
 
         token_codes = [held.tile([P, T], U32, name=f"token_codes{s}", align_bytes=64) for s in range(S)]
         token_scales = [held.tile([P, T], U8, name=f"token_scales{s}", align_bytes=64) for s in range(S)]
@@ -191,21 +195,24 @@ def tile_moe_shr_glu_sigmoid_kernel(
         h_scales = held.tile([P, SLOTS + T], U8, name="h_scales", align_bytes=64)
         hs = {}
 
-        ORDER = (LEAD, E, E + 1, E + 2, E + 3, 0, 1, 2, E + 4, E + 5)
+        ORDER = (E - 1, LEAD, E, E + 1, E + 2, E + 3, 0, 1, E + 4, E + 5)
 
         def first_layer(step):
             i = ORDER[step]
             if i < E:
-                e, codes, scales, cols = i, slot_codes, slot_scales, slice(i * P, (i + 1) * P)
+                e = i
+                cols = [slice(slot_at(s, i * P), slot_at(s, i * P) + P) for s in range(S)]
+                codes, scales = [slot_codes] * S, [slot_scales] * S
             else:
-                e, codes, scales, cols = E, token_codes, token_scales, slice((i - E) * P, (i - E + 1) * P)
+                e, codes, scales = E, token_codes, token_scales
+                cols = [slice((i - E) * P, (i - E + 1) * P)] * S
             a, g = a_banks[step % 2], g_banks[step % 3]
             for s in range(S):
                 for m, acc in enumerate((a, g)):
                     nc.tensor.matmul_mx(
                         out=acc[:],
-                        lhsT=codes[s][:, cols].bitcast(FP8X4),
-                        lhsT_scale=scales[s][:, cols],
+                        lhsT=codes[s][:, cols[s]].bitcast(FP8X4),
+                        lhsT_scale=scales[s][:, cols[s]],
                         rhs=words13[m, e, s].bitcast(FP4X4),
                         rhs_scale=plane13(m, e, s),
                         start=(s == 0),
@@ -232,7 +239,10 @@ def tile_moe_shr_glu_sigmoid_kernel(
             words = hs[i][:].bitcast(F32)
             for u in range(2):
                 nc.tensor.transpose(turned[:, u, :], words[:, u * P : (u + 1) * P], ident[:])
-            grouped = work.tile([P, 4 * P], BF16, name="h_grouped", align_bytes=64)
+            if step < 2:
+                grouped = slot_values[:, 4 * HALF * step : 4 * HALF * step + 4 * P]
+            else:
+                grouped = work.tile([P, 4 * P], BF16, name="h_grouped", align_bytes=64)
             move = nc.scalar.copy
             move(
                 grouped[:].bitcast(F32).rearrange("p (c u) -> p c u", u=2), turned.rearrange("p u c -> p c u")
@@ -270,31 +280,43 @@ def tile_moe_shr_glu_sigmoid_kernel(
                 else:
                     nc.vector.tensor_tensor(window, y[:, j * n : (j + 1) * n], weights, MULT)
 
+        ON_TENSOR = 2
         shared = {}
 
         def shared_out(c, cols):
             if cols == LOW:
-                bank = (g_banks[1], g_banks[2], g_banks[0], t_banks[1])[c][:]
+                bank = (g_banks[1], g_banks[2], g_banks[0], a_banks[0])[c][:]
             else:
-                bank = a_banks[c // 2][:, 256 * (c % 2) : 256 * (c % 2 + 1)]
+                bank = (t_banks[1], a_banks[1])[c // 2][:, 256 * (c % 2) : 256 * (c % 2 + 1)]
             second_layer(bank, E, c, SLOTS + cols.start, SLOTS + cols.stop)
-            if GP and c < 3:
-                if cols == LOW:
-                    shared[c] = held.tile([P, T], F32, name=f"shared{c}")
-                nc.scalar.copy(shared[c][:, cols], bank)
+            if c < ON_TENSOR and cols == LOW:
+                shared[c, cols.start] = held.tile([P, 512], F32, name=f"shared{c}")
+                nc.scalar.copy(shared[c, cols.start][:], bank)
             else:
                 shared[c, cols.start] = bank
 
-        def finish(c):
-            if GP and c < 3:
-                nc.gpsimd.tensor_tensor(results[c][:], shared[c][:], routed[c][:], ADD)
-                nc.sync.dma_start(out=out[c * P : (c + 1) * P, :], in_=results[c][:])
-                return
-            for cols in (LOW, HIGH):
+        def finish(c, cols):
+            if c < ON_TENSOR and cols == LOW:
+                there, back = g_banks[1 + c % 2], (t_banks[0], t_banks[2])[c % 2]
+                for at in range(0, 512, P):
+                    block = slice(at, at + P)
+                    for first, part in ((True, shared[c, 0]), (False, routed[c])):
+                        nc.tensor.matmul(
+                            there[:, block], part[:, block], ident[:], start=first, stop=not first, is_transpose=True
+                        )
+                summed = work.tile([P, 512], F32, name="summed")
+                nc.scalar.copy(summed[:], there[:])
+                for at in range(0, 512, P):
+                    nc.tensor.transpose(back[:, at : at + P], summed[:, at : at + P], ident[:])
+                nc.scalar.copy(results[c][:, cols], back[:])
+                queue = nc.scalar
+            else:
                 nc.vector.tensor_tensor(results[c][:, cols], shared[c, cols.start], routed[c][:, cols], ADD)
-                nc.sync.dma_start(out=out[c * P : (c + 1) * P, cols], in_=results[c][:, cols])
+                queue = nc.sync
+            queue.dma_start(out=out[c * P : (c + 1) * P, cols], in_=results[c][:, cols])
 
         groups = E + T // P
+        REST_MOVE = nc.vector.tensor_copy
         for s in range(S):
             quantise_tokens(s, LOW, ("raw100", "tokens1")[s])
         for s in range(S):
@@ -305,26 +327,27 @@ def tile_moe_shr_glu_sigmoid_kernel(
             if step == 0:
                 for u in range(2):
                     gather(1, u, 0, REST)
-                quantise_slots(1, 0, REST, nc.vector.tensor_copy, ((0, C), (C, REST)))
+            if step == 2:
+                turn(1)
+                interleave_slots(0, 0, planes[0][:, :HALF, :], REST_MOVE)
+                interleave_slots(1, 0, planes[1], REST_MOVE)
+                quantise_slots(0, 2 * HALF)
             if step == 1:
                 turn(0)
-            if step >= 3:
+            if step >= 4:
                 turn(step - 2)
-            if step == 2:
-                route(LEAD, E, (0, 1), t_banks[2])
-            if step == 5:
-                route(LEAD, E, (2, 3), t_banks[(step - 3) % 3])
-            if step in (8, 9):
-                route(0, 1, (2 * step - 16, 2 * step - 15), t_banks[(step - 3) % 3])
+            if step in (3, 5, 7, 9):
+                route(LEAD, E, ((3, 5, 7, 9).index(step),), t_banks[step % 3])
+            if step == 9:
+                for c in range(2):
+                    shared_out(c, LOW)
             if step in (10, 11):
-                route(1, LEAD, (step - 10,), t_banks[(step - 3) % 3])
-        for c in range(4):
+                route(0, LEAD, ((10, 11).index(step),), t_banks[step % 3])
+        route(0, LEAD, (2, 3), t_banks[0])
+        for c in range(2, 4):
             shared_out(c, LOW)
         for c in range(4):
             shared_out(c, HIGH)
-        finish(0)
-        route(1, LEAD, (2,), t_banks[0])
-        finish(1)
-        route(1, LEAD, (3,), t_banks[2])
-        finish(2)
-        finish(3)
+        for c in range(4):
+            for cols in (LOW, HIGH):
+                finish(c, cols)

@@ -8,11 +8,11 @@ P = 128
 S = K // 512
 SLOTS = E * C
 HALF = SLOTS // 2
+CHUNKS = N // P
 LOW, HIGH = slice(0, 512), slice(512, 768)
-FLOPS = 2 * (T + SLOTS) * (2 * K * H + H * N)
-GP = False
 LEAD = E - 2
-REST = LEAD * C
+ON_TENSOR = 2
+FLOPS = 2 * (T + SLOTS) * (2 * K * H + H * N)
 
 F32 = mybir.dt.float32
 BF16 = mybir.dt.bfloat16
@@ -42,52 +42,50 @@ def tile_moe_shr_glu_sigmoid_kernel(
         offsets = held.tile([P, SLOTS // 16], U16, name="offsets")
         nc.sync.dma_start(offsets[:], offs)
 
-        warm = held.tile([P, 1], F32, name="warm")
-        nc.vector.memset(warm[:], 0.0)
+        zero = held.tile([P, 1], F32, name="warm")
+        nc.vector.memset(zero[:], 0.0)
 
         runs = ((LEAD, E + 1), (0, LEAD))
-        planes13 = {}
+        scales13 = {}
         for lo, hi in runs:
-            tile = held.tile([P, 2 * (hi - lo) * S * H], U8, name=f"planes13_{lo}", align_bytes=64)
-            for m in range(2):
-                nc.vector.memset(tile[:, m * (hi - lo) * S * H : (m + 1) * (hi - lo) * S * H].bitcast(I32), 0)
-            planes13[lo] = tile
-        planes2 = held.tile([P, (E + 1) * N], U8, name="planes2", align_bytes=64)
-        nc.vector.memset(planes2[:].bitcast(I32), 0)
-
-        def load_scales(queue, plane, scales):
-            rows = scales.bitcast(I32).rearrange("e s (q r) i -> r q (e s) i", r=4)
-            view = plane.bitcast(I32).rearrange("p (g i) -> p g i", i=H // 4)
-            for r in range(4):
-                queue.dma_start(out=view[r:P:32, :, :], in_=rows[r])
-
-        def load_run(queue, m, lo, hi):
             width = (hi - lo) * S * H
-            load_scales(queue, planes13[lo][:, m * width : (m + 1) * width], (w1_scales, w3_scales)[m][lo:hi])
+            tile = held.tile([P, 2 * width], U8, name=f"planes13_{lo}", align_bytes=64)
+            for m in range(2):
+                nc.vector.memset(tile[:, m * width : (m + 1) * width].bitcast(I32), 0)
+            scales13[lo] = tile
+        scales2 = held.tile([P, (E + 1) * N], U8, name="planes2", align_bytes=64)
+        nc.vector.memset(scales2[:].bitcast(I32), 0)
 
-        def plane13(m, e, s):
+        def load_scales(target, source):
+            rows = source.bitcast(I32).rearrange("e s (q r) i -> r q (e s) i", r=4)
+            view = target.bitcast(I32).rearrange("p (g i) -> p g i", i=H // 4)
+            for r in range(4):
+                nc.sync.dma_start(out=view[r:P:32, :, :], in_=rows[r])
+
+        def load_run(m, lo, hi):
+            width = (hi - lo) * S * H
+            load_scales(scales13[lo][:, m * width : (m + 1) * width], (w1_scales, w3_scales)[m][lo:hi])
+
+        def scale13(m, e, s):
             lo, hi = runs[0] if e >= LEAD else runs[1]
             at = ((m * (hi - lo) + e - lo) * S + s) * H
-            return planes13[lo][:, at : at + H]
-
-        warmed = held.tile([P, 1], F32, name="warmed")
-        nc.scalar.activation(warmed[:], warm[:], SIGMOID)
+            return scales13[lo][:, at : at + H]
 
         ident = held.tile([P, P], F32, name="ident")
         make_identity(nc, ident[:])
 
         routed = []
-        for c in range(4):
+        for c in range(CHUNKS):
             window = held.tile([P, T], F32, name=f"routed{c}")
-            if c < 2:
-                nc.scalar.copy(window[:], warm[:].to_broadcast([P, T]))
+            if c < CHUNKS // 2:
+                nc.scalar.copy(window[:], zero[:].to_broadcast([P, T]))
             else:
                 nc.gpsimd.memset(window[:], 0.0)
             routed.append(window)
 
         rows = xT.rearrange("(s p u b) w -> s u p b w", s=S, p=P, u=2, b=2)
-        pieces = {(s, u): (slice(0, T),) for s in range(S) for u in range(2)}
-        pieces[0, 0] = pieces[0, 1] = pieces[1, 1] = (LOW, HIGH)
+        pieces = {(s, u): (LOW, HIGH) for s in range(S) for u in range(2)}
+        pieces[1, 0] = (slice(0, T),)
         raws = {}
         for (s, u), cuts in pieces.items():
             for j, cols in enumerate(cuts):
@@ -115,16 +113,16 @@ def tile_moe_shr_glu_sigmoid_kernel(
 
         gates = held.tile([P, SLOTS], F32, name="gates")
         for m in range(2):
-            load_run(nc.sync, m, *runs[0])
+            load_run(m, *runs[0])
             load_first(m, E - 1, E)
         for e in (LEAD, E):
             for m in range(2):
                 load_first(m, e, e + 1)
-        load_scales(nc.sync, planes2[:], w2_scales)
+        load_scales(scales2[:], w2_scales)
         load_second(LEAD, E + 1)
         nc.sync.dma_start(out=gates[:], in_=gate[:P, :])
         for m in range(2):
-            load_run(nc.sync, m, *runs[1])
+            load_run(m, *runs[1])
             load_first(m, 0, 1)
         for m in range(2):
             load_first(m, 1, 2)
@@ -141,41 +139,43 @@ def tile_moe_shr_glu_sigmoid_kernel(
 
         def cast(s, u):
             paired = pairs[s][:, 2 * T * u : 2 * T * (u + 1)].rearrange("p (w b) -> p w b", b=2)
+            on_vector = LOW if s else HIGH
             for j, cols in enumerate(pieces[s, u]):
-                move = nc.vector.tensor_copy if cols == (LOW if s else HIGH) else nc.scalar.copy
+                move = nc.vector.tensor_copy if cols == on_vector else nc.scalar.copy
                 move(paired[:, cols, :], raws[s, u, j][:].rearrange("p b w -> p w b"))
 
         gathered = [held.tile([P, 4 * SLOTS], BF16, name=f"gathered{s}", align_bytes=64) for s in range(S)]
-
-        planes_apart = (2 * SLOTS, 2 * REST)
+        u_apart = (2 * SLOTS, 2 * HALF)
 
         def gather(s, u, lo, hi):
-            at = u * planes_apart[s]
+            at = u * u_apart[s]
             nc.vector.tensor_copy(
                 gathered[s][:, at : at + 2 * (hi - lo)].bitcast(U32),
                 pairs[s][:, 2 * T * u : 2 * T * (u + 1)].bitcast(U32).indirect(offsets[:, lo // 16 : hi // 16]),
             )
 
-        def interleave_slots(s, lo, source, move):
+        def interleave_slots(s, lo, source):
             at = 4 * slot_at(s, lo)
-            move(slot_values[:, at : at + 4 * HALF].bitcast(F32).rearrange("p (c u) -> p c u", u=2), source)
+            nc.vector.tensor_copy(
+                slot_values[:, at : at + 4 * HALF].bitcast(F32).rearrange("p (c u) -> p c u", u=2), source
+            )
 
         def quantise_slots(lo, hi):
             nc.vector.quantize_mx(
                 out=slot_codes[:, lo:hi].bitcast(FP8X4), scales=slot_scales[:, lo:hi], in_=slot_values[:, 4 * lo : 4 * hi]
             )
 
-        planes = [gathered[s][:, : 2 * planes_apart[s]].bitcast(F32).rearrange("p (u c) -> p c u", u=2) for s in range(S)]
+        by_slot = [gathered[s][:, : 2 * u_apart[s]].bitcast(F32).rearrange("p (u c) -> p c u", u=2) for s in range(S)]
         for u in range(2):
             cast(0, u)
             gather(0, u, 0, SLOTS)
-        interleave_slots(0, HALF, planes[0][:, HALF:, :], nc.vector.tensor_copy)
-        quantise_slots(2 * HALF, 3 * HALF)
+        interleave_slots(0, HALF, by_slot[0][:, HALF:, :])
+        quantise_slots(slot_at(0, HALF), slot_at(0, HALF) + HALF)
         for u in range(2):
             cast(1, u)
-            gather(1, u, REST, SLOTS)
-        interleave_slots(1, HALF, planes[1], nc.vector.tensor_copy)
-        quantise_slots(3 * HALF, 4 * HALF)
+            gather(1, u, HALF, SLOTS)
+        interleave_slots(1, HALF, by_slot[1])
+        quantise_slots(slot_at(1, HALF), slot_at(1, HALF) + HALF)
 
         token_codes = [held.tile([P, T], U32, name=f"token_codes{s}", align_bytes=64) for s in range(S)]
         token_scales = [held.tile([P, T], U8, name=f"token_scales{s}", align_bytes=64) for s in range(S)]
@@ -190,15 +190,15 @@ def tile_moe_shr_glu_sigmoid_kernel(
                 out=token_codes[s][:, cols].bitcast(FP8X4), scales=token_scales[s][:, cols], in_=grouped[:]
             )
 
-        results = [held.tile([P, T], F32, name=f"result{c}") for c in range(4)]
+        results = [held.tile([P, T], F32, name=f"result{c}") for c in range(CHUNKS)]
         h_codes = held.tile([P, SLOTS + T], U32, name="h_codes", align_bytes=64)
         h_scales = held.tile([P, SLOTS + T], U8, name="h_scales", align_bytes=64)
         hs = {}
 
-        ORDER = (E - 1, LEAD, E, E + 1, E + 2, E + 3, 0, 1, E + 4, E + 5)
+        order = (E - 1, LEAD, E, E + 1, E + 2, E + 3, 0, 1, E + 4, E + 5)
 
         def first_layer(step):
-            i = ORDER[step]
+            i = order[step]
             if i < E:
                 e = i
                 cols = [slice(slot_at(s, i * P), slot_at(s, i * P) + P) for s in range(S)]
@@ -214,37 +214,36 @@ def tile_moe_shr_glu_sigmoid_kernel(
                         lhsT=codes[s][:, cols[s]].bitcast(FP8X4),
                         lhsT_scale=scales[s][:, cols[s]],
                         rhs=words13[m, e, s].bitcast(FP4X4),
-                        rhs_scale=plane13(m, e, s),
+                        rhs_scale=scale13(m, e, s),
                         start=(s == 0),
                         stop=(s == S - 1),
                     )
-            order, flat = "t (p u b) -> t u p b", "t (u p b) -> t u p b"
+            natural, by_pair = "t (p u b) -> t u p b", "t (u p b) -> t u p b"
             if step == 0:
-                sig = gathered[1][:, 2 * REST : 2 * REST + 2 * H].bitcast(F32)
+                sig = gathered[1][:, 2 * HALF : 2 * HALF + 2 * H].bitcast(F32)
             else:
                 sig = work.tile([P, H], F32, name="sig")
-            nc.scalar.activation(sig[:].rearrange(flat, u=2, b=2), a[:].rearrange(order, u=2, b=2), SIGMOID)
+            nc.scalar.activation(sig[:].rearrange(by_pair, u=2, b=2), a[:].rearrange(natural, u=2, b=2), SIGMOID)
             h = work.tile([P, H], BF16, name="h", align_bytes=64)
             nc.vector.tensor_tensor(
-                h[:].rearrange(flat, u=2, b=2),
-                sig[:].rearrange(flat, u=2, b=2),
-                g[:].rearrange(order, u=2, b=2),
+                h[:].rearrange(by_pair, u=2, b=2),
+                sig[:].rearrange(by_pair, u=2, b=2),
+                g[:].rearrange(natural, u=2, b=2),
                 MULT,
             )
             hs[i] = h
 
         def turn(step):
-            i = ORDER[step]
+            i = order[step]
             turned = t_banks[step % 3][:, : 2 * P].rearrange("p (u c) -> p u c", u=2)
             words = hs[i][:].bitcast(F32)
             for u in range(2):
                 nc.tensor.transpose(turned[:, u, :], words[:, u * P : (u + 1) * P], ident[:])
-            if step < 2:
-                grouped = slot_values[:, 4 * HALF * step : 4 * HALF * step + 4 * P]
+            if step < S:
+                grouped = slot_values[:, 4 * slot_at(step, 0) : 4 * slot_at(step, 0) + 4 * P]
             else:
                 grouped = work.tile([P, 4 * P], BF16, name="h_grouped", align_bytes=64)
-            move = nc.scalar.copy
-            move(
+            nc.scalar.copy(
                 grouped[:].bitcast(F32).rearrange("p (c u) -> p c u", u=2), turned.rearrange("p u c -> p c u")
             )
             cols = slice(P * i, P * (i + 1))
@@ -254,7 +253,7 @@ def tile_moe_shr_glu_sigmoid_kernel(
             nc.tensor.matmul_mx(
                 out=acc,
                 lhsT=words2[e][:, 2 * P * c : 2 * P * (c + 1)].bitcast(FP4X4),
-                lhsT_scale=planes2[:, e * N + c * P : e * N + (c + 1) * P],
+                lhsT_scale=scales2[:, e * N + c * P : e * N + (c + 1) * P],
                 rhs=h_codes[:, lo:hi].bitcast(FP8X4),
                 rhs_scale=h_scales[:, lo:hi],
                 start=True,
@@ -268,45 +267,39 @@ def tile_moe_shr_glu_sigmoid_kernel(
                     at = j * n + (e - lo) * C
                     second_layer(bank[:, at : at + C], e, c, e * C, (e + 1) * C)
             y = work.tile([P, len(chunks) * n], F32, name="y_slots", bufs=4)
-            move = nc.scalar.copy
-            move(y[:], bank[:, : len(chunks) * n])
+            nc.scalar.copy(y[:], bank[:, : len(chunks) * n])
             weights = gates[:, lo * C : hi * C]
             for j, c in enumerate(chunks):
-                window = routed[c][:].indirect(offsets[:, 8 * lo : 8 * hi])
-                if GP:
-                    gy = work.tile([P, n], F32, name="gy", bufs=4)
-                    nc.gpsimd.tensor_tensor(gy[:], y[:, j * n : (j + 1) * n], weights, MULT)
-                    nc.vector.tensor_copy(window, gy[:])
-                else:
-                    nc.vector.tensor_tensor(window, y[:, j * n : (j + 1) * n], weights, MULT)
+                window = routed[c][:].indirect(offsets[:, lo * C // 16 : hi * C // 16])
+                nc.vector.tensor_tensor(window, y[:, j * n : (j + 1) * n], weights, MULT)
 
-        ON_TENSOR = 2
         shared = {}
 
         def shared_out(c, cols):
             if cols == LOW:
                 bank = (g_banks[1], g_banks[2], g_banks[0], a_banks[0])[c][:]
             else:
-                bank = (t_banks[1], a_banks[1])[c // 2][:, 256 * (c % 2) : 256 * (c % 2 + 1)]
+                width = HIGH.stop - HIGH.start
+                bank = (t_banks[1], a_banks[1])[c // 2][:, width * (c % 2) : width * (c % 2 + 1)]
             second_layer(bank, E, c, SLOTS + cols.start, SLOTS + cols.stop)
             if c < ON_TENSOR and cols == LOW:
-                shared[c, cols.start] = held.tile([P, 512], F32, name=f"shared{c}")
+                shared[c, cols.start] = held.tile([P, LOW.stop], F32, name=f"shared{c}")
                 nc.scalar.copy(shared[c, cols.start][:], bank)
             else:
                 shared[c, cols.start] = bank
 
         def finish(c, cols):
             if c < ON_TENSOR and cols == LOW:
-                there, back = g_banks[1 + c % 2], (t_banks[0], t_banks[2])[c % 2]
-                for at in range(0, 512, P):
+                there, back = g_banks[1 + c], t_banks[2 * c]
+                for at in range(0, LOW.stop, P):
                     block = slice(at, at + P)
                     for first, part in ((True, shared[c, 0]), (False, routed[c])):
                         nc.tensor.matmul(
                             there[:, block], part[:, block], ident[:], start=first, stop=not first, is_transpose=True
                         )
-                summed = work.tile([P, 512], F32, name="summed")
+                summed = work.tile([P, LOW.stop], F32, name="summed")
                 nc.scalar.copy(summed[:], there[:])
-                for at in range(0, 512, P):
+                for at in range(0, LOW.stop, P):
                     nc.tensor.transpose(back[:, at : at + P], summed[:, at : at + P], ident[:])
                 nc.scalar.copy(results[c][:, cols], back[:])
                 queue = nc.scalar
@@ -315,39 +308,38 @@ def tile_moe_shr_glu_sigmoid_kernel(
                 queue = nc.sync
             queue.dma_start(out=out[c * P : (c + 1) * P, cols], in_=results[c][:, cols])
 
-        groups = E + T // P
-        REST_MOVE = nc.vector.tensor_copy
         for s in range(S):
             quantise_tokens(s, LOW, ("raw100", "tokens1")[s])
         for s in range(S):
             quantise_tokens(s, HIGH, f"tokens_high{s}")
+
+        groups = len(order)
         for step in range(groups + 2):
             if step < groups:
                 first_layer(step)
             if step == 0:
                 for u in range(2):
-                    gather(1, u, 0, REST)
+                    gather(1, u, 0, HALF)
+            if step in (1, 2):
+                turn(step - 1)
             if step == 2:
-                turn(1)
-                interleave_slots(0, 0, planes[0][:, :HALF, :], REST_MOVE)
-                interleave_slots(1, 0, planes[1], REST_MOVE)
-                quantise_slots(0, 2 * HALF)
-            if step == 1:
-                turn(0)
+                interleave_slots(0, 0, by_slot[0][:, :HALF, :])
+                interleave_slots(1, 0, by_slot[1])
+                quantise_slots(0, S * HALF)
             if step >= 4:
                 turn(step - 2)
-            if step in (3, 5, 7, 9):
-                route(LEAD, E, ((3, 5, 7, 9).index(step),), t_banks[step % 3])
-            if step == 9:
-                for c in range(2):
+            if step % 2 == 1 and 3 <= step < groups:
+                route(LEAD, E, ((step - 3) // 2,), t_banks[step % 3])
+            if step == groups - 1:
+                for c in range(ON_TENSOR):
                     shared_out(c, LOW)
-            if step in (10, 11):
-                route(0, LEAD, ((10, 11).index(step),), t_banks[step % 3])
+            if step >= groups:
+                route(0, LEAD, (step - groups,), t_banks[step % 3])
         route(0, LEAD, (2, 3), t_banks[0])
-        for c in range(2, 4):
+        for c in range(ON_TENSOR, CHUNKS):
             shared_out(c, LOW)
-        for c in range(4):
+        for c in range(CHUNKS):
             shared_out(c, HIGH)
-        for c in range(4):
+        for c in range(CHUNKS):
             for cols in (LOW, HIGH):
                 finish(c, cols)

@@ -10,7 +10,7 @@ SLOTS = E * C
 HALF = SLOTS // 2
 CHUNKS = N // P
 LOW, HIGH = slice(0, 512), slice(512, 768)
-LEAD = E - 2
+LEAD = E - 1
 ON_TENSOR = 2
 FLOPS = 2 * (T + SLOTS) * (2 * K * H + H * N)
 
@@ -35,26 +35,20 @@ def tile_moe_shr_glu_sigmoid_kernel(
         held = ctx.enter_context(tc.tile_pool(name="held", bufs=1))
         work = ctx.enter_context(tc.tile_pool(name="work", bufs=3))
         psum = ctx.enter_context(tc.psum_pool(name="psum", bufs=1))
-        a_banks = [psum.tile([P, 512], F32, name=f"a{j}") for j in range(2)]
+        a_banks = [psum.tile([P, 512], F32, name=f"a{j}") for j in range(3)]
+        x_banks = [psum.tile([P, 512], F32, name=f"x{j}") for j in range(2)]
         g_banks = [psum.tile([P, 512], F32, name=f"g{j}") for j in range(3)]
-        t_banks = [psum.tile([P, 512], F32, name=f"t{j}") for j in range(3)]
 
-        offsets = held.tile([P, SLOTS // 16], U16, name="offsets")
-        nc.sync.dma_start(offsets[:], offs)
-
-        zero = held.tile([P, 1], F32, name="warm")
+        zero = held.tile([P, 1], F32, name="zero")
         nc.vector.memset(zero[:], 0.0)
 
         runs = ((LEAD, E + 1), (0, LEAD))
         scales13 = {}
         for lo, hi in runs:
-            width = (hi - lo) * S * H
-            tile = held.tile([P, 2 * width], U8, name=f"planes13_{lo}", align_bytes=64)
-            for m in range(2):
-                nc.vector.memset(tile[:, m * width : (m + 1) * width].bitcast(I32), 0)
-            scales13[lo] = tile
+            scales13[lo] = held.tile([P, 2 * (hi - lo) * S * H], U8, name=f"planes13_{lo}", align_bytes=64)
         scales2 = held.tile([P, (E + 1) * N], U8, name="planes2", align_bytes=64)
-        nc.vector.memset(scales2[:].bitcast(I32), 0)
+        for tile in (scales13[LEAD], scales2, scales13[0]):
+            nc.vector.memset(tile[:].bitcast(I32), 0)
 
         def load_scales(target, source):
             rows = source.bitcast(I32).rearrange("e s (q r) i -> r q (e s) i", r=4)
@@ -62,9 +56,10 @@ def tile_moe_shr_glu_sigmoid_kernel(
             for r in range(4):
                 nc.sync.dma_start(out=view[r:P:32, :, :], in_=rows[r])
 
-        def load_run(m, lo, hi):
+        def load_run(lo, hi):
             width = (hi - lo) * S * H
-            load_scales(scales13[lo][:, m * width : (m + 1) * width], (w1_scales, w3_scales)[m][lo:hi])
+            for m in range(2):
+                load_scales(scales13[lo][:, m * width : (m + 1) * width], (w1_scales, w3_scales)[m][lo:hi])
 
         def scale13(m, e, s):
             lo, hi = runs[0] if e >= LEAD else runs[1]
@@ -84,24 +79,33 @@ def tile_moe_shr_glu_sigmoid_kernel(
             routed.append(window)
 
         rows = xT.rearrange("(s p u b) w -> s u p b w", s=S, p=P, u=2, b=2)
-        pieces = {(s, u): (LOW, HIGH) for s in range(S) for u in range(2)}
-        pieces[1, 0] = (slice(0, T),)
+        offsets = held.tile([P, SLOTS // 16], U16, name="offsets")
+        HALVES = (slice(0, T // 2), slice(T // 2, T))
         raws = {}
-        for (s, u), cuts in pieces.items():
-            for j, cols in enumerate(cuts):
-                raw = held.tile([P, 2, cols.stop - cols.start], F32, name=f"raw{s}{u}{j}", align_bytes=64)
-                nc.sync.dma_start(out=raw[:], in_=rows[s, u][:, :, cols])
-                raws[s, u, j] = raw
+        for s in range(S):
+            for u in range(2):
+                if s == 0 and u == 0:
+                    for cols in HALVES:
+                        raw = held.tile([P, 2, cols.stop - cols.start], F32, name=f"raw00_{cols.start}", align_bytes=64)
+                        nc.sync.dma_start(out=raw[:], in_=rows[s, u][:, :, cols])
+                        raws[s, u, cols.start] = raw[:]
+                    nc.sync.dma_start(offsets[:], offs)
+                else:
+                    raw = held.tile([P, 2, T], F32, name=f"raw{s}{u}", align_bytes=64)
+                    nc.sync.dma_start(out=raw[:], in_=rows[s, u])
+                    for cols in HALVES:
+                        raws[s, u, cols.start] = raw[:, :, cols]
 
         words13, words2 = {}, {}
 
-        def load_first(m, lo, hi):
-            tile = held.tile([P, (hi - lo) * S, 2 * H], U8, name=f"w13_{m}{lo}", align_bytes=64)
-            source = (w1_words, w3_words)[m][lo:hi]
-            nc.sync.dma_start(out=tile[:].bitcast(I32), in_=source.bitcast(I32).rearrange("e s p b -> p (e s) b"))
-            for e in range(lo, hi):
-                for s in range(S):
-                    words13[m, e, s] = tile[:, (e - lo) * S + s, :]
+        def load_first(lo, hi):
+            for m in range(2):
+                tile = held.tile([P, (hi - lo) * S, 2 * H], U8, name=f"w13_{m}{lo}", align_bytes=64)
+                source = (w1_words, w3_words)[m][lo:hi]
+                nc.sync.dma_start(out=tile[:].bitcast(I32), in_=source.bitcast(I32).rearrange("e s p b -> p (e s) b"))
+                for e in range(lo, hi):
+                    for s in range(S):
+                        words13[m, e, s] = tile[:, (e - lo) * S + s, :]
 
         def load_second(lo, hi):
             tile = held.tile([P, hi - lo, 2 * N], U8, name=f"w2_{lo}", align_bytes=64)
@@ -112,115 +116,117 @@ def tile_moe_shr_glu_sigmoid_kernel(
                 words2[e] = tile[:, e - lo, :]
 
         gates = held.tile([P, SLOTS], F32, name="gates")
-        for m in range(2):
-            load_run(m, *runs[0])
-            load_first(m, E - 1, E)
-        for e in (LEAD, E):
-            for m in range(2):
-                load_first(m, e, e + 1)
+        load_first(LEAD, E)
+        load_run(*runs[0])
+        load_first(E, E + 1)
         load_scales(scales2[:], w2_scales)
         load_second(LEAD, E + 1)
         nc.sync.dma_start(out=gates[:], in_=gate[:P, :])
-        for m in range(2):
-            load_run(m, *runs[1])
-            load_first(m, 0, 1)
-        for m in range(2):
-            load_first(m, 1, 2)
+        load_run(*runs[1])
+        load_first(2, 3)
+        load_first(1, 2)
+        load_first(0, 1)
         load_second(0, LEAD)
 
+        REST = LEAD * C
         slot_codes = held.tile([P, S * SLOTS], U32, name="slot_codes", align_bytes=64)
         slot_scales = held.tile([P, S * SLOTS], U8, name="slot_scales", align_bytes=64)
-        slot_values = held.tile([P, 4 * S * SLOTS], BF16, name="slot_values", align_bytes=64)
+        pairs = held.tile([P, 8 * T], BF16, name="pairs", align_bytes=64)
 
-        def slot_at(s, slot):
-            return (slot // HALF * S + s) * HALF + slot % HALF
-
-        pairs = [held.tile([P, 4 * T], BF16, name=f"pair{s}", align_bytes=64) for s in range(S)]
+        def plane(s, u):
+            at = 2 * T * (2 * s + u)
+            return pairs[:, at : at + 2 * T]
 
         def cast(s, u):
-            paired = pairs[s][:, 2 * T * u : 2 * T * (u + 1)].rearrange("p (w b) -> p w b", b=2)
-            on_vector = LOW if s else HIGH
-            for j, cols in enumerate(pieces[s, u]):
-                move = nc.vector.tensor_copy if cols == on_vector else nc.scalar.copy
-                move(paired[:, cols, :], raws[s, u, j][:].rearrange("p b w -> p w b"))
+            paired = plane(s, u).rearrange("p (w b) -> p w b", b=2)
+            for cols, move in zip(HALVES, (nc.scalar.copy, nc.vector.tensor_copy)):
+                move(paired[:, cols, :], raws[s, u, cols.start].rearrange("p b w -> p w b"))
 
-        gathered = [held.tile([P, 4 * SLOTS], BF16, name=f"gathered{s}", align_bytes=64) for s in range(S)]
-        u_apart = (2 * SLOTS, 2 * HALF)
+        def gather(target, s, u, lo, hi):
+            nc.vector.tensor_copy(target, plane(s, u).bitcast(U32).indirect(offsets[:, lo // 16 : hi // 16]))
 
-        def gather(s, u, lo, hi):
-            at = u * u_apart[s]
-            nc.vector.tensor_copy(
-                gathered[s][:, at : at + 2 * (hi - lo)].bitcast(U32),
-                pairs[s][:, 2 * T * u : 2 * T * (u + 1)].bitcast(U32).indirect(offsets[:, lo // 16 : hi // 16]),
+        def quantise_slots(s, lo, values):
+            cols = slice(s * SLOTS + lo, s * SLOTS + lo + values.shape[1] // 4)
+            nc.vector.quantize_mx(out=slot_codes[:, cols].bitcast(FP8X4), scales=slot_scales[:, cols], in_=values)
+
+        gathered = [held.tile([P, 4 * REST], BF16, name=f"gathered{s}", align_bytes=64) for s in range(S)]
+
+        def gather_rest(s, u):
+            gather(gathered[s][:, 2 * REST * u : 2 * REST * (u + 1)].bitcast(U32), s, u, 0, REST)
+
+        for s in range(S):
+            lead = held.tile([P, 4 * C], BF16, name=f"lead{s}", align_bytes=64)
+            for u in range(2):
+                cast(s, u)
+                gather(lead[:].bitcast(U32).rearrange("p (c u) -> p c u", u=2)[:, :, u], s, u, REST, SLOTS)
+                if s == 0:
+                    gather_rest(s, u)
+            quantise_slots(s, REST, lead[:])
+
+        def finish_slots(s, move, tag):
+            values = held.tile([P, 4 * REST], BF16, name=tag, align_bytes=64)
+            move(
+                values[:].bitcast(F32).rearrange("p (c u) -> p c u", u=2),
+                gathered[s][:].bitcast(F32).rearrange("p (u c) -> p c u", u=2),
             )
+            quantise_slots(s, C, values[:, 4 * C :])
+            quantise_slots(s, 0, values[:, : 4 * C])
 
-        def interleave_slots(s, lo, source):
-            at = 4 * slot_at(s, lo)
-            nc.vector.tensor_copy(
-                slot_values[:, at : at + 4 * HALF].bitcast(F32).rearrange("p (c u) -> p c u", u=2), source
-            )
+        BLOCK = 256
+        token_codes = held.tile([P, S * T], U32, name="token_codes", align_bytes=64)
+        token_scales = held.tile([P, S * T], U8, name="token_scales", align_bytes=64)
+        grouped_tokens = [
+            held.tile([P, 4 * S * BLOCK], BF16, name=f"tokens{b}", align_bytes=64)[:] for b in range(T // BLOCK)
+        ]
 
-        def quantise_slots(lo, hi):
-            nc.vector.quantize_mx(
-                out=slot_codes[:, lo:hi].bitcast(FP8X4), scales=slot_scales[:, lo:hi], in_=slot_values[:, 4 * lo : 4 * hi]
-            )
+        def quantise_tokens(b):
+            grouped = grouped_tokens[b]
+            for s in range(S):
+                both = pairs[:, 4 * T * s : 4 * T * (s + 1)].bitcast(F32).rearrange("p (u w) -> p w u", u=2)
+                nc.scalar.copy(
+                    grouped[:, 4 * BLOCK * s : 4 * BLOCK * (s + 1)].bitcast(F32).rearrange("p (w u) -> p w u", u=2),
+                    both[:, b * BLOCK : (b + 1) * BLOCK, :],
+                )
+            cols = slice(S * BLOCK * b, S * BLOCK * (b + 1))
+            nc.vector.quantize_mx(out=token_codes[:, cols].bitcast(FP8X4), scales=token_scales[:, cols], in_=grouped)
 
-        by_slot = [gathered[s][:, : 2 * u_apart[s]].bitcast(F32).rearrange("p (u c) -> p c u", u=2) for s in range(S)]
-        for u in range(2):
-            cast(0, u)
-            gather(0, u, 0, SLOTS)
-        interleave_slots(0, HALF, by_slot[0][:, HALF:, :])
-        quantise_slots(slot_at(0, HALF), slot_at(0, HALF) + HALF)
-        for u in range(2):
-            cast(1, u)
-            gather(1, u, HALF, SLOTS)
-        interleave_slots(1, HALF, by_slot[1])
-        quantise_slots(slot_at(1, HALF), slot_at(1, HALF) + HALF)
-
-        token_codes = [held.tile([P, T], U32, name=f"token_codes{s}", align_bytes=64) for s in range(S)]
-        token_scales = [held.tile([P, T], U8, name=f"token_scales{s}", align_bytes=64) for s in range(S)]
-
-        def quantise_tokens(s, cols, tag):
-            grouped = held.tile([P, 4 * (cols.stop - cols.start)], BF16, name=tag, align_bytes=64)
-            nc.scalar.copy(
-                grouped[:].bitcast(F32).rearrange("p (w u) -> p w u", u=2),
-                pairs[s][:].bitcast(F32).rearrange("p (u w) -> p w u", u=2)[:, cols, :],
-            )
-            nc.vector.quantize_mx(
-                out=token_codes[s][:, cols].bitcast(FP8X4), scales=token_scales[s][:, cols], in_=grouped[:]
-            )
+        quantise_tokens(0)
+        quantise_tokens(1)
+        finish_slots(0, nc.scalar.copy, "raw11")
 
         results = [held.tile([P, T], F32, name=f"result{c}") for c in range(CHUNKS)]
         h_codes = held.tile([P, SLOTS + T], U32, name="h_codes", align_bytes=64)
         h_scales = held.tile([P, SLOTS + T], U8, name="h_scales", align_bytes=64)
         hs = {}
 
-        order = (E - 1, LEAD, E, E + 1, E + 2, E + 3, 0, 1, E + 4, E + 5)
+        order = (3, E, E + 1, E + 2, E + 3, 2, 1, 0, E + 4, E + 5)
+
+        borrowed = {0: gathered[1][:, REST - 128 : REST - 128 + 2 * H], 1: grouped_tokens[2][:, H : 3 * H]}
 
         def first_layer(step):
             i = order[step]
             if i < E:
-                e = i
-                cols = [slice(slot_at(s, i * P), slot_at(s, i * P) + P) for s in range(S)]
-                codes, scales = [slot_codes] * S, [slot_scales] * S
+                e, codes, scales = i, slot_codes, slot_scales
+                starts = [s * SLOTS + i * C for s in range(S)]
             else:
                 e, codes, scales = E, token_codes, token_scales
-                cols = [slice((i - E) * P, (i - E + 1) * P)] * S
-            a, g = a_banks[step % 2], g_banks[step % 3]
+                starts = [((i - E) // 2 * S + s) * BLOCK + (i - E) % 2 * P for s in range(S)]
+            a, g = a_banks[step % 3], g_banks[(0, 1, 0, 2, 1, 0, 2, 1, 0, 2)[step]]
             for s in range(S):
+                cols = slice(starts[s], starts[s] + P)
                 for m, acc in enumerate((a, g)):
                     nc.tensor.matmul_mx(
                         out=acc[:],
-                        lhsT=codes[s][:, cols[s]].bitcast(FP8X4),
-                        lhsT_scale=scales[s][:, cols[s]],
+                        lhsT=codes[:, cols].bitcast(FP8X4),
+                        lhsT_scale=scales[:, cols],
                         rhs=words13[m, e, s].bitcast(FP4X4),
                         rhs_scale=scale13(m, e, s),
                         start=(s == 0),
                         stop=(s == S - 1),
                     )
             natural, by_pair = "t (p u b) -> t u p b", "t (u p b) -> t u p b"
-            if step == 0:
-                sig = gathered[1][:, 2 * HALF : 2 * HALF + 2 * H].bitcast(F32)
+            if step in borrowed:
+                sig = borrowed[step].bitcast(F32)
             else:
                 sig = work.tile([P, H], F32, name="sig")
             nc.scalar.activation(sig[:].rearrange(by_pair, u=2, b=2), a[:].rearrange(natural, u=2, b=2), SIGMOID)
@@ -233,16 +239,13 @@ def tile_moe_shr_glu_sigmoid_kernel(
             )
             hs[i] = h
 
-        def turn(step):
+        def turn(step, bank):
             i = order[step]
-            turned = t_banks[step % 3][:, : 2 * P].rearrange("p (u c) -> p u c", u=2)
+            turned = bank[:, : 2 * P].rearrange("p (u c) -> p u c", u=2)
             words = hs[i][:].bitcast(F32)
             for u in range(2):
                 nc.tensor.transpose(turned[:, u, :], words[:, u * P : (u + 1) * P], ident[:])
-            if step < S:
-                grouped = slot_values[:, 4 * slot_at(step, 0) : 4 * slot_at(step, 0) + 4 * P]
-            else:
-                grouped = work.tile([P, 4 * P], BF16, name="h_grouped", align_bytes=64)
+            grouped = work.tile([P, 4 * P], BF16, name="h_grouped", align_bytes=64)
             nc.scalar.copy(
                 grouped[:].bitcast(F32).rearrange("p (c u) -> p c u", u=2), turned.rearrange("p u c -> p c u")
             )
@@ -266,7 +269,7 @@ def tile_moe_shr_glu_sigmoid_kernel(
                 for e in range(lo, hi):
                     at = j * n + (e - lo) * C
                     second_layer(bank[:, at : at + C], e, c, e * C, (e + 1) * C)
-            y = work.tile([P, len(chunks) * n], F32, name="y_slots", bufs=4)
+            y = held.tile([P, len(chunks) * n], F32, name=f"y{lo}{hi}{chunks[0]}")
             nc.scalar.copy(y[:], bank[:, : len(chunks) * n])
             weights = gates[:, lo * C : hi * C]
             for j, c in enumerate(chunks):
@@ -277,10 +280,10 @@ def tile_moe_shr_glu_sigmoid_kernel(
 
         def shared_out(c, cols):
             if cols == LOW:
-                bank = (g_banks[1], g_banks[2], g_banks[0], a_banks[0])[c][:]
+                bank = (a_banks[2], x_banks[1], g_banks[2], x_banks[0])[c][:]
             else:
                 width = HIGH.stop - HIGH.start
-                bank = (t_banks[1], a_banks[1])[c // 2][:, width * (c % 2) : width * (c % 2 + 1)]
+                bank = (x_banks[1], a_banks[0])[c // 2][:, width * (c % 2) : width * (c % 2 + 1)]
             second_layer(bank, E, c, SLOTS + cols.start, SLOTS + cols.stop)
             if c < ON_TENSOR and cols == LOW:
                 shared[c, cols.start] = held.tile([P, LOW.stop], F32, name=f"shared{c}")
@@ -290,7 +293,7 @@ def tile_moe_shr_glu_sigmoid_kernel(
 
         def finish(c, cols):
             if c < ON_TENSOR and cols == LOW:
-                there, back = g_banks[1 + c], t_banks[2 * c]
+                there, back = (g_banks[1], g_banks[0])[c], (a_banks[1], g_banks[1])[c]
                 for at in range(0, LOW.stop, P):
                     block = slice(at, at + P)
                     for first, part in ((True, shared[c, 0]), (False, routed[c])):
@@ -308,38 +311,47 @@ def tile_moe_shr_glu_sigmoid_kernel(
                 queue = nc.sync
             queue.dma_start(out=out[c * P : (c + 1) * P, cols], in_=results[c][:, cols])
 
-        for s in range(S):
-            quantise_tokens(s, LOW, ("raw100", "tokens1")[s])
-        for s in range(S):
-            quantise_tokens(s, HIGH, f"tokens_high{s}")
-
-        groups = len(order)
-        for step in range(groups + 2):
-            if step < groups:
-                first_layer(step)
-            if step == 0:
-                for u in range(2):
-                    gather(1, u, 0, HALF)
-            if step in (1, 2):
-                turn(step - 1)
-            if step == 2:
-                interleave_slots(0, 0, by_slot[0][:, :HALF, :])
-                interleave_slots(1, 0, by_slot[1])
-                quantise_slots(0, S * HALF)
-            if step >= 4:
-                turn(step - 2)
-            if step % 2 == 1 and 3 <= step < groups:
-                route(LEAD, E, ((step - 3) // 2,), t_banks[step % 3])
-            if step == groups - 1:
-                for c in range(ON_TENSOR):
-                    shared_out(c, LOW)
-            if step >= groups:
-                route(0, LEAD, (step - groups,), t_banks[step % 3])
-        route(0, LEAD, (2, 3), t_banks[0])
+        first_layer(0)
+        for u in range(2):
+            gather_rest(1, u)
+        first_layer(1)
+        turn(0, x_banks[0])
+        route(3, 4, (0, 1), x_banks[1])
+        finish_slots(1, nc.vector.tensor_copy, "rest1")
+        first_layer(2)
+        turn(1, x_banks[0])
+        quantise_tokens(2)
+        first_layer(3)
+        turn(2, x_banks[0])
+        first_layer(4)
+        turn(3, x_banks[0])
+        first_layer(5)
+        route(3, 4, (2, 3), a_banks[2])
+        turn(5, x_banks[0])
+        first_layer(6)
+        turn(4, a_banks[2])
+        turn(6, x_banks[1])
+        route(2, 3, (0, 1), a_banks[0])
+        first_layer(7)
+        turn(7, x_banks[0])
+        route(1, 2, (0, 1), a_banks[1])
+        for c in range(ON_TENSOR):
+            shared_out(c, LOW)
+        first_layer(8)
+        first_layer(9)
+        route(0, 1, (0, 1), a_banks[2])
+        turn(8, x_banks[0])
+        turn(9, x_banks[1])
+        route(0, LEAD, (2,), a_banks[0])
+        for c in range(ON_TENSOR):
+            finish(c, LOW)
+        route(0, LEAD, (3,), a_banks[2])
         for c in range(ON_TENSOR, CHUNKS):
             shared_out(c, LOW)
         for c in range(CHUNKS):
             shared_out(c, HIGH)
-        for c in range(CHUNKS):
+        for c in range(ON_TENSOR):
+            finish(c, HIGH)
+        for c in range(ON_TENSOR, CHUNKS):
             for cols in (LOW, HIGH):
                 finish(c, cols)

@@ -41,13 +41,16 @@ def tile_moe_shr_glu_sigmoid_kernel(
 
         zero = held.tile([P, 1], F32, name="zero")
         nc.vector.memset(zero[:], 0.0)
+        warm = held.tile([P, 1], F32, name="warm")
+        nc.scalar.activation(warm[:], zero[:], SIGMOID)
 
         runs = ((LEAD, E + 1), (0, LEAD))
         scales13 = {}
         for lo, hi in runs:
-            scales13[lo] = held.tile([P, 2 * (hi - lo) * S * H], U8, name=f"planes13_{lo}", align_bytes=64)
+            for m in range(2):
+                scales13[m, lo] = held.tile([P, (hi - lo) * S * H], U8, name=f"planes13_{m}{lo}", align_bytes=64)
         scales2 = held.tile([P, (E + 1) * N], U8, name="planes2", align_bytes=64)
-        for tile in (scales13[LEAD], scales2, scales13[0]):
+        for tile in (scales13[0, LEAD], scales13[1, LEAD], scales2, scales13[0, 0], scales13[1, 0]):
             nc.vector.memset(tile[:].bitcast(I32), 0)
 
         def load_scales(target, source):
@@ -56,15 +59,13 @@ def tile_moe_shr_glu_sigmoid_kernel(
             for r in range(4):
                 nc.sync.dma_start(out=view[r:P:32, :, :], in_=rows[r])
 
-        def load_run(lo, hi):
-            width = (hi - lo) * S * H
-            for m in range(2):
-                load_scales(scales13[lo][:, m * width : (m + 1) * width], (w1_scales, w3_scales)[m][lo:hi])
+        def load_run(m, lo, hi):
+            load_scales(scales13[m, lo][:], (w1_scales, w3_scales)[m][lo:hi])
 
         def scale13(m, e, s):
-            lo, hi = runs[0] if e >= LEAD else runs[1]
-            at = ((m * (hi - lo) + e - lo) * S + s) * H
-            return scales13[lo][:, at : at + H]
+            lo = LEAD if e >= LEAD else 0
+            at = ((e - lo) * S + s) * H
+            return scales13[m, lo][:, at : at + H]
 
         ident = held.tile([P, P], F32, name="ident")
         make_identity(nc, ident[:])
@@ -95,11 +96,13 @@ def tile_moe_shr_glu_sigmoid_kernel(
                     nc.sync.dma_start(out=raw[:], in_=rows[s, u])
                     for cols in HALVES:
                         raws[s, u, cols.start] = raw[:, :, cols]
+                if (s, u) == (0, 1):
+                    load_run(0, *runs[0])
 
         words13, words2 = {}, {}
 
-        def load_first(lo, hi):
-            for m in range(2):
+        def load_first(lo, hi, matrices=(0, 1)):
+            for m in matrices:
                 tile = held.tile([P, (hi - lo) * S, 2 * H], U8, name=f"w13_{m}{lo}", align_bytes=64)
                 source = (w1_words, w3_words)[m][lo:hi]
                 nc.sync.dma_start(out=tile[:].bitcast(I32), in_=source.bitcast(I32).rearrange("e s p b -> p (e s) b"))
@@ -116,13 +119,15 @@ def tile_moe_shr_glu_sigmoid_kernel(
                 words2[e] = tile[:, e - lo, :]
 
         gates = held.tile([P, SLOTS], F32, name="gates")
-        load_first(LEAD, E)
-        load_run(*runs[0])
+        load_first(LEAD, E, (0,))
+        load_run(1, *runs[0])
+        load_first(LEAD, E, (1,))
         load_first(E, E + 1)
         load_scales(scales2[:], w2_scales)
         load_second(LEAD, E + 1)
         nc.sync.dma_start(out=gates[:], in_=gate[:P, :])
-        load_run(*runs[1])
+        for m in range(2):
+            load_run(m, *runs[1])
         load_first(2, 3)
         load_first(1, 2)
         load_first(0, 1)

@@ -70,14 +70,17 @@ def tile_moe_shr_glu_sigmoid_kernel(
         ident = held.tile([P, P], F32, name="ident")
         make_identity(nc, ident[:])
 
-        routed = []
-        for c in range(CHUNKS):
-            window = held.tile([P, T], F32, name=f"routed{c}")
-            if c < CHUNKS // 2:
-                nc.scalar.copy(window[:], zero[:].to_broadcast([P, T]))
+        routed = {}
+
+        def clear_window(c, tag):
+            routed[c] = held.tile([P, T], F32, name=tag, align_bytes=64)
+            if c < 2:
+                nc.scalar.copy(routed[c][:], zero[:].to_broadcast([P, T]))
             else:
-                nc.gpsimd.memset(window[:], 0.0)
-            routed.append(window)
+                nc.vector.memset(routed[c][:], 0.0)
+
+        for c in range(1, CHUNKS):
+            clear_window(c, f"routed{c}")
 
         rows = xT.rearrange("(s p u b) w -> s u p b w", s=S, p=P, u=2, b=2)
         offsets = held.tile([P, SLOTS // 16], U16, name="offsets")
@@ -96,8 +99,6 @@ def tile_moe_shr_glu_sigmoid_kernel(
                     nc.sync.dma_start(out=raw[:], in_=rows[s, u])
                     for cols in HALVES:
                         raws[s, u, cols.start] = raw[:, :, cols]
-                if (s, u) == (0, 1):
-                    load_run(0, *runs[0])
 
         words13, words2 = {}, {}
 
@@ -119,6 +120,7 @@ def tile_moe_shr_glu_sigmoid_kernel(
                 words2[e] = tile[:, e - lo, :]
 
         gates = held.tile([P, SLOTS], F32, name="gates")
+        load_run(0, *runs[0])
         load_first(LEAD, E, (0,))
         load_run(1, *runs[0])
         load_first(LEAD, E, (1,))
@@ -154,26 +156,38 @@ def tile_moe_shr_glu_sigmoid_kernel(
             cols = slice(s * SLOTS + lo, s * SLOTS + lo + values.shape[1] // 4)
             nc.vector.quantize_mx(out=slot_codes[:, cols].bitcast(FP8X4), scales=slot_scales[:, cols], in_=values)
 
-        gathered = [held.tile([P, 4 * REST], BF16, name=f"gathered{s}", align_bytes=64) for s in range(S)]
+        gathered = [held.tile([P, 4 * n], BF16, name=f"gathered{n}", align_bytes=64) for n in (SLOTS, REST)]
 
-        def gather_rest(s, u):
-            gather(gathered[s][:, 2 * REST * u : 2 * REST * (u + 1)].bitcast(U32), s, u, 0, REST)
+        def gather_plain(s, u):
+            n = (SLOTS, REST)[s]
+            gather(gathered[s][:, 2 * n * u : 2 * n * (u + 1)].bitcast(U32), s, u, 0, n)
 
-        for s in range(S):
-            lead = held.tile([P, 4 * C], BF16, name=f"lead{s}", align_bytes=64)
-            for u in range(2):
-                cast(s, u)
-                gather(lead[:].bitcast(U32).rearrange("p (c u) -> p c u", u=2)[:, :, u], s, u, REST, SLOTS)
-                if s == 0:
-                    gather_rest(s, u)
-            quantise_slots(s, REST, lead[:])
-
-        def finish_slots(s, move, tag):
-            values = held.tile([P, 4 * REST], BF16, name=tag, align_bytes=64)
+        def interleave(move, s, lo, hi, tag):
+            values = held.tile([P, 4 * (hi - lo)], BF16, name=tag, align_bytes=64)
             move(
                 values[:].bitcast(F32).rearrange("p (c u) -> p c u", u=2),
-                gathered[s][:].bitcast(F32).rearrange("p (u c) -> p c u", u=2),
+                gathered[s][:].bitcast(F32).rearrange("p (u c) -> p c u", u=2)[:, lo:hi, :],
             )
+            return values
+
+        for u in range(2):
+            cast(0, u)
+            gather_plain(0, u)
+        clear_window(0, "raw00_0")
+        quantise_slots(0, REST, interleave(nc.vector.tensor_copy, 0, REST, SLOTS, "lead0")[:])
+        lead_pairs = held.tile([P, 4 * C], BF16, name="lead_pairs", align_bytes=64)
+        for u in range(2):
+            cast(1, u)
+            gather(lead_pairs[:, 2 * C * u : 2 * C * (u + 1)].bitcast(U32), 1, u, REST, SLOTS)
+        lead = held.tile([P, 4 * C], BF16, name="lead1", align_bytes=64)
+        nc.vector.tensor_copy(
+            lead[:].bitcast(F32).rearrange("p (c u) -> p c u", u=2),
+            lead_pairs[:].bitcast(F32).rearrange("p (u c) -> p c u", u=2),
+        )
+        quantise_slots(1, REST, lead[:])
+
+        def finish_slots(s, move, tag):
+            values = interleave(move, s, 0, REST, tag)
             quantise_slots(s, C, values[:, 4 * C :])
             quantise_slots(s, 0, values[:, : 4 * C])
 
@@ -204,7 +218,7 @@ def tile_moe_shr_glu_sigmoid_kernel(
         h_scales = held.tile([P, SLOTS + T], U8, name="h_scales", align_bytes=64)
         hs = {}
 
-        order = (3, E, E + 1, E + 2, E + 3, 2, 1, 0, E + 4, E + 5)
+        order = (3, E, E + 1, E + 2, E + 3, E + 4, 2, 1, 0, E + 5)
 
         borrowed = {0: gathered[1][:, REST - 128 : REST - 128 + 2 * H], 1: grouped_tokens[2][:, H : 3 * H]}
 
@@ -268,60 +282,69 @@ def tile_moe_shr_glu_sigmoid_kernel(
                 stop=True,
             )
 
-        def route(lo, hi, chunks, bank):
-            n = (hi - lo) * C
-            for j, c in enumerate(chunks):
+        def route(units, bank):
+            at = 0
+            for lo, hi, c in units:
                 for e in range(lo, hi):
-                    at = j * n + (e - lo) * C
                     second_layer(bank[:, at : at + C], e, c, e * C, (e + 1) * C)
-            y = held.tile([P, len(chunks) * n], F32, name=f"y{lo}{hi}{chunks[0]}")
-            nc.scalar.copy(y[:], bank[:, : len(chunks) * n])
-            weights = gates[:, lo * C : hi * C]
-            for j, c in enumerate(chunks):
+                    at += C
+            y = held.tile([P, at], F32, name="y%d%d%d" % units[0])
+            nc.scalar.copy(y[:], bank[:, :at])
+            at = 0
+            for lo, hi, c in units:
                 window = routed[c][:].indirect(offsets[:, lo * C // 16 : hi * C // 16])
-                nc.vector.tensor_tensor(window, y[:, j * n : (j + 1) * n], weights, MULT)
+                nc.vector.tensor_tensor(window, y[:, at : at + (hi - lo) * C], gates[:, lo * C : hi * C], MULT)
+                at += (hi - lo) * C
 
         shared = {}
 
-        def shared_out(c, cols):
-            if cols == LOW:
-                bank = (a_banks[2], x_banks[1], g_banks[2], x_banks[0])[c][:]
-            else:
-                width = HIGH.stop - HIGH.start
-                bank = (x_banks[1], a_banks[0])[c // 2][:, width * (c % 2) : width * (c % 2 + 1)]
+        def shared_out(c, cols, bank, keep):
             second_layer(bank, E, c, SLOTS + cols.start, SLOTS + cols.stop)
-            if c < ON_TENSOR and cols == LOW:
-                shared[c, cols.start] = held.tile([P, LOW.stop], F32, name=f"shared{c}")
+            if keep:
+                shared[c, cols.start] = held.tile([P, cols.stop - cols.start], F32, name=f"shared{c}_{cols.start}")
                 nc.scalar.copy(shared[c, cols.start][:], bank)
             else:
                 shared[c, cols.start] = bank
 
-        def finish(c, cols):
-            if c < ON_TENSOR and cols == LOW:
-                there, back = (g_banks[1], g_banks[0])[c], (a_banks[1], g_banks[1])[c]
-                for at in range(0, LOW.stop, P):
-                    block = slice(at, at + P)
-                    for first, part in ((True, shared[c, 0]), (False, routed[c])):
-                        nc.tensor.matmul(
-                            there[:, block], part[:, block], ident[:], start=first, stop=not first, is_transpose=True
-                        )
-                summed = work.tile([P, LOW.stop], F32, name="summed")
-                nc.scalar.copy(summed[:], there[:])
-                for at in range(0, LOW.stop, P):
-                    nc.tensor.transpose(back[:, at : at + P], summed[:, at : at + P], ident[:])
-                nc.scalar.copy(results[c][:, cols], back[:])
-                queue = nc.scalar
-            else:
-                nc.vector.tensor_tensor(results[c][:, cols], shared[c, cols.start], routed[c][:, cols], ADD)
-                queue = nc.sync
+        def shared_high(bank):
+            width = HIGH.stop - HIGH.start
+            both = held.tile([P, 2 * width], F32, name="shared_high")
+            for c in range(2):
+                second_layer(bank[:, c * width : (c + 1) * width], E, c, SLOTS + HIGH.start, SLOTS + HIGH.stop)
+                shared[c, HIGH.start] = both[:, c * width : (c + 1) * width]
+            nc.scalar.copy(both[:], bank[:])
+
+        def store(queue, c, cols):
             queue.dma_start(out=out[c * P : (c + 1) * P, cols], in_=results[c][:, cols])
+
+        def add_on_vector(c, cols):
+            nc.vector.tensor_tensor(results[c][:, cols], shared[c, cols.start], routed[c][:, cols], ADD)
+            store(nc.sync, c, cols)
+
+        def add_on_tensor(parts, there, back):
+            blocks = [(c, cols, at) for c, cols in parts for at in range(0, cols.stop - cols.start, P)]
+            for j, (c, cols, at) in enumerate(blocks):
+                pair = (shared[c, cols.start][:, at : at + P], routed[c][:, cols.start + at : cols.start + at + P])
+                for n, part in enumerate(pair):
+                    nc.tensor.matmul(
+                        there[:, j * P : (j + 1) * P], part, ident[:], start=n == 0, stop=n == 1, is_transpose=True
+                    )
+            summed = work.tile([P, 512], F32, name="summed")
+            nc.scalar.copy(summed[:], there[:])
+            for at in range(0, 512, P):
+                nc.tensor.transpose(back[:, at : at + P], summed[:, at : at + P], ident[:])
+            at = 0
+            for c, cols in parts:
+                nc.scalar.copy(results[c][:, cols], back[:, at : at + cols.stop - cols.start])
+                store(nc.scalar, c, cols)
+                at += cols.stop - cols.start
 
         first_layer(0)
         for u in range(2):
-            gather_rest(1, u)
+            gather_plain(1, u)
         first_layer(1)
         turn(0, x_banks[0])
-        route(3, 4, (0, 1), x_banks[1])
+        route(((3, 4, 0), (3, 4, 1)), x_banks[1])
         finish_slots(1, nc.vector.tensor_copy, "rest1")
         first_layer(2)
         turn(1, x_banks[0])
@@ -331,32 +354,31 @@ def tile_moe_shr_glu_sigmoid_kernel(
         first_layer(4)
         turn(3, x_banks[0])
         first_layer(5)
-        route(3, 4, (2, 3), a_banks[2])
-        turn(5, x_banks[0])
         first_layer(6)
-        turn(4, a_banks[2])
-        turn(6, x_banks[1])
-        route(2, 3, (0, 1), a_banks[0])
+        route(((3, 4, 2), (3, 4, 3)), a_banks[0])
         first_layer(7)
-        turn(7, x_banks[0])
-        route(1, 2, (0, 1), a_banks[1])
-        for c in range(ON_TENSOR):
-            shared_out(c, LOW)
+        turn(6, x_banks[0])
         first_layer(8)
+        turn(7, x_banks[1])
+        route(((2, 3, 0), (2, 3, 1)), a_banks[2])
+        turn(4, a_banks[0])
         first_layer(9)
-        route(0, 1, (0, 1), a_banks[2])
+        turn(5, a_banks[1])
         turn(8, x_banks[0])
-        turn(9, x_banks[1])
-        route(0, LEAD, (2,), a_banks[0])
-        for c in range(ON_TENSOR):
-            finish(c, LOW)
-        route(0, LEAD, (3,), a_banks[2])
-        for c in range(ON_TENSOR, CHUNKS):
-            shared_out(c, LOW)
-        for c in range(CHUNKS):
-            shared_out(c, HIGH)
-        for c in range(ON_TENSOR):
-            finish(c, HIGH)
-        for c in range(ON_TENSOR, CHUNKS):
-            for cols in (LOW, HIGH):
-                finish(c, cols)
+        route(((1, 2, 0), (1, 2, 1)), a_banks[1])
+        turn(9, a_banks[0])
+        route(((0, 1, 0), (0, 1, 1)), a_banks[2])
+        route(((0, 3, 2), (0, 1, 3)), a_banks[2])
+        shared_out(0, LOW, a_banks[1][:], True)
+        shared_out(1, LOW, a_banks[1][:], True)
+        shared_high(a_banks[2])
+        shared_out(2, LOW, g_banks[1][:], False)
+        shared_out(3, LOW, g_banks[0][:], False)
+        shared_out(3, HIGH, g_banks[2][:, :256], False)
+        add_on_tensor(((0, LOW),), x_banks[1], a_banks[0])
+        route(((1, 3, 3),), a_banks[1])
+        shared_out(2, HIGH, a_banks[1][:, :256], False)
+        add_on_tensor(((1, LOW),), x_banks[0], x_banks[1])
+        add_on_tensor(((0, HIGH), (1, HIGH)), a_banks[2], x_banks[0])
+        for c, cols in ((2, LOW), (2, HIGH), (3, LOW), (3, HIGH)):
+            add_on_vector(c, cols)

@@ -25,6 +25,7 @@ FP4X4 = mybir.dt.float4_e2m1fn_x4
 MULT = mybir.AluOpType.mult
 ADD = mybir.AluOpType.add
 SIGMOID = mybir.ActivationFunctionType.Sigmoid
+COPY = mybir.ActivationFunctionType.Copy
 
 
 def tile_moe_shr_glu_sigmoid_kernel(
@@ -134,6 +135,9 @@ def tile_moe_shr_glu_sigmoid_kernel(
         load_first(1, 2)
         load_first(0, 1)
         load_second(0, LEAD)
+        gate_columns = held.tile([P, LEAD], F32, name="gate_columns")
+        with nc.allow_non_contiguous_dma(reason="one gate value a partition and expert"):
+            nc.sync.dma_start(out=gate_columns[:], in_=gate[0, : LEAD * C].rearrange("(e p) -> p e", p=P))
 
         REST = LEAD * C
         slot_codes = held.tile([P, S * SLOTS], U32, name="slot_codes", align_bytes=64)
@@ -296,48 +300,43 @@ def tile_moe_shr_glu_sigmoid_kernel(
                 nc.vector.tensor_tensor(window, y[:, at : at + (hi - lo) * C], gates[:, lo * C : hi * C], MULT)
                 at += (hi - lo) * C
 
-        shared = {}
+        WIDE = 2 * P
+        weighted = held.tile([P, LEAD * WIDE], F32, name="weighted")
+
+        def weigh(e, acc):
+            nc.tensor.matmul_mx(
+                out=acc,
+                lhsT=h_codes[:, e * C : (e + 1) * C].bitcast(FP8X4),
+                lhsT_scale=h_scales[:, e * C : (e + 1) * C],
+                rhs=words2[e][:, 2 * WIDE :].bitcast(FP4X4),
+                rhs_scale=scales2[:, e * N + WIDE : (e + 1) * N],
+                start=True,
+                stop=True,
+            )
+            nc.scalar.activation(weighted[:, e * WIDE : (e + 1) * WIDE], acc, COPY, scale=gate_columns[:, e : e + 1])
+
+        def route_weighted(c, bank):
+            for e in range(LEAD):
+                at = e * WIDE + (c - 2) * P
+                nc.tensor.transpose(bank[:, e * C : (e + 1) * C], weighted[:, at : at + P], ident[:])
+            y = held.tile([P, REST], F32, name=f"y_late{c}")
+            nc.scalar.copy(y[:], bank[:, :REST])
+            nc.vector.tensor_copy(routed[c][:].indirect(offsets[:, : REST // 16]), y[:])
+
+        shared = [held.tile([P, T], F32, name=f"shared{c}") for c in range(CHUNKS - 1)]
 
         def shared_out(c, cols, bank, keep):
-            second_layer(bank, E, c, SLOTS + cols.start, SLOTS + cols.stop)
+            acc = bank[:, : cols.stop - cols.start]
+            second_layer(acc, E, c, SLOTS + cols.start, SLOTS + cols.stop)
             if keep:
-                shared[c, cols.start] = held.tile([P, cols.stop - cols.start], F32, name=f"shared{c}_{cols.start}")
-                nc.scalar.copy(shared[c, cols.start][:], bank)
+                nc.scalar.copy(shared[c][:, cols], acc)
             else:
-                shared[c, cols.start] = bank
+                nc.vector.tensor_tensor(results[c][:, cols], acc, routed[c][:, cols], ADD)
+                nc.sync.dma_start(out=out[c * P : (c + 1) * P, cols], in_=results[c][:, cols])
 
-        def shared_high(bank):
-            width = HIGH.stop - HIGH.start
-            both = held.tile([P, 2 * width], F32, name="shared_high")
-            for c in range(2):
-                second_layer(bank[:, c * width : (c + 1) * width], E, c, SLOTS + HIGH.start, SLOTS + HIGH.stop)
-                shared[c, HIGH.start] = both[:, c * width : (c + 1) * width]
-            nc.scalar.copy(both[:], bank[:])
-
-        def store(queue, c, cols):
-            queue.dma_start(out=out[c * P : (c + 1) * P, cols], in_=results[c][:, cols])
-
-        def add_on_vector(c, cols):
-            nc.vector.tensor_tensor(results[c][:, cols], shared[c, cols.start], routed[c][:, cols], ADD)
-            store(nc.sync, c, cols)
-
-        def add_on_tensor(parts, there, back):
-            blocks = [(c, cols, at) for c, cols in parts for at in range(0, cols.stop - cols.start, P)]
-            for j, (c, cols, at) in enumerate(blocks):
-                pair = (shared[c, cols.start][:, at : at + P], routed[c][:, cols.start + at : cols.start + at + P])
-                for n, part in enumerate(pair):
-                    nc.tensor.matmul(
-                        there[:, j * P : (j + 1) * P], part, ident[:], start=n == 0, stop=n == 1, is_transpose=True
-                    )
-            summed = work.tile([P, 512], F32, name="summed")
-            nc.scalar.copy(summed[:], there[:])
-            for at in range(0, 512, P):
-                nc.tensor.transpose(back[:, at : at + P], summed[:, at : at + P], ident[:])
-            at = 0
-            for c, cols in parts:
-                nc.scalar.copy(results[c][:, cols], back[:, at : at + cols.stop - cols.start])
-                store(nc.scalar, c, cols)
-                at += cols.stop - cols.start
+        def add_on_gpsimd(c, cols):
+            nc.gpsimd.tensor_tensor(results[c][:, cols], shared[c][:, cols], routed[c][:, cols], ADD)
+            nc.scalar.dma_start(out=out[c * P : (c + 1) * P, cols], in_=results[c][:, cols])
 
         first_layer(0)
         for u in range(2):
@@ -368,17 +367,17 @@ def tile_moe_shr_glu_sigmoid_kernel(
         route(((1, 2, 0), (1, 2, 1)), a_banks[1])
         turn(9, a_banks[0])
         route(((0, 1, 0), (0, 1, 1)), a_banks[2])
-        route(((0, 3, 2), (0, 1, 3)), a_banks[2])
-        shared_out(0, LOW, a_banks[1][:], True)
-        shared_out(1, LOW, a_banks[1][:], True)
-        shared_high(a_banks[2])
-        shared_out(2, LOW, g_banks[1][:], False)
-        shared_out(3, LOW, g_banks[0][:], False)
-        shared_out(3, HIGH, g_banks[2][:, :256], False)
-        add_on_tensor(((0, LOW),), x_banks[1], a_banks[0])
-        route(((1, 3, 3),), a_banks[1])
-        shared_out(2, HIGH, a_banks[1][:, :256], False)
-        add_on_tensor(((1, LOW),), x_banks[0], x_banks[1])
-        add_on_tensor(((0, HIGH), (1, HIGH)), a_banks[2], x_banks[0])
-        for c, cols in ((2, LOW), (2, HIGH), (3, LOW), (3, HIGH)):
-            add_on_vector(c, cols)
+        for e, bank in ((2, g_banks[1]), (1, x_banks[1]), (0, g_banks[0])):
+            weigh(e, bank[:, :WIDE])
+        route_weighted(2, a_banks[2])
+        shared_out(0, LOW, a_banks[1], True)
+        shared_out(0, HIGH, a_banks[2], True)
+        route_weighted(3, x_banks[0])
+        shared_out(1, LOW, a_banks[1], True)
+        shared_out(1, HIGH, a_banks[2], True)
+        shared_out(2, LOW, a_banks[1], True)
+        for c, cols in ((0, LOW), (1, LOW), (0, HIGH), (1, HIGH), (2, LOW)):
+            add_on_gpsimd(c, cols)
+        shared_out(2, HIGH, x_banks[0], False)
+        shared_out(3, LOW, g_banks[1], False)
+        shared_out(3, HIGH, a_banks[2], False)

@@ -7,11 +7,15 @@ K, T, E, C, H, N = 1024, 768, 4, 128, 512, 512
 P = 128
 S = K // 512
 SLOTS = E * C
-HALF = SLOTS // 2
 CHUNKS = N // P
 LOW, HIGH = slice(0, 512), slice(512, 768)
 LEAD = E - 1
-ON_TENSOR = 2
+LATE = LEAD * C
+BLOCK = 2 * P
+HALVES = (slice(0, T // 2), slice(T // 2, T))
+WEIGHED = 2
+RING = 3
+H_RING = 6
 FLOPS = 2 * (T + SLOTS) * (2 * K * H + H * N)
 
 F32 = mybir.dt.float32
@@ -34,23 +38,23 @@ def tile_moe_shr_glu_sigmoid_kernel(
     nc = tc.nc
     with ExitStack() as ctx:
         held = ctx.enter_context(tc.tile_pool(name="held", bufs=1))
-        work = ctx.enter_context(tc.tile_pool(name="work", bufs=3))
+        work = ctx.enter_context(tc.tile_pool(name="work", bufs=RING))
         psum = ctx.enter_context(tc.psum_pool(name="psum", bufs=1))
-        a_banks = [psum.tile([P, 512], F32, name=f"a{j}") for j in range(3)]
-        x_banks = [psum.tile([P, 512], F32, name=f"x{j}") for j in range(2)]
-        g_banks = [psum.tile([P, 512], F32, name=f"g{j}") for j in range(3)]
+        a_banks = [psum.tile([P, 512], F32, name=f"a{j}") for j in range(RING)]
+        spare_banks = [psum.tile([P, 512], F32, name=f"spare{j}") for j in range(2)]
+        g_banks = [psum.tile([P, 512], F32, name=f"g{j}") for j in range(RING)]
 
         zero = held.tile([P, 1], F32, name="zero")
         nc.vector.memset(zero[:], 0.0)
         warm = held.tile([P, 1], F32, name="warm")
         nc.scalar.activation(warm[:], zero[:], SIGMOID)
 
-        runs = ((LEAD, E + 1), (0, LEAD))
+        first_run, late_run = (LEAD, E + 1), (0, LEAD)
         scales13 = {}
-        for lo, hi in runs:
+        for lo, hi in (first_run, late_run):
             for m in range(2):
-                scales13[m, lo] = held.tile([P, (hi - lo) * S * H], U8, name=f"planes13_{m}{lo}", align_bytes=64)
-        scales2 = held.tile([P, (E + 1) * N], U8, name="planes2", align_bytes=64)
+                scales13[m, lo] = held.tile([P, (hi - lo) * S * H], U8, name=f"scales13_{m}{lo}", align_bytes=64)
+        scales2 = held.tile([P, (E + 1) * N], U8, name="scales2", align_bytes=64)
         for tile in (scales13[0, LEAD], scales13[1, LEAD], scales2, scales13[0, 0], scales13[1, 0]):
             nc.vector.memset(tile[:].bitcast(I32), 0)
 
@@ -60,7 +64,7 @@ def tile_moe_shr_glu_sigmoid_kernel(
             for r in range(4):
                 nc.sync.dma_start(out=view[r:P:32, :, :], in_=rows[r])
 
-        def load_run(m, lo, hi):
+        def load_scales13(m, lo, hi):
             load_scales(scales13[m, lo][:], (w1_scales, w3_scales)[m][lo:hi])
 
         def scale13(m, e, s):
@@ -71,49 +75,42 @@ def tile_moe_shr_glu_sigmoid_kernel(
         ident = held.tile([P, P], F32, name="ident")
         make_identity(nc, ident[:])
 
-        routed = {}
+        windows = {}
 
         def clear_window(c, tag):
-            routed[c] = held.tile([P, T], F32, name=tag, align_bytes=64)
-            if c < 2:
-                nc.scalar.copy(routed[c][:], zero[:].to_broadcast([P, T]))
+            windows[c] = held.tile([P, T], F32, name=tag, align_bytes=64)
+            if c < CHUNKS // 2:
+                nc.scalar.copy(windows[c][:], zero[:].to_broadcast([P, T]))
             else:
-                nc.vector.memset(routed[c][:], 0.0)
+                nc.vector.memset(windows[c][:], 0.0)
 
         for c in range(1, CHUNKS):
-            clear_window(c, f"routed{c}")
+            clear_window(c, f"window{c}")
 
         rows = xT.rearrange("(s p u b) w -> s u p b w", s=S, p=P, u=2, b=2)
         offsets = held.tile([P, SLOTS // 16], U16, name="offsets")
-        HALVES = (slice(0, T // 2), slice(T // 2, T))
         raws = {}
-        for s in range(S):
-            for u in range(2):
-                if s == 0 and u == 0:
-                    for cols in HALVES:
-                        raw = held.tile([P, 2, cols.stop - cols.start], F32, name=f"raw00_{cols.start}", align_bytes=64)
-                        nc.sync.dma_start(out=raw[:], in_=rows[s, u][:, :, cols])
-                        raws[s, u, cols.start] = raw[:]
-                    nc.sync.dma_start(offsets[:], offs)
-                else:
-                    raw = held.tile([P, 2, T], F32, name=f"raw{s}{u}", align_bytes=64)
-                    nc.sync.dma_start(out=raw[:], in_=rows[s, u])
-                    for cols in HALVES:
-                        raws[s, u, cols.start] = raw[:, :, cols]
+        for cols in HALVES:
+            raw = held.tile([P, 2, T // 2], F32, name=f"raw00_{cols.start}", align_bytes=64)
+            nc.sync.dma_start(out=raw[:], in_=rows[0, 0][:, :, cols])
+            raws[0, 0, cols.start] = raw[:]
+        nc.sync.dma_start(offsets[:], offs)
+        for s, u in ((0, 1), (1, 0), (1, 1)):
+            raw = held.tile([P, 2, T], F32, name=f"raw{s}{u}", align_bytes=64)
+            nc.sync.dma_start(out=raw[:], in_=rows[s, u])
+            for cols in HALVES:
+                raws[s, u, cols.start] = raw[:, :, cols]
 
         words13, words2 = {}, {}
 
-        def load_first(lo, hi, matrices=(0, 1)):
-            for m in matrices:
-                tile = held.tile([P, (hi - lo) * S, 2 * H], U8, name=f"w13_{m}{lo}", align_bytes=64)
-                source = (w1_words, w3_words)[m][lo:hi]
-                nc.sync.dma_start(out=tile[:].bitcast(I32), in_=source.bitcast(I32).rearrange("e s p b -> p (e s) b"))
-                for e in range(lo, hi):
-                    for s in range(S):
-                        words13[m, e, s] = tile[:, (e - lo) * S + s, :]
+        def load_words13(m, e):
+            tile = held.tile([P, S, 2 * H], U8, name=f"words13_{m}{e}", align_bytes=64)
+            source = (w1_words, w3_words)[m][e]
+            nc.sync.dma_start(out=tile[:].bitcast(I32), in_=source.bitcast(I32).rearrange("s p b -> p s b"))
+            words13[m, e] = tile
 
-        def load_second(lo, hi):
-            tile = held.tile([P, hi - lo, 2 * N], U8, name=f"w2_{lo}", align_bytes=64)
+        def load_words2(lo, hi):
+            tile = held.tile([P, hi - lo, 2 * N], U8, name=f"words2_{lo}", align_bytes=64)
             nc.sync.dma_start(
                 out=tile[:].bitcast(I32), in_=w2_words[lo:hi, 0].bitcast(I32).rearrange("e p b -> p e b")
             )
@@ -121,28 +118,27 @@ def tile_moe_shr_glu_sigmoid_kernel(
                 words2[e] = tile[:, e - lo, :]
 
         gates = held.tile([P, SLOTS], F32, name="gates")
-        load_run(0, *runs[0])
-        load_first(LEAD, E, (0,))
-        load_run(1, *runs[0])
-        load_first(LEAD, E, (1,))
-        load_first(E, E + 1)
+        for m in range(2):
+            load_scales13(m, *first_run)
+            load_words13(m, LEAD)
+        for m in range(2):
+            load_words13(m, E)
         load_scales(scales2[:], w2_scales)
-        load_second(LEAD, E + 1)
+        load_words2(*first_run)
         nc.sync.dma_start(out=gates[:], in_=gate[:P, :])
         for m in range(2):
-            load_run(m, *runs[1])
-        load_first(2, 3)
-        load_first(1, 2)
-        load_first(0, 1)
-        load_second(0, LEAD)
+            load_scales13(m, *late_run)
+        for e in reversed(range(LEAD)):
+            for m in range(2):
+                load_words13(m, e)
+        load_words2(*late_run)
         gate_columns = held.tile([P, LEAD], F32, name="gate_columns")
         with nc.allow_non_contiguous_dma(reason="one gate value a partition and expert"):
-            nc.sync.dma_start(out=gate_columns[:], in_=gate[0, : LEAD * C].rearrange("(e p) -> p e", p=P))
+            nc.sync.dma_start(out=gate_columns[:], in_=gate[0, :LATE].rearrange("(e p) -> p e", p=P))
 
-        REST = LEAD * C
         slot_codes = held.tile([P, S * SLOTS], U32, name="slot_codes", align_bytes=64)
         slot_scales = held.tile([P, S * SLOTS], U8, name="slot_scales", align_bytes=64)
-        pairs = held.tile([P, 8 * T], BF16, name="pairs", align_bytes=64)
+        pairs = held.tile([P, 2 * S * 2 * T], BF16, name="pairs", align_bytes=64)
 
         def plane(s, u):
             at = 2 * T * (2 * s + u)
@@ -154,77 +150,71 @@ def tile_moe_shr_glu_sigmoid_kernel(
                 move(paired[:, cols, :], raws[s, u, cols.start].rearrange("p b w -> p w b"))
 
         def gather(target, s, u, lo, hi):
-            nc.vector.tensor_copy(target, plane(s, u).bitcast(U32).indirect(offsets[:, lo // 16 : hi // 16]))
+            width = 2 * (hi - lo)
+            part = target[:, width * u : width * (u + 1)].bitcast(U32)
+            nc.vector.tensor_copy(part, plane(s, u).bitcast(U32).indirect(offsets[:, lo // 16 : hi // 16]))
+
+        def join_pairs(move, gathered, lo, hi, tag):
+            values = held.tile([P, 4 * (hi - lo)], BF16, name=tag, align_bytes=64)
+            move(
+                values[:].bitcast(F32).rearrange("p (c u) -> p c u", u=2),
+                gathered.bitcast(F32).rearrange("p (u c) -> p c u", u=2)[:, lo:hi, :],
+            )
+            return values
 
         def quantise_slots(s, lo, values):
             cols = slice(s * SLOTS + lo, s * SLOTS + lo + values.shape[1] // 4)
             nc.vector.quantize_mx(out=slot_codes[:, cols].bitcast(FP8X4), scales=slot_scales[:, cols], in_=values)
 
-        gathered = [held.tile([P, 4 * n], BF16, name=f"gathered{n}", align_bytes=64) for n in (SLOTS, REST)]
-
-        def gather_plain(s, u):
-            n = (SLOTS, REST)[s]
-            gather(gathered[s][:, 2 * n * u : 2 * n * (u + 1)].bitcast(U32), s, u, 0, n)
-
-        def interleave(move, s, lo, hi, tag):
-            values = held.tile([P, 4 * (hi - lo)], BF16, name=tag, align_bytes=64)
-            move(
-                values[:].bitcast(F32).rearrange("p (c u) -> p c u", u=2),
-                gathered[s][:].bitcast(F32).rearrange("p (u c) -> p c u", u=2)[:, lo:hi, :],
-            )
-            return values
-
-        for u in range(2):
-            cast(0, u)
-            gather_plain(0, u)
-        clear_window(0, "raw00_0")
-        quantise_slots(0, REST, interleave(nc.vector.tensor_copy, 0, REST, SLOTS, "lead0")[:])
-        lead_pairs = held.tile([P, 4 * C], BF16, name="lead_pairs", align_bytes=64)
-        for u in range(2):
-            cast(1, u)
-            gather(lead_pairs[:, 2 * C * u : 2 * C * (u + 1)].bitcast(U32), 1, u, REST, SLOTS)
-        lead = held.tile([P, 4 * C], BF16, name="lead1", align_bytes=64)
-        nc.vector.tensor_copy(
-            lead[:].bitcast(F32).rearrange("p (c u) -> p c u", u=2),
-            lead_pairs[:].bitcast(F32).rearrange("p (u c) -> p c u", u=2),
-        )
-        quantise_slots(1, REST, lead[:])
-
-        def finish_slots(s, move, tag):
-            values = interleave(move, s, 0, REST, tag)
+        def quantise_late_slots(s, gathered, tag):
+            values = join_pairs(nc.scalar.copy, gathered, 0, LATE, tag)
             quantise_slots(s, C, values[:, 4 * C :])
             quantise_slots(s, 0, values[:, : 4 * C])
 
-        BLOCK = 256
+        pair1_at = 2 * H
+        tokens_at = pair1_at + 2 * LATE
+        reused = held.tile([P, tokens_at + 4 * S * BLOCK], BF16, name="reused", align_bytes=64)
+        first_sigmoid = reused[:, :pair1_at].bitcast(F32)
+        first_h = reused[:, tokens_at - H // 2 : tokens_at + H // 2]
+        late_gathered = reused[:, pair1_at - 2 * LATE : tokens_at]
+
+        gathered0 = held.tile([P, 4 * SLOTS], BF16, name="gathered0", align_bytes=64)
+        for u in range(2):
+            cast(0, u)
+            gather(gathered0[:], 0, u, 0, SLOTS)
+        clear_window(0, "raw00_0")
+        quantise_slots(0, LATE, join_pairs(nc.vector.tensor_copy, gathered0[:], LATE, SLOTS, "lead0")[:])
+        lead_gathered = held.tile([P, 4 * C], BF16, name="lead_gathered", align_bytes=64)
+        for u in range(2):
+            cast(1, u)
+            gather(lead_gathered[:], 1, u, LATE, SLOTS)
+        quantise_slots(1, LATE, join_pairs(nc.vector.tensor_copy, lead_gathered[:], 0, C, "lead1")[:])
+
         token_codes = held.tile([P, S * T], U32, name="token_codes", align_bytes=64)
         token_scales = held.tile([P, S * T], U8, name="token_scales", align_bytes=64)
-        grouped_tokens = [
-            held.tile([P, 4 * S * BLOCK], BF16, name=f"tokens{b}", align_bytes=64)[:] for b in range(T // BLOCK)
-        ]
+        all_pairs = pairs[:].bitcast(F32).rearrange("p (s u w) -> p s w u", s=S, u=2)
+        last_block = T // BLOCK - 1
 
-        def quantise_tokens(b):
-            grouped = grouped_tokens[b]
-            for s in range(S):
-                both = pairs[:, 4 * T * s : 4 * T * (s + 1)].bitcast(F32).rearrange("p (u w) -> p w u", u=2)
-                nc.scalar.copy(
-                    grouped[:, 4 * BLOCK * s : 4 * BLOCK * (s + 1)].bitcast(F32).rearrange("p (w u) -> p w u", u=2),
-                    both[:, b * BLOCK : (b + 1) * BLOCK, :],
-                )
+        def quantise_tokens(b, values):
             cols = slice(S * BLOCK * b, S * BLOCK * (b + 1))
-            nc.vector.quantize_mx(out=token_codes[:, cols].bitcast(FP8X4), scales=token_scales[:, cols], in_=grouped)
+            nc.vector.quantize_mx(out=token_codes[:, cols].bitcast(FP8X4), scales=token_scales[:, cols], in_=values)
 
-        quantise_tokens(0)
-        quantise_tokens(1)
-        finish_slots(0, nc.scalar.copy, "raw11")
+        def by_word(values):
+            return values.bitcast(F32).rearrange("p (s w u) -> p s w u", s=S, u=2)
+
+        early_blocks = [held.tile([P, 4 * S * BLOCK], BF16, name=f"tokens{b}", align_bytes=64) for b in range(last_block)]
+        for b, values in enumerate(early_blocks):
+            for s in range(S):
+                nc.scalar.copy(by_word(values[:])[:, s, :, :], all_pairs[:, s, b * BLOCK : (b + 1) * BLOCK, :])
+            quantise_tokens(b, values[:])
+        quantise_late_slots(0, gathered0[:], "raw11")
 
         results = [held.tile([P, T], F32, name=f"result{c}") for c in range(CHUNKS)]
         h_codes = held.tile([P, SLOTS + T], U32, name="h_codes", align_bytes=64)
         h_scales = held.tile([P, SLOTS + T], U8, name="h_scales", align_bytes=64)
+        h_values = held.tile([P, 4 * (SLOTS + T)], BF16, name="h_values", align_bytes=64)
         hs = {}
-
-        order = (3, E, E + 1, E + 2, E + 3, E + 4, 2, 1, 0, E + 5)
-
-        borrowed = {0: gathered[1][:, REST - 128 : REST - 128 + 2 * H], 1: grouped_tokens[2][:, H : 3 * H]}
+        order = (LEAD, *range(E, E + 5), *reversed(range(LEAD)), E + 5)
 
         def first_layer(step):
             i = order[step]
@@ -234,7 +224,7 @@ def tile_moe_shr_glu_sigmoid_kernel(
             else:
                 e, codes, scales = E, token_codes, token_scales
                 starts = [((i - E) // 2 * S + s) * BLOCK + (i - E) % 2 * P for s in range(S)]
-            a, g = a_banks[step % 3], g_banks[(0, 1, 0, 2, 1, 0, 2, 1, 0, 2)[step]]
+            a, g = a_banks[step % RING], g_banks[step % RING]
             for s in range(S):
                 cols = slice(starts[s], starts[s] + P)
                 for m, acc in enumerate((a, g)):
@@ -242,38 +232,46 @@ def tile_moe_shr_glu_sigmoid_kernel(
                         out=acc[:],
                         lhsT=codes[:, cols].bitcast(FP8X4),
                         lhsT_scale=scales[:, cols],
-                        rhs=words13[m, e, s].bitcast(FP4X4),
+                        rhs=words13[m, e][:, s, :].bitcast(FP4X4),
                         rhs_scale=scale13(m, e, s),
                         start=(s == 0),
                         stop=(s == S - 1),
                     )
-            natural, by_pair = "t (p u b) -> t u p b", "t (u p b) -> t u p b"
-            if step in borrowed:
-                sig = borrowed[step].bitcast(F32)
+            if step == 0:
+                sig, h = first_sigmoid, first_h
             else:
-                sig = work.tile([P, H], F32, name="sig")
-            nc.scalar.activation(sig[:].rearrange(by_pair, u=2, b=2), a[:].rearrange(natural, u=2, b=2), SIGMOID)
-            h = work.tile([P, H], BF16, name="h", align_bytes=64)
+                sig = work.tile([P, H], F32, name="sig")[:]
+                h = work.tile([P, H], BF16, name="h", align_bytes=64, bufs=H_RING)[:]
+            natural, by_pair = "t (p u b) -> t u p b", "t (u p b) -> t u p b"
+            nc.scalar.activation(sig.rearrange(by_pair, u=2, b=2), a[:].rearrange(natural, u=2, b=2), SIGMOID)
             nc.vector.tensor_tensor(
-                h[:].rearrange(by_pair, u=2, b=2),
-                sig[:].rearrange(by_pair, u=2, b=2),
+                h.rearrange(by_pair, u=2, b=2),
+                sig.rearrange(by_pair, u=2, b=2),
                 g[:].rearrange(natural, u=2, b=2),
                 MULT,
             )
             hs[i] = h
 
-        def turn(step, bank):
-            i = order[step]
-            turned = bank[:, : 2 * P].rearrange("p (u c) -> p u c", u=2)
-            words = hs[i][:].bitcast(F32)
-            for u in range(2):
-                nc.tensor.transpose(turned[:, u, :], words[:, u * P : (u + 1) * P], ident[:])
-            grouped = work.tile([P, 4 * P], BF16, name="h_grouped", align_bytes=64)
+        def turn(i, count, bank):
+            turned = bank[:, : count * 2 * P].rearrange("p (j u c) -> p j u c", j=count, u=2)
+            for j in range(count):
+                words = hs[i + j].bitcast(F32)
+                for u in range(2):
+                    nc.tensor.transpose(turned[:, j, u, :], words[:, u * P : (u + 1) * P], ident[:])
+            values = h_values[:, 4 * P * i : 4 * P * (i + count)]
             nc.scalar.copy(
-                grouped[:].bitcast(F32).rearrange("p (c u) -> p c u", u=2), turned.rearrange("p u c -> p c u")
+                values.bitcast(F32).rearrange("p (j c u) -> p j c u", j=count, u=2),
+                turned.rearrange("p j u c -> p j c u"),
             )
-            cols = slice(P * i, P * (i + 1))
-            nc.vector.quantize_mx(out=h_codes[:, cols].bitcast(FP8X4), scales=h_scales[:, cols], in_=grouped[:])
+
+        def quantise_h(lo, hi):
+            nc.vector.quantize_mx(
+                out=h_codes[:, lo:hi].bitcast(FP8X4), scales=h_scales[:, lo:hi], in_=h_values[:, 4 * lo : 4 * hi]
+            )
+
+        def turn_expert(e, bank):
+            turn(e, 1, bank)
+            quantise_h(e * C, (e + 1) * C)
 
         def second_layer(acc, e, c, lo, hi):
             nc.tensor.matmul_mx(
@@ -286,98 +284,104 @@ def tile_moe_shr_glu_sigmoid_kernel(
                 stop=True,
             )
 
-        def route(units, bank):
-            at = 0
-            for lo, hi, c in units:
-                for e in range(lo, hi):
-                    second_layer(bank[:, at : at + C], e, c, e * C, (e + 1) * C)
-                    at += C
-            y = held.tile([P, at], F32, name="y%d%d%d" % units[0])
-            nc.scalar.copy(y[:], bank[:, :at])
-            at = 0
-            for lo, hi, c in units:
-                window = routed[c][:].indirect(offsets[:, lo * C // 16 : hi * C // 16])
-                nc.vector.tensor_tensor(window, y[:, at : at + (hi - lo) * C], gates[:, lo * C : hi * C], MULT)
-                at += (hi - lo) * C
+        def route(e, first, bank):
+            for j in range(2):
+                second_layer(bank[:, j * C : (j + 1) * C], e, first + j, e * C, (e + 1) * C)
+            y = held.tile([P, 2 * C], F32, name=f"y{e}{first}")
+            nc.scalar.copy(y[:], bank[:, : 2 * C])
+            for j in range(2):
+                window = windows[first + j][:].indirect(offsets[:, e * C // 16 : (e + 1) * C // 16])
+                nc.vector.tensor_tensor(window, y[:, j * C : (j + 1) * C], gates[:, e * C : (e + 1) * C], MULT)
 
-        WIDE = 2 * P
-        weighted = held.tile([P, LEAD * WIDE], F32, name="weighted")
+        wide = N - WEIGHED * P
+        weighed = held.tile([P, LEAD * wide], F32, name="weighed")
 
-        def weigh(e, acc):
+        def weigh(e, bank):
             nc.tensor.matmul_mx(
-                out=acc,
+                out=bank[:, :wide],
                 lhsT=h_codes[:, e * C : (e + 1) * C].bitcast(FP8X4),
                 lhsT_scale=h_scales[:, e * C : (e + 1) * C],
-                rhs=words2[e][:, 2 * WIDE :].bitcast(FP4X4),
-                rhs_scale=scales2[:, e * N + WIDE : (e + 1) * N],
+                rhs=words2[e][:, 2 * WEIGHED * P :].bitcast(FP4X4),
+                rhs_scale=scales2[:, e * N + WEIGHED * P : (e + 1) * N],
                 start=True,
                 stop=True,
             )
-            nc.scalar.activation(weighted[:, e * WIDE : (e + 1) * WIDE], acc, COPY, scale=gate_columns[:, e : e + 1])
+            nc.scalar.activation(
+                weighed[:, e * wide : (e + 1) * wide], bank[:, :wide], COPY, scale=gate_columns[:, e : e + 1]
+            )
 
-        def route_weighted(c, bank):
+        def route_weighed(c, bank):
             for e in range(LEAD):
-                at = e * WIDE + (c - 2) * P
-                nc.tensor.transpose(bank[:, e * C : (e + 1) * C], weighted[:, at : at + P], ident[:])
-            y = held.tile([P, REST], F32, name=f"y_late{c}")
-            nc.scalar.copy(y[:], bank[:, :REST])
-            nc.vector.tensor_copy(routed[c][:].indirect(offsets[:, : REST // 16]), y[:])
+                at = e * wide + (c - WEIGHED) * P
+                nc.tensor.transpose(bank[:, e * C : (e + 1) * C], weighed[:, at : at + P], ident[:])
+            y = held.tile([P, LATE], F32, name=f"y_late{c}")
+            nc.scalar.copy(y[:], bank[:, :LATE])
+            nc.vector.tensor_copy(windows[c][:].indirect(offsets[:, : LATE // 16]), y[:])
+
+        def shared_result(c, cols, bank):
+            acc = bank[:, : cols.stop - cols.start]
+            second_layer(acc, E, c, SLOTS + cols.start, SLOTS + cols.stop)
+            return acc
 
         shared = [held.tile([P, T], F32, name=f"shared{c}") for c in range(CHUNKS - 1)]
 
-        def shared_out(c, cols, bank, keep):
-            acc = bank[:, : cols.stop - cols.start]
-            second_layer(acc, E, c, SLOTS + cols.start, SLOTS + cols.stop)
-            if keep:
-                nc.scalar.copy(shared[c][:, cols], acc)
-            else:
-                nc.vector.tensor_tensor(results[c][:, cols], acc, routed[c][:, cols], ADD)
-                nc.sync.dma_start(out=out[c * P : (c + 1) * P, cols], in_=results[c][:, cols])
+        def keep_shared(c, cols, bank):
+            nc.scalar.copy(shared[c][:, cols], shared_result(c, cols, bank))
 
         def add_on_gpsimd(c, cols):
-            nc.gpsimd.tensor_tensor(results[c][:, cols], shared[c][:, cols], routed[c][:, cols], ADD)
+            nc.gpsimd.tensor_tensor(results[c][:, cols], shared[c][:, cols], windows[c][:, cols], ADD)
             nc.scalar.dma_start(out=out[c * P : (c + 1) * P, cols], in_=results[c][:, cols])
 
+        def add_on_vector(c, cols, bank):
+            nc.vector.tensor_tensor(results[c][:, cols], shared_result(c, cols, bank), windows[c][:, cols], ADD)
+            nc.sync.dma_start(out=out[c * P : (c + 1) * P, cols], in_=results[c][:, cols])
+
         first_layer(0)
-        for u in range(2):
-            gather_plain(1, u)
+        gather(late_gathered, 1, 0, 0, LATE)
         first_layer(1)
-        turn(0, x_banks[0])
-        route(((3, 4, 0), (3, 4, 1)), x_banks[1])
-        finish_slots(1, nc.vector.tensor_copy, "rest1")
+        turn_expert(LEAD, spare_banks[0])
+        gather(late_gathered, 1, 1, 0, LATE)
+        route(LEAD, 0, spare_banks[1])
         first_layer(2)
-        turn(1, x_banks[0])
-        quantise_tokens(2)
+        last_tokens = reused[:, tokens_at:]
+        nc.scalar.copy(by_word(last_tokens), all_pairs[:, :, last_block * BLOCK :, :])
+        quantise_tokens(last_block, last_tokens)
         first_layer(3)
-        turn(2, x_banks[0])
+        quantise_late_slots(1, late_gathered, "late_values")
         first_layer(4)
-        turn(3, x_banks[0])
+        turn(E, 2, spare_banks[1])
+        turn(E + 2, 1, spare_banks[0])
         first_layer(5)
+
         first_layer(6)
-        route(((3, 4, 2), (3, 4, 3)), a_banks[0])
+        route(LEAD, 2, a_banks[6 % RING])
         first_layer(7)
-        turn(6, x_banks[0])
+        turn_expert(2, spare_banks[0])
         first_layer(8)
-        turn(7, x_banks[1])
-        route(((2, 3, 0), (2, 3, 1)), a_banks[2])
-        turn(4, a_banks[0])
+        turn_expert(1, spare_banks[1])
+        route(2, 0, a_banks[8 % RING])
+        turn(E + 3, 1, a_banks[6 % RING])
+        quantise_h(SLOTS + LOW.start, SLOTS + LOW.stop)
         first_layer(9)
-        turn(5, a_banks[1])
-        turn(8, x_banks[0])
-        route(((1, 2, 0), (1, 2, 1)), a_banks[1])
-        turn(9, a_banks[0])
-        route(((0, 1, 0), (0, 1, 1)), a_banks[2])
-        for e, bank in ((2, g_banks[1]), (1, x_banks[1]), (0, g_banks[0])):
-            weigh(e, bank[:, :WIDE])
-        route_weighted(2, a_banks[2])
-        shared_out(0, LOW, a_banks[1], True)
-        shared_out(0, HIGH, a_banks[2], True)
-        route_weighted(3, x_banks[0])
-        shared_out(1, LOW, a_banks[1], True)
-        shared_out(1, HIGH, a_banks[2], True)
-        shared_out(2, LOW, a_banks[1], True)
+        turn(E + 4, 1, a_banks[7 % RING])
+        turn_expert(0, spare_banks[0])
+        route(1, 0, a_banks[7 % RING])
+        turn(E + 5, 1, a_banks[9 % RING])
+        quantise_h(SLOTS + HIGH.start, SLOTS + HIGH.stop)
+        route(0, 0, a_banks[8 % RING])
+
+        for e, bank in ((2, g_banks[7 % RING]), (1, spare_banks[1]), (0, g_banks[8 % RING])):
+            weigh(e, bank)
+        low_bank, high_bank = a_banks[7 % RING], a_banks[8 % RING]
+        route_weighed(2, high_bank)
+        keep_shared(0, LOW, low_bank)
+        keep_shared(0, HIGH, high_bank)
+        route_weighed(3, spare_banks[0])
+        keep_shared(1, LOW, low_bank)
+        keep_shared(1, HIGH, high_bank)
+        keep_shared(2, LOW, low_bank)
         for c, cols in ((0, LOW), (1, LOW), (0, HIGH), (1, HIGH), (2, LOW)):
             add_on_gpsimd(c, cols)
-        shared_out(2, HIGH, x_banks[0], False)
-        shared_out(3, LOW, g_banks[1], False)
-        shared_out(3, HIGH, a_banks[2], False)
+        add_on_vector(2, HIGH, spare_banks[0])
+        add_on_vector(3, LOW, g_banks[7 % RING])
+        add_on_vector(3, HIGH, high_bank)

@@ -82,10 +82,9 @@ def tile_moe_shr_glu_sigmoid_kernel(
             if c < CHUNKS // 2:
                 nc.scalar.copy(windows[c][:], zero[:].to_broadcast([P, T]))
             else:
-                nc.vector.memset(windows[c][:], 0.0)
+                nc.gpsimd.memset(windows[c][:], 0.0)
 
-        for c in range(1, CHUNKS):
-            clear_window(c, f"window{c}")
+        clear_window(1, "window1")
 
         rows = xT.rearrange("(s p u b) w -> s u p b w", s=S, p=P, u=2, b=2)
         offsets = held.tile([P, SLOTS // 16], U16, name="offsets")
@@ -183,6 +182,8 @@ def tile_moe_shr_glu_sigmoid_kernel(
             cast(0, u)
             gather(gathered0[:], 0, u, 0, SLOTS)
         clear_window(0, "raw00_0")
+        clear_window(2, f"raw00_{T // 2}")
+        clear_window(3, "raw01")
         quantise_slots(0, LATE, join_pairs(nc.vector.tensor_copy, gathered0[:], LATE, SLOTS, "lead0")[:])
         lead_gathered = held.tile([P, 4 * C], BF16, name="lead_gathered", align_bytes=64)
         for u in range(2):

@@ -15,7 +15,7 @@ BLOCK = 2 * P
 HALVES = (slice(0, T // 2), slice(T // 2, T))
 WEIGHED = 2
 RING = 3
-H_RING = 6
+H_RING = 9
 FLOPS = 2 * (T + SLOTS) * (2 * K * H + H * N)
 
 F32 = mybir.dt.float32
@@ -40,9 +40,7 @@ def tile_moe_shr_glu_sigmoid_kernel(
         held = ctx.enter_context(tc.tile_pool(name="held", bufs=1))
         work = ctx.enter_context(tc.tile_pool(name="work", bufs=RING))
         psum = ctx.enter_context(tc.psum_pool(name="psum", bufs=1))
-        a_banks = [psum.tile([P, 512], F32, name=f"a{j}") for j in range(RING)]
-        spare_banks = [psum.tile([P, 512], F32, name=f"spare{j}") for j in range(2)]
-        g_banks = [psum.tile([P, 512], F32, name=f"g{j}") for j in range(RING)]
+        a0, a1, a2, s0, s1, g0, g1, g2 = [psum.tile([P, 512], F32, name=f"bank{j}") for j in range(8)]
 
         zero = held.tile([P, 1], F32, name="zero")
         nc.vector.memset(zero[:], 0.0)
@@ -116,21 +114,22 @@ def tile_moe_shr_glu_sigmoid_kernel(
             for e in range(lo, hi):
                 words2[e] = tile[:, e - lo, :]
 
-        gates = held.tile([P, SLOTS], F32, name="gates")
+        gates = {0: held.tile([P, LATE], F32, name="late_gates"), LEAD: held.tile([P, C], F32, name="lead_gates")}
         for m in range(2):
             load_scales13(m, *first_run)
             load_words13(m, LEAD)
         for m in range(2):
             load_words13(m, E)
         load_scales(scales2[:], w2_scales)
-        load_words2(*first_run)
-        nc.sync.dma_start(out=gates[:], in_=gate[:P, :])
+        load_words2(LEAD, E + 1)
+        nc.sync.dma_start(out=gates[LEAD][:], in_=gate[:P, LATE:])
         for m in range(2):
             load_scales13(m, *late_run)
         for e in reversed(range(LEAD)):
             for m in range(2):
                 load_words13(m, e)
         load_words2(*late_run)
+        nc.sync.dma_start(out=gates[0][:], in_=gate[:P, :LATE])
         gate_columns = held.tile([P, LEAD], F32, name="gate_columns")
         with nc.allow_non_contiguous_dma(reason="one gate value a partition and expert"):
             nc.sync.dma_start(out=gate_columns[:], in_=gate[0, :LATE].rearrange("(e p) -> p e", p=P))
@@ -165,17 +164,15 @@ def tile_moe_shr_glu_sigmoid_kernel(
             cols = slice(s * SLOTS + lo, s * SLOTS + lo + values.shape[1] // 4)
             nc.vector.quantize_mx(out=slot_codes[:, cols].bitcast(FP8X4), scales=slot_scales[:, cols], in_=values)
 
-        def quantise_late_slots(s, gathered, tag):
-            values = join_pairs(nc.scalar.copy, gathered, 0, LATE, tag)
+        def quantise_late_slots(s, gathered, tag, move=nc.scalar.copy):
+            values = join_pairs(move, gathered, 0, LATE, tag)
             quantise_slots(s, C, values[:, 4 * C :])
             quantise_slots(s, 0, values[:, : 4 * C])
 
-        pair1_at = 2 * H
-        tokens_at = pair1_at + 2 * LATE
-        reused = held.tile([P, tokens_at + 4 * S * BLOCK], BF16, name="reused", align_bytes=64)
-        first_sigmoid = reused[:, :pair1_at].bitcast(F32)
-        first_h = reused[:, tokens_at - H // 2 : tokens_at + H // 2]
-        late_gathered = reused[:, pair1_at - 2 * LATE : tokens_at]
+        block_values = 4 * S * BLOCK
+        reused = held.tile([P, block_values + 2 * H], BF16, name="reused", align_bytes=64)
+        first_sigmoid = reused[:, block_values:].bitcast(F32)
+        late_gathered = reused[:, block_values - 2 * LATE : block_values + 2 * LATE]
 
         gathered0 = held.tile([P, 4 * SLOTS], BF16, name="gathered0", align_bytes=64)
         for u in range(2):
@@ -203,7 +200,7 @@ def tile_moe_shr_glu_sigmoid_kernel(
         def by_word(values):
             return values.bitcast(F32).rearrange("p (s w u) -> p s w u", s=S, u=2)
 
-        early_blocks = [held.tile([P, 4 * S * BLOCK], BF16, name=f"tokens{b}", align_bytes=64) for b in range(last_block)]
+        early_blocks = [held.tile([P, block_values], BF16, name="tokens0", align_bytes=64), reused[:, :block_values]]
         for b, values in enumerate(early_blocks):
             for s in range(S):
                 nc.scalar.copy(by_word(values[:])[:, s, :, :], all_pairs[:, s, b * BLOCK : (b + 1) * BLOCK, :])
@@ -215,20 +212,17 @@ def tile_moe_shr_glu_sigmoid_kernel(
         h_scales = held.tile([P, SLOTS + T], U8, name="h_scales", align_bytes=64)
         h_values = held.tile([P, 4 * (SLOTS + T)], BF16, name="h_values", align_bytes=64)
         hs = {}
-        order = (LEAD, *range(E, E + 5), *reversed(range(LEAD)), E + 5)
 
-        def first_layer(step):
-            i = order[step]
+        def first_layer(i, a, g):
             if i < E:
                 e, codes, scales = i, slot_codes, slot_scales
                 starts = [s * SLOTS + i * C for s in range(S)]
             else:
                 e, codes, scales = E, token_codes, token_scales
                 starts = [((i - E) // 2 * S + s) * BLOCK + (i - E) % 2 * P for s in range(S)]
-            a, g = a_banks[step % RING], g_banks[step % RING]
-            for s in range(S):
-                cols = slice(starts[s], starts[s] + P)
-                for m, acc in enumerate((a, g)):
+            for m, acc in enumerate((a, g)):
+                for s in range(S):
+                    cols = slice(starts[s], starts[s] + P)
                     nc.tensor.matmul_mx(
                         out=acc[:],
                         lhsT=codes[:, cols].bitcast(FP8X4),
@@ -238,11 +232,8 @@ def tile_moe_shr_glu_sigmoid_kernel(
                         start=(s == 0),
                         stop=(s == S - 1),
                     )
-            if step == 0:
-                sig, h = first_sigmoid, first_h
-            else:
-                sig = work.tile([P, H], F32, name="sig")[:]
-                h = work.tile([P, H], BF16, name="h", align_bytes=64, bufs=H_RING)[:]
+            sig = first_sigmoid if i == LEAD else work.tile([P, H], F32, name="sig")[:]
+            h = work.tile([P, H], BF16, name="h", align_bytes=64, bufs=H_RING)[:]
             natural, by_pair = "t (p u b) -> t u p b", "t (u p b) -> t u p b"
             nc.scalar.activation(sig.rearrange(by_pair, u=2, b=2), a[:].rearrange(natural, u=2, b=2), SIGMOID)
             nc.vector.tensor_tensor(
@@ -285,14 +276,27 @@ def tile_moe_shr_glu_sigmoid_kernel(
                 stop=True,
             )
 
-        def route(e, first, bank):
-            for j in range(2):
-                second_layer(bank[:, j * C : (j + 1) * C], e, first + j, e * C, (e + 1) * C)
-            y = held.tile([P, 2 * C], F32, name=f"y{e}{first}")
-            nc.scalar.copy(y[:], bank[:, : 2 * C])
-            for j in range(2):
-                window = windows[first + j][:].indirect(offsets[:, e * C // 16 : (e + 1) * C // 16])
-                nc.vector.tensor_tensor(window, y[:, j * C : (j + 1) * C], gates[:, e * C : (e + 1) * C], MULT)
+        def gate_of(e):
+            return gates[LEAD][:] if e == LEAD else gates[0][:, e * C : (e + 1) * C]
+
+        def routed(e, chunks, bank):
+            for j, c in enumerate(chunks):
+                second_layer(bank[:, j * C : (j + 1) * C], e, c, e * C, (e + 1) * C)
+
+        def scatter(e, chunks, acc, y):
+            nc.scalar.copy(y, acc)
+            for j, c in enumerate(chunks):
+                window = windows[c][:].indirect(offsets[:, e * C // 16 : (e + 1) * C // 16])
+                nc.vector.tensor_tensor(window, y[:, j * C : (j + 1) * C], gate_of(e), MULT)
+
+        def y_tile(tag, count):
+            return held.tile([P, count * C], F32, name=tag, align_bytes=64)[:]
+
+        def route(e, first, bank, count=2, y=None):
+            chunks = range(first, first + count)
+            routed(e, chunks, bank)
+            y = y_tile(f"y{e}{first}", count) if y is None else y[:, : count * C]
+            scatter(e, chunks, bank[:, : count * C], y)
 
         wide = N - WEIGHED * P
         weighed = held.tile([P, LEAD * wide], F32, name="weighed")
@@ -333,56 +337,57 @@ def tile_moe_shr_glu_sigmoid_kernel(
             nc.gpsimd.tensor_tensor(results[c][:, cols], shared[c][:, cols], windows[c][:, cols], ADD)
             nc.scalar.dma_start(out=out[c * P : (c + 1) * P, cols], in_=results[c][:, cols])
 
-        def add_on_vector(c, cols, bank):
-            nc.vector.tensor_tensor(results[c][:, cols], shared_result(c, cols, bank), windows[c][:, cols], ADD)
+        def add_on_vector(c, cols, acc):
+            nc.vector.tensor_tensor(results[c][:, cols], acc, windows[c][:, cols], ADD)
             nc.sync.dma_start(out=out[c * P : (c + 1) * P, cols], in_=results[c][:, cols])
 
-        first_layer(0)
         gather(late_gathered, 1, 0, 0, LATE)
-        first_layer(1)
-        turn_expert(LEAD, spare_banks[0])
+        first_layer(LEAD, a0, g0)
+        first_layer(E, a1, g1)
+        turn_expert(LEAD, s0)
         gather(late_gathered, 1, 1, 0, LATE)
-        route(LEAD, 0, spare_banks[1])
-        first_layer(2)
-        last_tokens = reused[:, tokens_at:]
+        last_tokens = held.tile([P, block_values], BF16, name="words13_13", align_bytes=64)[:]
         nc.scalar.copy(by_word(last_tokens), all_pairs[:, :, last_block * BLOCK :, :])
         quantise_tokens(last_block, last_tokens)
-        first_layer(3)
+        first_layer(E + 1, a2, g2)
+        routed(LEAD, (0, 1, 3), s1)
+        scatter(LEAD, (0,), s1[:, :C], y_tile("y30", 1))
+        first_layer(E + 2, a0, g0)
         quantise_late_slots(1, late_gathered, "late_values")
-        first_layer(4)
-        turn(E, 2, spare_banks[1])
-        turn(E + 2, 1, spare_banks[0])
-        first_layer(5)
-
-        first_layer(6)
-        route(LEAD, 2, a_banks[6 % RING])
-        first_layer(7)
-        turn_expert(2, spare_banks[0])
-        first_layer(8)
-        turn_expert(1, spare_banks[1])
-        route(2, 0, a_banks[8 % RING])
-        turn(E + 3, 1, a_banks[6 % RING])
+        first_layer(E + 3, a1, g1)
+        first_layer(2, a2, g2)
+        scatter(LEAD, (1,), s1[:, C : 2 * C], y_tile("words13_12", 1))
+        routed(LEAD, (2,), a2)
+        first_layer(1, a0, g0)
+        turn_expert(2, s0)
+        scatter(LEAD, (2,), a2[:, :C], hs[2].bitcast(F32)[:, :C])
+        first_layer(0, a1, g1)
+        turn_expert(1, s0)
+        scatter(LEAD, (3,), s1[:, 2 * C : 3 * C], hs[1].bitcast(F32)[:, :C])
+        routed(2, (0, 1), a1)
+        scatter(2, (0,), a1[:, :C], y_tile("y20", 1))
+        first_layer(E + 4, a2, g2)
+        turn_expert(0, s0)
+        scatter(2, (1,), a1[:, C : 2 * C], hs[0].bitcast(F32)[:, :C])
+        turn(E, 2, g1)
+        first_layer(E + 5, a0, g0)
+        turn(E + 2, 2, a0)
         quantise_h(SLOTS + LOW.start, SLOTS + LOW.stop)
-        first_layer(9)
-        turn(E + 4, 1, a_banks[7 % RING])
-        turn_expert(0, spare_banks[0])
-        route(1, 0, a_banks[7 % RING])
-        turn(E + 5, 1, a_banks[9 % RING])
+        route(1, 0, s1, 2, hs[E + 3].bitcast(F32))
+        turn(E + 4, 2, a2)
         quantise_h(SLOTS + HIGH.start, SLOTS + HIGH.stop)
-        route(0, 0, a_banks[8 % RING])
-
-        for e, bank in ((2, g_banks[7 % RING]), (1, spare_banks[1]), (0, g_banks[8 % RING])):
+        route(0, 0, a1, 2, hs[E + 5].bitcast(F32))
+        for e, bank in ((2, g1), (1, s0), (0, g2)):
             weigh(e, bank)
-        low_bank, high_bank = a_banks[7 % RING], a_banks[8 % RING]
-        route_weighed(2, high_bank)
-        keep_shared(0, LOW, low_bank)
-        keep_shared(0, HIGH, high_bank)
-        route_weighed(3, spare_banks[0])
-        keep_shared(1, LOW, low_bank)
-        keep_shared(1, HIGH, high_bank)
-        keep_shared(2, LOW, low_bank)
+        route_weighed(2, a1)
+        route_weighed(3, a2)
+        keep_shared(0, LOW, s1)
+        keep_shared(1, LOW, a0)
+        keep_shared(0, HIGH, a1)
+        keep_shared(1, HIGH, a2)
+        keep_shared(2, LOW, s1)
         for c, cols in ((0, LOW), (1, LOW), (0, HIGH), (1, HIGH), (2, LOW)):
             add_on_gpsimd(c, cols)
-        add_on_vector(2, HIGH, spare_banks[0])
-        add_on_vector(3, LOW, g_banks[7 % RING])
-        add_on_vector(3, HIGH, high_bank)
+        last = ((2, HIGH, g2[:, BLOCK:]), (3, LOW, g0), (3, HIGH, g2))
+        for c, cols, acc in [(c, cols, shared_result(c, cols, bank)) for c, cols, bank in last]:
+            add_on_vector(c, cols, acc)

@@ -117,19 +117,20 @@ def tile_moe_shr_glu_sigmoid_kernel(
         gates = {0: held.tile([P, LATE], F32, name="late_gates"), LEAD: held.tile([P, C], F32, name="lead_gates")}
         for m in range(2):
             load_scales13(m, *first_run)
-            load_words13(m, LEAD)
-        for m in range(2):
-            load_words13(m, E)
+        for e in (LEAD, E):
+            for m in range(2):
+                load_words13(m, e)
         load_scales(scales2[:], w2_scales)
-        load_words2(LEAD, E + 1)
-        nc.sync.dma_start(out=gates[LEAD][:], in_=gate[:P, LATE:])
         for m in range(2):
             load_scales13(m, *late_run)
+        load_words2(LEAD, E)
+        nc.sync.dma_start(out=gates[LEAD][:], in_=gate[:P, LATE:])
         for e in reversed(range(LEAD)):
             for m in range(2):
                 load_words13(m, e)
         load_words2(*late_run)
         nc.sync.dma_start(out=gates[0][:], in_=gate[:P, :LATE])
+        load_words2(E, E + 1)
         gate_columns = held.tile([P, LEAD], F32, name="gate_columns")
         with nc.allow_non_contiguous_dma(reason="one gate value a partition and expert"):
             nc.sync.dma_start(out=gate_columns[:], in_=gate[0, :LATE].rearrange("(e p) -> p e", p=P))

@@ -120,17 +120,16 @@ def tile_moe_shr_glu_sigmoid_kernel(
         for e in (LEAD, E):
             for m in range(2):
                 load_words13(m, e)
+        load_words2(LEAD, E + 1)
+        nc.sync.dma_start(out=gates[LEAD][:], in_=gate[:P, LATE:])
         load_scales(scales2[:], w2_scales)
         for m in range(2):
             load_scales13(m, *late_run)
-        load_words2(LEAD, E)
-        nc.sync.dma_start(out=gates[LEAD][:], in_=gate[:P, LATE:])
         for e in reversed(range(LEAD)):
             for m in range(2):
                 load_words13(m, e)
         load_words2(*late_run)
         nc.sync.dma_start(out=gates[0][:], in_=gate[:P, :LATE])
-        load_words2(E, E + 1)
         gate_columns = held.tile([P, LEAD], F32, name="gate_columns")
         with nc.allow_non_contiguous_dma(reason="one gate value a partition and expert"):
             nc.sync.dma_start(out=gate_columns[:], in_=gate[0, :LATE].rearrange("(e p) -> p e", p=P))
@@ -351,41 +350,41 @@ def tile_moe_shr_glu_sigmoid_kernel(
         nc.scalar.copy(by_word(last_tokens), all_pairs[:, :, last_block * BLOCK :, :])
         quantise_tokens(last_block, last_tokens)
         first_layer(E + 1, a2, g2)
-        routed(LEAD, (0, 1, 3), s1)
-        scatter(LEAD, (0,), s1[:, :C], y_tile("y30", 1))
         first_layer(E + 2, a0, g0)
         quantise_late_slots(1, late_gathered, "late_values")
         first_layer(E + 3, a1, g1)
-        first_layer(2, a2, g2)
+        routed(LEAD, (0, 1, 3), s1)
+        scatter(LEAD, (0,), s1[:, :C], y_tile("y30", 1))
+        first_layer(E + 4, a2, g2)
+        first_layer(2, a0, g0)
         scatter(LEAD, (1,), s1[:, C : 2 * C], y_tile("words13_12", 1))
-        routed(LEAD, (2,), a2)
-        first_layer(1, a0, g0)
+        routed(LEAD, (2,), a0)
+        first_layer(1, a1, g1)
         turn_expert(2, s0)
-        scatter(LEAD, (2,), a2[:, :C], hs[2].bitcast(F32)[:, :C])
-        first_layer(0, a1, g1)
+        scatter(LEAD, (2,), a0[:, :C], hs[2].bitcast(F32)[:, :C])
+        first_layer(0, a2, g2)
         turn_expert(1, s0)
         scatter(LEAD, (3,), s1[:, 2 * C : 3 * C], hs[1].bitcast(F32)[:, :C])
-        routed(2, (0, 1), a1)
-        scatter(2, (0,), a1[:, :C], y_tile("y20", 1))
-        first_layer(E + 4, a2, g2)
-        turn_expert(0, s0)
-        scatter(2, (1,), a1[:, C : 2 * C], hs[0].bitcast(F32)[:, :C])
-        turn(E, 2, g1)
+        routed(2, (0, 1), a2)
+        scatter(2, (0,), a2[:, :C], y_tile("y20", 1))
         first_layer(E + 5, a0, g0)
-        turn(E + 2, 2, a0)
+        turn_expert(0, s0)
+        scatter(2, (1,), a2[:, C : 2 * C], hs[0].bitcast(F32)[:, :C])
+        turn(E, 2, a1)
+        turn(E + 2, 2, g1)
         quantise_h(SLOTS + LOW.start, SLOTS + LOW.stop)
         route(1, 0, s1, 2, hs[E + 3].bitcast(F32))
-        turn(E + 4, 2, a2)
+        turn(E + 4, 2, a0)
         quantise_h(SLOTS + HIGH.start, SLOTS + HIGH.stop)
-        route(0, 0, a1, 2, hs[E + 5].bitcast(F32))
-        for e, bank in ((2, g1), (1, s0), (0, g2)):
+        route(0, 0, a2, 2, hs[E + 5].bitcast(F32))
+        for e, bank in ((2, a1), (1, s0), (0, g2)):
             weigh(e, bank)
-        route_weighed(2, a1)
-        route_weighed(3, a2)
+        route_weighed(2, a2)
+        route_weighed(3, a0)
         keep_shared(0, LOW, s1)
-        keep_shared(1, LOW, a0)
-        keep_shared(0, HIGH, a1)
-        keep_shared(1, HIGH, a2)
+        keep_shared(1, LOW, g1)
+        keep_shared(0, HIGH, a2)
+        keep_shared(1, HIGH, a0)
         keep_shared(2, LOW, s1)
         for c, cols in ((0, LOW), (1, LOW), (0, HIGH), (1, HIGH), (2, LOW)):
             add_on_gpsimd(c, cols)

@@ -15,7 +15,7 @@ BLOCK = 2 * P
 HALVES = (slice(0, T // 2), slice(T // 2, T))
 WEIGHED = 2
 RING = 3
-H_RING = 9
+H_RING = E - 1 + T // P
 FLOPS = 2 * (T + SLOTS) * (2 * K * H + H * N)
 
 F32 = mybir.dt.float32
@@ -40,7 +40,7 @@ def tile_moe_shr_glu_sigmoid_kernel(
         held = ctx.enter_context(tc.tile_pool(name="held", bufs=1))
         work = ctx.enter_context(tc.tile_pool(name="work", bufs=RING))
         psum = ctx.enter_context(tc.psum_pool(name="psum", bufs=1))
-        a0, a1, a2, s0, s1, g0, g1, g2 = [psum.tile([P, 512], F32, name=f"bank{j}") for j in range(8)]
+        a0, a1, a2, spare0, spare1, g0, g1, g2 = [psum.tile([P, 512], F32, name=f"bank{j}") for j in range(8)]
 
         zero = held.tile([P, 1], F32, name="zero")
         nc.vector.memset(zero[:], 0.0)
@@ -57,10 +57,10 @@ def tile_moe_shr_glu_sigmoid_kernel(
             nc.vector.memset(tile[:].bitcast(I32), 0)
 
         def load_scales(target, source):
-            rows = source.bitcast(I32).rearrange("e s (q r) i -> r q (e s) i", r=4)
-            view = target.bitcast(I32).rearrange("p (g i) -> p g i", i=H // 4)
+            scale_rows = source.bitcast(I32).rearrange("e s (q r) i -> r q (e s) i", r=4)
+            view = target.bitcast(I32).rearrange("p (es i) -> p es i", i=H // 4)
             for r in range(4):
-                nc.sync.dma_start(out=view[r:P:32, :, :], in_=rows[r])
+                nc.sync.dma_start(out=view[r:P:32, :, :], in_=scale_rows[r])
 
         def load_scales13(m, lo, hi):
             load_scales(scales13[m, lo][:], (w1_scales, w3_scales)[m][lo:hi])
@@ -84,17 +84,17 @@ def tile_moe_shr_glu_sigmoid_kernel(
 
         clear_window(1, "window1")
 
-        rows = xT.rearrange("(s p u b) w -> s u p b w", s=S, p=P, u=2, b=2)
+        x_rows = xT.rearrange("(s p u b) w -> s u p b w", s=S, p=P, u=2, b=2)
         offsets = held.tile([P, SLOTS // 16], U16, name="offsets")
         raws = {}
         for cols in HALVES:
             raw = held.tile([P, 2, T // 2], F32, name=f"raw00_{cols.start}", align_bytes=64)
-            nc.sync.dma_start(out=raw[:], in_=rows[0, 0][:, :, cols])
+            nc.sync.dma_start(out=raw[:], in_=x_rows[0, 0][:, :, cols])
             raws[0, 0, cols.start] = raw[:]
         nc.sync.dma_start(offsets[:], offs)
         for s, u in ((0, 1), (1, 0), (1, 1)):
             raw = held.tile([P, 2, T], F32, name=f"raw{s}{u}", align_bytes=64)
-            nc.sync.dma_start(out=raw[:], in_=rows[s, u])
+            nc.sync.dma_start(out=raw[:], in_=x_rows[s, u])
             for cols in HALVES:
                 raws[s, u, cols.start] = raw[:, :, cols]
 
@@ -114,14 +114,15 @@ def tile_moe_shr_glu_sigmoid_kernel(
             for e in range(lo, hi):
                 words2[e] = tile[:, e - lo, :]
 
-        gates = {0: held.tile([P, LATE], F32, name="late_gates"), LEAD: held.tile([P, C], F32, name="lead_gates")}
+        late_gates = held.tile([P, LATE], F32, name="late_gates")
+        lead_gates = held.tile([P, C], F32, name="lead_gates")
         for m in range(2):
             load_scales13(m, *first_run)
         for e in (LEAD, E):
             for m in range(2):
                 load_words13(m, e)
         load_words2(LEAD, E + 1)
-        nc.sync.dma_start(out=gates[LEAD][:], in_=gate[:P, LATE:])
+        nc.sync.dma_start(out=lead_gates[:], in_=gate[:P, LATE:])
         load_scales(scales2[:], w2_scales)
         for m in range(2):
             load_scales13(m, *late_run)
@@ -129,7 +130,7 @@ def tile_moe_shr_glu_sigmoid_kernel(
             for m in range(2):
                 load_words13(m, e)
         load_words2(*late_run)
-        nc.sync.dma_start(out=gates[0][:], in_=gate[:P, :LATE])
+        nc.sync.dma_start(out=late_gates[:], in_=gate[:P, :LATE])
         gate_columns = held.tile([P, LEAD], F32, name="gate_columns")
         with nc.allow_non_contiguous_dma(reason="one gate value a partition and expert"):
             nc.sync.dma_start(out=gate_columns[:], in_=gate[0, :LATE].rearrange("(e p) -> p e", p=P))
@@ -164,8 +165,8 @@ def tile_moe_shr_glu_sigmoid_kernel(
             cols = slice(s * SLOTS + lo, s * SLOTS + lo + values.shape[1] // 4)
             nc.vector.quantize_mx(out=slot_codes[:, cols].bitcast(FP8X4), scales=slot_scales[:, cols], in_=values)
 
-        def quantise_late_slots(s, gathered, tag, move=nc.scalar.copy):
-            values = join_pairs(move, gathered, 0, LATE, tag)
+        def quantise_late_slots(s, gathered, tag):
+            values = join_pairs(nc.scalar.copy, gathered, 0, LATE, tag)
             quantise_slots(s, C, values[:, 4 * C :])
             quantise_slots(s, 0, values[:, : 4 * C])
 
@@ -277,7 +278,7 @@ def tile_moe_shr_glu_sigmoid_kernel(
             )
 
         def gate_of(e):
-            return gates[LEAD][:] if e == LEAD else gates[0][:, e * C : (e + 1) * C]
+            return lead_gates[:] if e == LEAD else late_gates[:, e * C : (e + 1) * C]
 
         def routed(e, chunks, bank):
             for j, c in enumerate(chunks):
@@ -292,11 +293,8 @@ def tile_moe_shr_glu_sigmoid_kernel(
         def y_tile(tag, count):
             return held.tile([P, count * C], F32, name=tag, align_bytes=64)[:]
 
-        def route(e, first, bank, count=2, y=None):
-            chunks = range(first, first + count)
-            routed(e, chunks, bank)
-            y = y_tile(f"y{e}{first}", count) if y is None else y[:, : count * C]
-            scatter(e, chunks, bank[:, : count * C], y)
+        def h_bytes(i, count):
+            return hs[i].bitcast(F32)[:, : count * C]
 
         wide = N - WEIGHED * P
         weighed = held.tile([P, LEAD * wide], F32, name="weighed")
@@ -344,50 +342,52 @@ def tile_moe_shr_glu_sigmoid_kernel(
         gather(late_gathered, 1, 0, 0, LATE)
         first_layer(LEAD, a0, g0)
         first_layer(E, a1, g1)
-        turn_expert(LEAD, s0)
+        turn_expert(LEAD, spare0)
         gather(late_gathered, 1, 1, 0, LATE)
-        last_tokens = held.tile([P, block_values], BF16, name="words13_13", align_bytes=64)[:]
+        last_tokens = held.tile([P, block_values], BF16, name=f"words13_1{LEAD}", align_bytes=64)[:]
         nc.scalar.copy(by_word(last_tokens), all_pairs[:, :, last_block * BLOCK :, :])
         quantise_tokens(last_block, last_tokens)
         first_layer(E + 1, a2, g2)
         first_layer(E + 2, a0, g0)
         quantise_late_slots(1, late_gathered, "late_values")
         first_layer(E + 3, a1, g1)
-        routed(LEAD, (0, 1, 3), s1)
-        scatter(LEAD, (0,), s1[:, :C], y_tile("y30", 1))
+        routed(LEAD, (0, 1, 3), spare1)
+        scatter(LEAD, (0,), spare1[:, :C], y_tile("y_lead0", 1))
         first_layer(E + 4, a2, g2)
         first_layer(2, a0, g0)
-        scatter(LEAD, (1,), s1[:, C : 2 * C], y_tile("words13_12", 1))
+        scatter(LEAD, (1,), spare1[:, C : 2 * C], y_tile("words13_12", 1))
         routed(LEAD, (2,), a0)
         first_layer(1, a1, g1)
-        turn_expert(2, s0)
-        scatter(LEAD, (2,), a0[:, :C], hs[2].bitcast(F32)[:, :C])
+        turn_expert(2, spare0)
+        scatter(LEAD, (2,), a0[:, :C], h_bytes(2, 1))
         first_layer(0, a2, g2)
-        turn_expert(1, s0)
-        scatter(LEAD, (3,), s1[:, 2 * C : 3 * C], hs[1].bitcast(F32)[:, :C])
+        turn_expert(1, spare0)
+        scatter(LEAD, (3,), spare1[:, 2 * C : 3 * C], h_bytes(1, 1))
         routed(2, (0, 1), a2)
-        scatter(2, (0,), a2[:, :C], y_tile("y20", 1))
+        scatter(2, (0,), a2[:, :C], y_tile("y_second0", 1))
         first_layer(E + 5, a0, g0)
-        turn_expert(0, s0)
-        scatter(2, (1,), a2[:, C : 2 * C], hs[0].bitcast(F32)[:, :C])
+        turn_expert(0, spare0)
+        scatter(2, (1,), a2[:, C : 2 * C], h_bytes(0, 1))
         turn(E, 2, a1)
         turn(E + 2, 2, g1)
         quantise_h(SLOTS + LOW.start, SLOTS + LOW.stop)
-        route(1, 0, s1, 2, hs[E + 3].bitcast(F32))
+        routed(1, (0, 1), spare1)
+        scatter(1, (0, 1), spare1[:, : 2 * C], h_bytes(E + 3, 2))
         turn(E + 4, 2, a0)
         quantise_h(SLOTS + HIGH.start, SLOTS + HIGH.stop)
-        route(0, 0, a2, 2, hs[E + 5].bitcast(F32))
-        for e, bank in ((2, a1), (1, s0), (0, g2)):
+        routed(0, (0, 1), a2)
+        scatter(0, (0, 1), a2[:, : 2 * C], h_bytes(E + 5, 2))
+        for e, bank in ((2, a1), (1, spare0), (0, g2)):
             weigh(e, bank)
         route_weighed(2, a2)
         route_weighed(3, a0)
-        keep_shared(0, LOW, s1)
+        keep_shared(0, LOW, spare1)
         keep_shared(1, LOW, g1)
         keep_shared(0, HIGH, a2)
         keep_shared(1, HIGH, a0)
-        keep_shared(2, LOW, s1)
-        for c, cols in ((0, LOW), (1, LOW), (0, HIGH), (1, HIGH), (2, LOW)):
+        keep_shared(2, LOW, spare1)
+        for c, cols in ((0, LOW), (1, LOW), (0, HIGH), (2, LOW), (1, HIGH)):
             add_on_gpsimd(c, cols)
-        last = ((2, HIGH, g2[:, BLOCK:]), (3, LOW, g0), (3, HIGH, g2))
-        for c, cols, acc in [(c, cols, shared_result(c, cols, bank)) for c, cols, bank in last]:
+        rest = ((2, HIGH, g2[:, BLOCK:]), (3, LOW, g0), (3, HIGH, g2))
+        for c, cols, acc in [(c, cols, shared_result(c, cols, bank)) for c, cols, bank in rest]:
             add_on_vector(c, cols, acc)

@@ -383,10 +383,10 @@ def tile_moe_shr_glu_sigmoid_kernel(
         route_weighed(3, a0)
         keep_shared(0, LOW, spare1)
         keep_shared(1, LOW, g1)
+        keep_shared(2, LOW, spare1)
         keep_shared(0, HIGH, a2)
         keep_shared(1, HIGH, a0)
-        keep_shared(2, LOW, spare1)
-        for c, cols in ((0, LOW), (1, LOW), (0, HIGH), (2, LOW), (1, HIGH)):
+        for c, cols in ((0, LOW), (1, LOW), (2, LOW), (0, HIGH), (1, HIGH)):
             add_on_gpsimd(c, cols)
         rest = ((2, HIGH, g2[:, BLOCK:]), (3, LOW, g0), (3, HIGH, g2))
         for c, cols, acc in [(c, cols, shared_result(c, cols, bank)) for c, cols, bank in rest]:

@@ -319,7 +319,11 @@ def tile_moe_shr_glu_sigmoid_kernel(
                 nc.tensor.transpose(bank[:, e * C : (e + 1) * C], weighed[:, at : at + P], ident[:])
             y = held.tile([P, LATE], F32, name=f"y_late{c}")
             nc.scalar.copy(y[:], bank[:, :LATE])
-            nc.vector.tensor_copy(windows[c][:].indirect(offsets[:, : LATE // 16]), y[:])
+            window = windows[c][:].indirect(offsets[:, : LATE // 16])
+            if c == CHUNKS - 1:
+                nc.scalar.activation(window, y[:], COPY)
+            else:
+                nc.vector.tensor_copy(window, y[:])
 
         def shared_result(c, cols, bank):
             acc = bank[:, : cols.stop - cols.start]

@@ -388,10 +388,8 @@ def tile_moe_shr_glu_sigmoid_kernel(
         keep_shared(0, LOW, spare1)
         keep_shared(1, LOW, g1)
         keep_shared(2, LOW, spare1)
-        keep_shared(0, HIGH, a2)
-        keep_shared(1, HIGH, a0)
-        for c, cols in ((0, LOW), (1, LOW), (2, LOW), (0, HIGH), (1, HIGH)):
+        for c, cols in ((0, LOW), (1, LOW), (2, LOW)):
             add_on_gpsimd(c, cols)
-        rest = ((2, HIGH, g2[:, BLOCK:]), (3, LOW, g0), (3, HIGH, g2))
+        rest = ((0, HIGH, a2), (1, HIGH, a0), (2, HIGH, g2[:, BLOCK:]), (3, LOW, g0), (3, HIGH, g2))
         for c, cols, acc in [(c, cols, shared_result(c, cols, bank)) for c, cols, bank in rest]:
             add_on_vector(c, cols, acc)

@@ -13,7 +13,6 @@ LEAD = E - 1
 LATE = LEAD * C
 BLOCK = 2 * P
 HALVES = (slice(0, T // 2), slice(T // 2, T))
-WEIGHED = 2
 RING = 3
 H_RING = E - 1 + T // P
 FLOPS = 2 * (T + SLOTS) * (2 * K * H + H * N)
@@ -131,9 +130,6 @@ def tile_moe_shr_glu_sigmoid_kernel(
                 load_words13(m, e)
         load_words2(*late_run)
         nc.sync.dma_start(out=late_gates[:], in_=gate[:P, :LATE])
-        gate_columns = held.tile([P, LEAD], F32, name="gate_columns")
-        with nc.allow_non_contiguous_dma(reason="one gate value a partition and expert"):
-            nc.sync.dma_start(out=gate_columns[:], in_=gate[0, :LATE].rearrange("(e p) -> p e", p=P))
 
         slot_codes = held.tile([P, S * SLOTS], U32, name="slot_codes", align_bytes=64)
         slot_scales = held.tile([P, S * SLOTS], U8, name="slot_scales", align_bytes=64)
@@ -194,9 +190,13 @@ def tile_moe_shr_glu_sigmoid_kernel(
         all_pairs = pairs[:].bitcast(F32).rearrange("p (s u w) -> p s w u", s=S, u=2)
         last_block = T // BLOCK - 1
 
-        def quantise_tokens(b, values):
-            cols = slice(S * BLOCK * b, S * BLOCK * (b + 1))
-            nc.vector.quantize_mx(out=token_codes[:, cols].bitcast(FP8X4), scales=token_scales[:, cols], in_=values)
+        def quantise_tokens(b, values, lo=0, hi=S):
+            cols = slice((S * b + lo) * BLOCK, (S * b + hi) * BLOCK)
+            nc.vector.quantize_mx(
+                out=token_codes[:, cols].bitcast(FP8X4),
+                scales=token_scales[:, cols],
+                in_=values[:, 4 * BLOCK * lo : 4 * BLOCK * hi],
+            )
 
         def by_word(values):
             return values.bitcast(F32).rearrange("p (s w u) -> p s w u", s=S, u=2)
@@ -205,14 +205,14 @@ def tile_moe_shr_glu_sigmoid_kernel(
         for b, values in enumerate(early_blocks):
             for s in range(S):
                 nc.scalar.copy(by_word(values[:])[:, s, :, :], all_pairs[:, s, b * BLOCK : (b + 1) * BLOCK, :])
-            quantise_tokens(b, values[:])
+                quantise_tokens(b, values[:], s, s + 1)
         quantise_late_slots(0, gathered0[:], "raw11")
 
         results = [held.tile([P, T], F32, name=f"result{c}") for c in range(CHUNKS)]
         h_codes = held.tile([P, SLOTS + T], U32, name="h_codes", align_bytes=64)
         h_scales = held.tile([P, SLOTS + T], U8, name="h_scales", align_bytes=64)
         h_values = held.tile([P, 4 * (SLOTS + T)], BF16, name="h_values", align_bytes=64)
-        hs = {}
+        hs, sigs = {}, {}
 
         def first_layer(i, a, g):
             if i < E:
@@ -244,15 +244,16 @@ def tile_moe_shr_glu_sigmoid_kernel(
                 MULT,
             )
             hs[i] = h
+            sigs[i] = sig
 
-        def turn(i, count, bank):
+        def turn(i, count, bank, move=nc.scalar.copy):
             turned = bank[:, : count * 2 * P].rearrange("p (j u c) -> p j u c", j=count, u=2)
             for j in range(count):
                 words = hs[i + j].bitcast(F32)
                 for u in range(2):
                     nc.tensor.transpose(turned[:, j, u, :], words[:, u * P : (u + 1) * P], ident[:])
             values = h_values[:, 4 * P * i : 4 * P * (i + count)]
-            nc.scalar.copy(
+            move(
                 values.bitcast(F32).rearrange("p (j c u) -> p j c u", j=count, u=2),
                 turned.rearrange("p j u c -> p j c u"),
             )
@@ -290,54 +291,36 @@ def tile_moe_shr_glu_sigmoid_kernel(
                 window = windows[c][:].indirect(offsets[:, e * C // 16 : (e + 1) * C // 16])
                 nc.vector.tensor_tensor(window, y[:, j * C : (j + 1) * C], gate_of(e), MULT)
 
+        ys = {}
+
+        def weigh_chunks(e, chunks, acc, y):
+            count = len(chunks)
+            nc.vector.tensor_tensor(
+                y.rearrange("p (c j) -> p c j", c=count),
+                acc.rearrange("p (c j) -> p c j", c=count),
+                gate_of(e).unsqueeze(1).to_broadcast([P, count, C]),
+                MULT,
+            )
+            for j, c in enumerate(chunks):
+                ys[e, c] = y[:, j * C : (j + 1) * C]
+
+        def place(e, c, on_scalar):
+            window = windows[c][:].indirect(offsets[:, e * C // 16 : (e + 1) * C // 16])
+            if on_scalar:
+                nc.scalar.activation(window, ys[e, c], COPY)
+            else:
+                nc.vector.tensor_copy(window, ys[e, c])
+
         def y_tile(tag, count):
             return held.tile([P, count * C], F32, name=tag, align_bytes=64)[:]
 
         def h_bytes(i, count):
             return hs[i].bitcast(F32)[:, : count * C]
 
-        wide = N - WEIGHED * P
-        weighed = held.tile([P, LEAD * wide], F32, name="weighed")
-
-        def weigh(e, bank):
-            nc.tensor.matmul_mx(
-                out=bank[:, :wide],
-                lhsT=h_codes[:, e * C : (e + 1) * C].bitcast(FP8X4),
-                lhsT_scale=h_scales[:, e * C : (e + 1) * C],
-                rhs=words2[e][:, 2 * WEIGHED * P :].bitcast(FP4X4),
-                rhs_scale=scales2[:, e * N + WEIGHED * P : (e + 1) * N],
-                start=True,
-                stop=True,
-            )
-            nc.scalar.activation(
-                weighed[:, e * wide : (e + 1) * wide], bank[:, :wide], COPY, scale=gate_columns[:, e : e + 1]
-            )
-
-        def route_weighed(c, bank):
-            for e in range(LEAD):
-                at = e * wide + (c - WEIGHED) * P
-                nc.tensor.transpose(bank[:, e * C : (e + 1) * C], weighed[:, at : at + P], ident[:])
-            y = held.tile([P, LATE], F32, name=f"y_late{c}")
-            nc.scalar.copy(y[:], bank[:, :LATE])
-            window = windows[c][:].indirect(offsets[:, : LATE // 16])
-            if c == CHUNKS - 1:
-                nc.scalar.activation(window, y[:], COPY)
-            else:
-                nc.vector.tensor_copy(window, y[:])
-
         def shared_result(c, cols, bank):
             acc = bank[:, : cols.stop - cols.start]
             second_layer(acc, E, c, SLOTS + cols.start, SLOTS + cols.stop)
             return acc
-
-        shared = [held.tile([P, T], F32, name=f"shared{c}") for c in range(CHUNKS - 1)]
-
-        def keep_shared(c, cols, bank):
-            nc.scalar.copy(shared[c][:, cols], shared_result(c, cols, bank))
-
-        def add_on_gpsimd(c, cols):
-            nc.gpsimd.tensor_tensor(results[c][:, cols], shared[c][:, cols], windows[c][:, cols], ADD)
-            nc.scalar.dma_start(out=out[c * P : (c + 1) * P, cols], in_=results[c][:, cols])
 
         def add_on_vector(c, cols, acc):
             nc.vector.tensor_tensor(results[c][:, cols], acc, windows[c][:, cols], ADD)
@@ -367,29 +350,25 @@ def tile_moe_shr_glu_sigmoid_kernel(
         first_layer(0, a2, g2)
         turn_expert(1, spare0)
         scatter(LEAD, (3,), spare1[:, 2 * C : 3 * C], h_bytes(1, 1))
-        routed(2, (0, 1), a2)
-        scatter(2, (0,), a2[:, :C], y_tile("y_second0", 1))
+        routed(2, range(CHUNKS), a2)
         first_layer(E + 5, a0, g0)
         turn_expert(0, spare0)
-        scatter(2, (1,), a2[:, C : 2 * C], h_bytes(0, 1))
         turn(E, 2, a1)
         turn(E + 2, 2, g1)
+        weigh_chunks(2, range(CHUNKS), a2[:], sigs[E + 5])
+        place(2, 0, True)
         quantise_h(SLOTS + LOW.start, SLOTS + LOW.stop)
-        routed(1, (0, 1), spare1)
-        scatter(1, (0, 1), spare1[:, : 2 * C], h_bytes(E + 3, 2))
-        turn(E + 4, 2, a0)
+        routed(1, range(CHUNKS), spare1)
+        weigh_chunks(1, range(CHUNKS), spare1[:], y_tile("y_first", CHUNKS))
+        turn(E + 4, 2, a0, nc.vector.tensor_copy)
         quantise_h(SLOTS + HIGH.start, SLOTS + HIGH.stop)
-        routed(0, (0, 1), a2)
-        scatter(0, (0, 1), a2[:, : 2 * C], h_bytes(E + 5, 2))
-        for e, bank in ((2, a1), (1, spare0), (0, g2)):
-            weigh(e, bank)
-        route_weighed(2, a2)
-        route_weighed(3, a0)
-        keep_shared(0, LOW, spare1)
-        keep_shared(1, LOW, g1)
-        keep_shared(2, LOW, spare1)
-        for c, cols in ((0, LOW), (1, LOW), (2, LOW)):
-            add_on_gpsimd(c, cols)
-        rest = ((0, HIGH, a2), (1, HIGH, a0), (2, HIGH, g2[:, BLOCK:]), (3, LOW, g0), (3, HIGH, g2))
+        routed(0, range(CHUNKS), g2)
+        weigh_chunks(0, range(CHUNKS), g2[:], y_tile("y_last", CHUNKS))
+        for e, c in ((1, 0), (1, 2), (0, 0)):
+            place(e, c, False)
+        for e, c in ((1, 1), (1, 3), (2, 1), (2, 3), (0, 1), (2, 2), (0, 3)):
+            place(e, c, True)
+        place(0, 2, True)
+        rest = ((0, LOW, a1), (0, HIGH, a2), (1, LOW, g1), (1, HIGH, a2[:, BLOCK:]), (3, LOW, g0), (3, HIGH, a0), (2, LOW, spare0), (2, HIGH, a0[:, BLOCK:]))
         for c, cols, acc in [(c, cols, shared_result(c, cols, bank)) for c, cols, bank in rest]:
             add_on_vector(c, cols, acc)

@@ -179,11 +179,12 @@ def tile_moe_shr_glu_sigmoid_kernel(
         clear_window(2, f"raw00_{T // 2}")
         clear_window(3, "raw01")
         quantise_slots(0, LATE, join_pairs(nc.vector.tensor_copy, gathered0[:], LATE, SLOTS, "lead0")[:])
-        lead_gathered = held.tile([P, 4 * C], BF16, name="lead_gathered", align_bytes=64)
+        lead_values = held.tile([P, 4 * C], BF16, name="lead1", align_bytes=64)
+        lead_words = lead_values[:].bitcast(U32).rearrange("p (c u) -> p c u", u=2)
         for u in range(2):
             cast(1, u)
-            gather(lead_gathered[:], 1, u, LATE, SLOTS)
-        quantise_slots(1, LATE, join_pairs(nc.vector.tensor_copy, lead_gathered[:], 0, C, "lead1")[:])
+            nc.vector.tensor_copy(lead_words[:, :, u], plane(1, u).bitcast(U32).indirect(offsets[:, LATE // 16 :]))
+        quantise_slots(1, LATE, lead_values[:])
 
         token_codes = held.tile([P, S * T], U32, name="token_codes", align_bytes=64)
         token_scales = held.tile([P, S * T], U8, name="token_scales", align_bytes=64)

from contextlib import ExitStack

import concourse.mybir as mybir
from concourse.masks import make_identity

K, T, E, C, H, N = 1024, 768, 4, 128, 512, 512
P = 128
S = K // 512
SLOTS = E * C
CHUNKS = N // P
LOW, HIGH = slice(0, 512), slice(512, 768)
LEAD = E - 1
LATE = LEAD * C
BLOCK = 2 * P
HALVES = (slice(0, T // 2), slice(T // 2, T))
RING = 3
H_RING = E - 1 + T // P
FLOPS = 2 * (T + SLOTS) * (2 * K * H + H * N)

F32 = mybir.dt.float32
BF16 = mybir.dt.bfloat16
U32 = mybir.dt.uint32
I32 = mybir.dt.int32
U16 = mybir.dt.uint16
U8 = mybir.dt.uint8
FP8X4 = mybir.dt.float8_e4m3fn_x4
FP4X4 = mybir.dt.float4_e2m1fn_x4
MULT = mybir.AluOpType.mult
ADD = mybir.AluOpType.add
SIGMOID = mybir.ActivationFunctionType.Sigmoid
COPY = mybir.ActivationFunctionType.Copy


def tile_moe_shr_glu_sigmoid_kernel(
    tc, xT, w1_words, w1_scales, w3_words, w3_scales, w2_words, w2_scales, gate, offs, out
):
    nc = tc.nc
    with ExitStack() as ctx:
        held = ctx.enter_context(tc.tile_pool(name="held", bufs=1))
        work = ctx.enter_context(tc.tile_pool(name="work", bufs=RING))
        psum = ctx.enter_context(tc.psum_pool(name="psum", bufs=1))
        a0, a1, a2, spare0, spare1, g0, g1, g2 = [psum.tile([P, 512], F32, name=f"bank{j}") for j in range(8)]

        zero = held.tile([P, 1], F32, name="zero")
        nc.vector.memset(zero[:], 0.0)
        warm = held.tile([P, 1], F32, name="warm")
        nc.scalar.activation(warm[:], zero[:], SIGMOID)

        first_run, late_run = (LEAD, E + 1), (0, LEAD)
        scales13 = {}
        for lo, hi in (first_run, late_run):
            for m in range(2):
                scales13[m, lo] = held.tile([P, (hi - lo) * S * H], U8, name=f"scales13_{m}{lo}", align_bytes=64)
        scales2 = held.tile([P, (E + 1) * N], U8, name="scales2", align_bytes=64)
        for tile in (scales13[0, LEAD], scales13[1, LEAD], scales2, scales13[0, 0], scales13[1, 0]):
            nc.vector.memset(tile[:].bitcast(I32), 0)

        def load_scales(target, source):
            scale_rows = source.bitcast(I32).rearrange("e s (q r) i -> r q (e s) i", r=4)
            view = target.bitcast(I32).rearrange("p (es i) -> p es i", i=H // 4)
            for r in range(4):
                nc.sync.dma_start(out=view[r:P:32, :, :], in_=scale_rows[r])

        def load_scales13(m, lo, hi):
            load_scales(scales13[m, lo][:], (w1_scales, w3_scales)[m][lo:hi])

        def scale13(m, e, s):
            lo = LEAD if e >= LEAD else 0
            at = ((e - lo) * S + s) * H
            return scales13[m, lo][:, at : at + H]

        ident = held.tile([P, P], F32, name="ident")
        make_identity(nc, ident[:])

        windows = {}

        def clear_window(c, tag):
            windows[c] = held.tile([P, T], F32, name=tag, align_bytes=64)
            if c < CHUNKS // 2:
                nc.scalar.copy(windows[c][:], zero[:].to_broadcast([P, T]))
            else:
                nc.gpsimd.memset(windows[c][:], 0.0)

        clear_window(1, "window1")

        x_rows = xT.rearrange("(s p u b) w -> s u p b w", s=S, p=P, u=2, b=2)
        offsets = held.tile([P, SLOTS // 16], U16, name="offsets")
        raws = {}
        for cols in HALVES:
            raw = held.tile([P, 2, T // 2], F32, name=f"raw00_{cols.start}", align_bytes=64)
            nc.sync.dma_start(out=raw[:], in_=x_rows[0, 0][:, :, cols])
            raws[0, 0, cols.start] = raw[:]
        nc.sync.dma_start(offsets[:], offs)
        for s, u in ((0, 1), (1, 0), (1, 1)):
            raw = held.tile([P, 2, T], F32, name=f"raw{s}{u}", align_bytes=64)
            nc.sync.dma_start(out=raw[:], in_=x_rows[s, u])
            for cols in HALVES:
                raws[s, u, cols.start] = raw[:, :, cols]

        words13, words2 = {}, {}

        def load_words13(m, e):
            tile = held.tile([P, S, 2 * H], U8, name=f"words13_{m}{e}", align_bytes=64)
            source = (w1_words, w3_words)[m][e]
            nc.sync.dma_start(out=tile[:].bitcast(I32), in_=source.bitcast(I32).rearrange("s p b -> p s b"))
            words13[m, e] = tile

        def load_words2(lo, hi):
            tile = held.tile([P, hi - lo, 2 * N], U8, name=f"words2_{lo}", align_bytes=64)
            nc.sync.dma_start(
                out=tile[:].bitcast(I32), in_=w2_words[lo:hi, 0].bitcast(I32).rearrange("e p b -> p e b")
            )
            for e in range(lo, hi):
                words2[e] = tile[:, e - lo, :]

        late_gates = held.tile([P, LATE], F32, name="late_gates")
        lead_gates = held.tile([P, C], F32, name="lead_gates")
        for m in range(2):
            load_scales13(m, *first_run)
        for e in (LEAD, E):
            for m in range(2):
                load_words13(m, e)
        load_words2(LEAD, E + 1)
        nc.sync.dma_start(out=lead_gates[:], in_=gate[:P, LATE:])
        load_scales(scales2[:], w2_scales)
        for m in range(2):
            load_scales13(m, *late_run)
        for e in reversed(range(LEAD)):
            for m in range(2):
                load_words13(m, e)
        load_words2(*late_run)
        nc.sync.dma_start(out=late_gates[:], in_=gate[:P, :LATE])

        slot_codes = held.tile([P, S * SLOTS], U32, name="slot_codes", align_bytes=64)
        slot_scales = held.tile([P, S * SLOTS], U8, name="slot_scales", align_bytes=64)
        pairs = held.tile([P, 2 * S * 2 * T], BF16, name="pairs", align_bytes=64)

        def plane(s, u):
            at = 2 * T * (2 * s + u)
            return pairs[:, at : at + 2 * T]

        def cast(s, u):
            paired = plane(s, u).rearrange("p (w b) -> p w b", b=2)
            for cols, move in zip(HALVES, (nc.scalar.copy, nc.vector.tensor_copy)):
                move(paired[:, cols, :], raws[s, u, cols.start].rearrange("p b w -> p w b"))

        def gather(target, s, u, lo, hi):
            width = 2 * (hi - lo)
            part = target[:, width * u : width * (u + 1)].bitcast(U32)
            nc.vector.tensor_copy(part, plane(s, u).bitcast(U32).indirect(offsets[:, lo // 16 : hi // 16]))

        def join_pairs(move, gathered, lo, hi, tag):
            values = held.tile([P, 4 * (hi - lo)], BF16, name=tag, align_bytes=64)
            move(
                values[:].bitcast(F32).rearrange("p (c u) -> p c u", u=2),
                gathered.bitcast(F32).rearrange("p (u c) -> p c u", u=2)[:, lo:hi, :],
            )
            return values

        def quantise_slots(s, lo, values):
            cols = slice(s * SLOTS + lo, s * SLOTS + lo + values.shape[1] // 4)
            nc.vector.quantize_mx(out=slot_codes[:, cols].bitcast(FP8X4), scales=slot_scales[:, cols], in_=values)

        def quantise_late_slots(s, gathered, tag):
            values = join_pairs(nc.scalar.copy, gathered, 0, LATE, tag)
            quantise_slots(s, C, values[:, 4 * C :])
            quantise_slots(s, 0, values[:, : 4 * C])

        block_values = 4 * S * BLOCK
        reused = held.tile([P, block_values + 2 * H], BF16, name="reused", align_bytes=64)
        first_sigmoid = reused[:, block_values:].bitcast(F32)
        late_gathered = reused[:, block_values - 2 * LATE : block_values + 2 * LATE]

        gathered0 = held.tile([P, 4 * SLOTS], BF16, name="gathered0", align_bytes=64)
        for u in range(2):
            cast(0, u)
            gather(gathered0[:], 0, u, 0, SLOTS)
        clear_window(0, "raw00_0")
        clear_window(2, f"raw00_{T // 2}")
        clear_window(3, "raw01")
        quantise_slots(0, LATE, join_pairs(nc.vector.tensor_copy, gathered0[:], LATE, SLOTS, "lead0")[:])
        lead_values = held.tile([P, 4 * C], BF16, name="lead1", align_bytes=64)
        lead_words = lead_values[:].bitcast(U32).rearrange("p (c u) -> p c u", u=2)
        for u in range(2):
            cast(1, u)
            nc.vector.tensor_copy(lead_words[:, :, u], plane(1, u).bitcast(U32).indirect(offsets[:, LATE // 16 :]))
        quantise_slots(1, LATE, lead_values[:])

        token_codes = held.tile([P, S * T], U32, name="token_codes", align_bytes=64)
        token_scales = held.tile([P, S * T], U8, name="token_scales", align_bytes=64)
        all_pairs = pairs[:].bitcast(F32).rearrange("p (s u w) -> p s w u", s=S, u=2)
        last_block = T // BLOCK - 1

        def quantise_tokens(b, values, lo=0, hi=S):
            cols = slice((S * b + lo) * BLOCK, (S * b + hi) * BLOCK)
            nc.vector.quantize_mx(
                out=token_codes[:, cols].bitcast(FP8X4),
                scales=token_scales[:, cols],
                in_=values[:, 4 * BLOCK * lo : 4 * BLOCK * hi],
            )

        def by_word(values):
            return values.bitcast(F32).rearrange("p (s w u) -> p s w u", s=S, u=2)

        early_blocks = [held.tile([P, block_values], BF16, name="tokens0", align_bytes=64), reused[:, :block_values]]
        for b, values in enumerate(early_blocks):
            for s in range(S):
                nc.scalar.copy(by_word(values[:])[:, s, :, :], all_pairs[:, s, b * BLOCK : (b + 1) * BLOCK, :])
                quantise_tokens(b, values[:], s, s + 1)
        quantise_late_slots(0, gathered0[:], "raw11")

        results = [held.tile([P, T], F32, name=f"result{c}") for c in range(CHUNKS)]
        h_codes = held.tile([P, SLOTS + T], U32, name="h_codes", align_bytes=64)
        h_scales = held.tile([P, SLOTS + T], U8, name="h_scales", align_bytes=64)
        h_values = held.tile([P, 4 * (SLOTS + T)], BF16, name="h_values", align_bytes=64)
        hs, sigs = {}, {}

        def first_layer(i, a, g):
            if i < E:
                e, codes, scales = i, slot_codes, slot_scales
                starts = [s * SLOTS + i * C for s in range(S)]
            else:
                e, codes, scales = E, token_codes, token_scales
                starts = [((i - E) // 2 * S + s) * BLOCK + (i - E) % 2 * P for s in range(S)]
            for m, acc in enumerate((a, g)):
                for s in range(S):
                    cols = slice(starts[s], starts[s] + P)
                    nc.tensor.matmul_mx(
                        out=acc[:],
                        lhsT=codes[:, cols].bitcast(FP8X4),
                        lhsT_scale=scales[:, cols],
                        rhs=words13[m, e][:, s, :].bitcast(FP4X4),
                        rhs_scale=scale13(m, e, s),
                        start=(s == 0),
                        stop=(s == S - 1),
                    )
            sig = first_sigmoid if i == LEAD else work.tile([P, H], F32, name="sig")[:]
            h = work.tile([P, H], BF16, name="h", align_bytes=64, bufs=H_RING)[:]
            natural, by_pair = "t (p u b) -> t u p b", "t (u p b) -> t u p b"
            nc.scalar.activation(sig.rearrange(by_pair, u=2, b=2), a[:].rearrange(natural, u=2, b=2), SIGMOID)
            nc.vector.tensor_tensor(
                h.rearrange(by_pair, u=2, b=2),
                sig.rearrange(by_pair, u=2, b=2),
                g[:].rearrange(natural, u=2, b=2),
                MULT,
            )
            hs[i] = h
            sigs[i] = sig

        def turn(i, count, bank, move=nc.scalar.copy):
            turned = bank[:, : count * 2 * P].rearrange("p (j u c) -> p j u c", j=count, u=2)
            for j in range(count):
                words = hs[i + j].bitcast(F32)
                for u in range(2):
                    nc.tensor.transpose(turned[:, j, u, :], words[:, u * P : (u + 1) * P], ident[:])
            values = h_values[:, 4 * P * i : 4 * P * (i + count)]
            move(
                values.bitcast(F32).rearrange("p (j c u) -> p j c u", j=count, u=2),
                turned.rearrange("p j u c -> p j c u"),
            )

        def quantise_h(lo, hi):
            nc.vector.quantize_mx(
                out=h_codes[:, lo:hi].bitcast(FP8X4), scales=h_scales[:, lo:hi], in_=h_values[:, 4 * lo : 4 * hi]
            )

        def turn_expert(e, bank):
            turn(e, 1, bank)
            quantise_h(e * C, (e + 1) * C)

        def second_layer(acc, e, c, lo, hi):
            nc.tensor.matmul_mx(
                out=acc,
                lhsT=words2[e][:, 2 * P * c : 2 * P * (c + 1)].bitcast(FP4X4),
                lhsT_scale=scales2[:, e * N + c * P : e * N + (c + 1) * P],
                rhs=h_codes[:, lo:hi].bitcast(FP8X4),
                rhs_scale=h_scales[:, lo:hi],
                start=True,
                stop=True,
            )

        def gate_of(e):
            return lead_gates[:] if e == LEAD else late_gates[:, e * C : (e + 1) * C]

        def routed(e, chunks, bank):
            for j, c in enumerate(chunks):
                second_layer(bank[:, j * C : (j + 1) * C], e, c, e * C, (e + 1) * C)

        def scatter(e, chunks, acc, y):
            nc.scalar.copy(y, acc)
            for j, c in enumerate(chunks):
                window = windows[c][:].indirect(offsets[:, e * C // 16 : (e + 1) * C // 16])
                nc.vector.tensor_tensor(window, y[:, j * C : (j + 1) * C], gate_of(e), MULT)

        ys = {}

        def weigh_chunks(e, chunks, acc, y):
            count = len(chunks)
            nc.vector.tensor_tensor(
                y.rearrange("p (c j) -> p c j", c=count),
                acc.rearrange("p (c j) -> p c j", c=count),
                gate_of(e).unsqueeze(1).to_broadcast([P, count, C]),
                MULT,
            )
            for j, c in enumerate(chunks):
                ys[e, c] = y[:, j * C : (j + 1) * C]

        def place(e, c, on_scalar):
            window = windows[c][:].indirect(offsets[:, e * C // 16 : (e + 1) * C // 16])
            if on_scalar:
                nc.scalar.activation(window, ys[e, c], COPY)
            else:
                nc.vector.tensor_copy(window, ys[e, c])

        def y_tile(tag, count):
            return held.tile([P, count * C], F32, name=tag, align_bytes=64)[:]

        def h_bytes(i, count):
            return hs[i].bitcast(F32)[:, : count * C]

        def shared_result(c, cols, bank):
            acc = bank[:, : cols.stop - cols.start]
            second_layer(acc, E, c, SLOTS + cols.start, SLOTS + cols.stop)
            return acc

        def add_on_vector(c, cols, acc):
            nc.vector.tensor_tensor(results[c][:, cols], acc, windows[c][:, cols], ADD)
            nc.sync.dma_start(out=out[c * P : (c + 1) * P, cols], in_=results[c][:, cols])

        gather(late_gathered, 1, 0, 0, LATE)
        first_layer(LEAD, a0, g0)
        first_layer(E, a1, g1)
        turn_expert(LEAD, spare0)
        gather(late_gathered, 1, 1, 0, LATE)
        last_tokens = held.tile([P, block_values], BF16, name=f"words13_1{LEAD}", align_bytes=64)[:]
        nc.scalar.copy(by_word(last_tokens), all_pairs[:, :, last_block * BLOCK :, :])
        quantise_tokens(last_block, last_tokens)
        first_layer(E + 1, a2, g2)
        first_layer(E + 2, a0, g0)
        quantise_late_slots(1, late_gathered, "late_values")
        first_layer(E + 3, a1, g1)
        routed(LEAD, (0, 1, 3), spare1)
        scatter(LEAD, (0,), spare1[:, :C], y_tile("y_lead0", 1))
        first_layer(E + 4, a2, g2)
        first_layer(2, a0, g0)
        scatter(LEAD, (1,), spare1[:, C : 2 * C], y_tile("words13_12", 1))
        routed(LEAD, (2,), a0)
        first_layer(1, a1, g1)
        turn_expert(2, spare0)
        scatter(LEAD, (2,), a0[:, :C], h_bytes(2, 1))
        first_layer(0, a2, g2)
        turn_expert(1, spare0)
        scatter(LEAD, (3,), spare1[:, 2 * C : 3 * C], h_bytes(1, 1))
        routed(2, range(CHUNKS), a2)
        first_layer(E + 5, a0, g0)
        turn_expert(0, spare0)
        turn(E, 2, a1)
        turn(E + 2, 2, g1)
        weigh_chunks(2, range(CHUNKS), a2[:], sigs[E + 5])
        place(2, 0, True)
        quantise_h(SLOTS + LOW.start, SLOTS + LOW.stop)
        routed(1, range(CHUNKS), spare1)
        weigh_chunks(1, range(CHUNKS), spare1[:], y_tile("y_first", CHUNKS))
        turn(E + 4, 2, a0, nc.vector.tensor_copy)
        quantise_h(SLOTS + HIGH.start, SLOTS + HIGH.stop)
        routed(0, range(CHUNKS), g2)
        weigh_chunks(0, range(CHUNKS), g2[:], y_tile("y_last", CHUNKS))
        for e, c in ((1, 0), (1, 2), (0, 0)):
            place(e, c, False)
        for e, c in ((1, 1), (1, 3), (2, 1), (2, 3), (0, 1), (2, 2), (0, 3)):
            place(e, c, True)
        place(0, 2, True)
        rest = ((0, LOW, a1), (0, HIGH, a2), (1, LOW, g1), (1, HIGH, a2[:, BLOCK:]), (3, LOW, g0), (3, HIGH, a0), (2, LOW, spare0), (2, HIGH, a0[:, BLOCK:]))
        for c, cols, acc in [(c, cols, shared_result(c, cols, bank)) for c, cols, bank in rest]:
            add_on_vector(c, cols, acc)
